import numpy as np
import ml_dtypes


def mxq(x, axis, fmt="e4m3"):
    dtype, down = {"e4m3": (ml_dtypes.float8_e4m3fn, 7), "e5m2": (ml_dtypes.float8_e5m2, 14)}[fmt]
    v = np.moveaxis(np.asarray(x, np.float32).astype(ml_dtypes.bfloat16).astype(np.float64), axis, -1)
    blocks = v.reshape(v.shape[:-1] + (-1, 32))
    amax = np.abs(blocks).max(-1, keepdims=True)
    byte = np.maximum(np.where(amax > 0, np.frexp(amax)[1] - 1 + 127, 0) - down, 1)
    scale = np.exp2(byte - 127.0)
    codes = (blocks / scale).astype(np.float32).astype(dtype).astype(np.float64)
    return np.moveaxis((codes * scale).reshape(v.shape), -1, axis)


WIDE = False


def mx_kscale(k):
    if not WIDE:
        return np.ones(k)
    levels = np.array([18, -18])
    if k % 512:
        return np.exp2(np.random.permutation(np.resize(levels, k // 32))).repeat(32)
    a = np.empty((k // 512, 16))
    for p in range(k // 512):
        a[p, :8] = np.random.permutation(np.resize(levels, 8))
        for g in range(8):
            far = levels[np.abs(levels - a[p, g]) >= 10]
            a[p, g + 8] = far[np.random.randint(len(far))]
    return np.exp2(a.ravel()).repeat(32)


def f64(x):
    return np.asarray(x).astype(np.float64)


def striped(idx):
    return np.tile(np.asarray(idx).reshape(-1, 16).T, (8, 1)).astype(np.uint16)


def unstriped(offs):
    return offs[:16].T.reshape(-1).astype(np.int64)


B, N, T, D, DV = 2, 512, 2048, 512, 512


def setup_inputs():
    n = np.random.standard_normal
    idx = np.random.permutation(T)[:B * N]
    u = np.ones(T)
    u[idx] = mx_kscale(B * N)
    v = mx_kscale(DV)[:, None]
    coarse = lambda x: x.astype(np.float32).astype(ml_dtypes.bfloat16).astype(np.float64)
    r = np.random.randint(8, 33, T) / 16.0 * u
    return {
        "xT": (n((D, T)) / np.sqrt(N) / u).astype(np.float32),
        "dyT": (coarse(n((DV, T))) * v).astype(np.float32),
        "hT": (np.random.randint(-15, 16, (DV, T)) / 16.0).astype(np.float32),
        "ts": np.tile(r, (128, 1)).astype(np.float32),
        "wm": (n((B, DV, D)) / np.sqrt(DV) / v).astype(np.float32),
        "offs": striped(idx),
    }


def reference(xT, dyT, hT, ts, wm, offs):
    idx = unstriped(offs)
    pick = lambda x: x[:, idx].reshape(x.shape[0], B, N).transpose(1, 0, 2)
    h = pick(f64(hT))
    dz = pick(f64(ts))[:, :1, :] * pick(f64(dyT)) * (1.0 - h * h)
    gw = mxq(pick(f64(xT)), 2, "e4m3") @ mxq(dz, 2, "e5m2").transpose(0, 2, 1)
    dx = mxq(f64(wm), 1, "e4m3").transpose(0, 2, 1) @ mxq(dz, 1, "e5m2")
    gx = np.zeros((D, T))
    gx[:, idx] = dx.transpose(1, 0, 2).reshape(D, B * N)
    return gw, gx

@@ -1,0 +1,256 @@
+from contextlib import ExitStack
+
+import concourse.mybir as mybir
+from concourse.masks import make_identity
+
+B, N, T, D, DV = 2, 512, 2048, 512, 512
+FLOPS = 2 * 2 * B * N * D * DV
+
+F32 = mybir.dt.float32
+BF16 = mybir.dt.bfloat16
+U32 = mybir.dt.uint32
+U16 = mybir.dt.uint16
+U8 = mybir.dt.uint8
+E4M3 = mybir.dt.float8_e4m3fn_x4
+E5M2 = mybir.dt.float8_e5m2_x4
+ALU = mybir.AluOpType
+ACT = mybir.ActivationFunctionType
+
+P = 128
+S = B * N
+COLS = N // 16
+HALF = D // 2
+
+
+def tile_attend_gex_tnh_wx_kernel(tc, xT, dyT, hT, ts, wm, offs, out_0, out_1):
+    nc = tc.nc
+    with ExitStack() as ctx:
+        keep = ctx.enter_context(tc.tile_pool(name="keep", bufs=1))
+        loads = ctx.enter_context(tc.tile_pool(name="loads", bufs=8))
+        ring = ctx.enter_context(tc.tile_pool(name="ring", bufs=2))
+        stage = ctx.enter_context(tc.tile_pool(name="stage", bufs=4))
+        ps_turn = ctx.enter_context(tc.psum_pool(name="ps_turn", bufs=3))
+        ps_dx = ctx.enter_context(tc.psum_pool(name="ps_dx", bufs=3))
+        ps_gw = ctx.enter_context(tc.psum_pool(name="ps_gw", bufs=2))
+
+        offsets = keep.tile([P, S // 16], U16, name="offsets")
+        nc.sync.dma_start(offsets[:], offs)
+        lists = [offsets[:, b * COLS:(b + 1) * COLS] for b in range(B)]
+        slots = [slice(b * N, (b + 1) * N) for b in range(B)]
+
+        h_planes = hT.rearrange("(p t) c -> p t c", t=4)
+        dy_planes = dyT.rearrange("(p t) c -> p t c", t=4)
+
+        def load(src):
+            win = loads.tile([P, T], F32, name="win")
+            nc.sync.dma_start(win[:], src)
+            return win
+
+        def load_w(b, half):
+            w_raw = ring.tile([P, 4, HALF], F32, name="w_raw", bufs=4)
+            src = wm[b].rearrange("(p t) d -> p t d", t=4)
+            nc.sync.dma_start(w_raw[:], src[:, :, half * HALF:(half + 1) * HALF])
+            return w_raw
+
+        h_win, dy_win, x_win, w_raws = {}, {}, {}, {}
+        ts_win = load(ts)
+        h_win[0] = load(h_planes[:, 0, :])
+        h_win[1] = load(h_planes[:, 1, :])
+        dy_win[0] = load(dy_planes[:, 0, :])
+        dy_win[1] = load(dy_planes[:, 1, :])
+        x_win[0] = load(xT[0:P, :])
+        h_win[2] = load(h_planes[:, 2, :])
+        h_win[3] = load(h_planes[:, 3, :])
+        w_raws[0, 0] = load_w(0, 0)
+        dy_win[2] = load(dy_planes[:, 2, :])
+        dy_win[3] = load(dy_planes[:, 3, :])
+        w_raws[1, 0] = load_w(1, 0)
+        x_win[1] = load(xT[P:2 * P, :])
+        w_raws[0, 1] = load_w(0, 1)
+        w_raws[1, 1] = load_w(1, 1)
+        x_win[2] = load(xT[2 * P:3 * P, :])
+        x_win[3] = load(xT[3 * P:4 * P, :])
+
+        ident = keep.tile([P, P], F32, name="ident")
+        make_identity(nc, ident[:])
+        gx = [keep.tile([P, T], F32, name=f"gx{j}") for j in range(4)]
+        for j in range(4):
+            nc.vector.memset(gx[j][:], 0.0)
+
+        def mx_tiles(name):
+            codes = keep.tile([P, B, 512], U32, name=name + "_codes", align_bytes=64)
+            scales = keep.tile([P, B, 512], U8, name=name + "_scales", align_bytes=64)
+            return codes, scales
+
+        w_mx, dzn_mx, x_mx, dzs_mx = mx_tiles("w"), mx_tiles("dzn"), mx_tiles("x"), mx_tiles("dzs")
+
+        def quantize(mx, b, cols, src, fmt):
+            nc.vector.quantize_mx(out=mx[0][:, b, cols].bitcast(fmt), scales=mx[1][:, b, cols], in_=src)
+
+        tsg = keep.tile([P, S], F32, name="tsg")
+        neg_ts = keep.tile([P, S], F32, name="neg_ts")
+        hg = keep.tile([P, 2, S], F32, name="hg")
+        hsq = keep.tile([P, S, 2], F32, name="hsq")
+        dyts = keep.tile([P, 2, S], F32, name="dyts")
+        dz_pairs = keep.tile([P, 2, 2 * S], BF16, name="dz_pairs", align_bytes=64)
+        dz_words = dz_pairs[:].bitcast(F32)
+        dzn = keep.tile([P, B, 4 * N], BF16, name="dzn", align_bytes=64)
+        dzs = keep.tile([P, B, 4 * DV], BF16, name="dzs", align_bytes=64)
+        xs = keep.tile([P, B, 4 * D], BF16, name="xs", align_bytes=64)
+
+        def gather_h(t):
+            nc.vector.tensor_copy(hg[:, t % 2, :], h_win[t][:].indirect(offsets[:]))
+
+        def square_h(b):
+            nc.scalar.activation(hsq[:, slots[b], :], hg[:, :, slots[b]].rearrange("p e i -> p i e"), ACT.Square)
+
+        def gather_dy(t, b=None):
+            cols = slice(0, S) if b is None else slots[b]
+            entries = offsets[:] if b is None else lists[b]
+            nc.vector.tensor_tensor(dyts[:, t % 2, cols], dy_win[t][:].indirect(entries), neg_ts[:, cols], ALU.mult)
+
+        def form_dz(v, b):
+            nc.vector.scalar_tensor_tensor(
+                out=dz_pairs[:, v, 2 * b * N:2 * (b + 1) * N].rearrange("p (i e) -> p i e", e=2),
+                in0=hsq[:, slots[b], :],
+                scalar=1.0,
+                in1=dyts[:, :, slots[b]].rearrange("p e i -> p i e"),
+                op0=ALU.subtract,
+                op1=ALU.mult,
+            )
+
+        def join_pairs(b):
+            nc.scalar.copy(
+                dzn[:, b, :].bitcast(F32).rearrange("p (i v) -> p i v", v=2),
+                dz_words[:, :, slots[b]].rearrange("p v i -> p i v"),
+            )
+
+        def turn_dz(v, b):
+            bank = ps_turn.tile([P, 4, P], F32, name="turn")
+            for s in range(4):
+                nc.tensor.transpose(bank[:, s, :], dz_words[:, v, b * N + s:(b + 1) * N:4], ident[:])
+            nc.scalar.copy(
+                dzs[:, b, v * 1024:(v + 1) * 1024].rearrange("q (c s) -> q c s", s=4),
+                bank[:].bitcast(BF16).rearrange("q s c -> q c s"),
+            )
+
+        def prepare_x(j):
+            x_bf = ring.tile([P, T], BF16, name="x_bf")
+            for half in range(2):
+                cols = slice(half * T // 2, (half + 1) * T // 2)
+                nc.scalar.copy(x_bf[:, cols], x_win[j][:, cols])
+            xg = ring.tile([P, B, N], BF16, name="xg")
+            for b in range(B):
+                nc.scalar.activation(
+                    xg[:, b, :].rearrange("p (u q e) -> p q u e", u=2, e=2), x_bf[:].indirect(lists[b]), ACT.Copy
+                )
+            words = xg[:].bitcast(F32)
+            bank = ps_turn.tile([P, 4, P], F32, name="turn")
+            for b in range(B):
+                for u in range(2):
+                    nc.tensor.transpose(bank[:, 2 * b + u, :], words[:, b, u * P:(u + 1) * P], ident[:])
+            nc.scalar.copy(
+                xs[:].bitcast(F32)[:, :, 2 * j * P:2 * (j + 1) * P].rearrange("q b (d u) -> q b d u", u=2),
+                bank[:].rearrange("q (b u) d -> q b d u", u=2),
+            )
+
+        def prepare_w(b, half):
+            w_bf = ring.tile([P, HALF * 4], BF16, name="w_bf", align_bytes=64)
+            nc.scalar.copy(
+                w_bf[:].rearrange("p (c i t) -> p c t i", i=4, t=4),
+                w_raws[b, half][:].rearrange("p t (c i) -> p c t i", i=4),
+            )
+            quantize(w_mx, b, slice(half * HALF, (half + 1) * HALF), w_bf[:], E4M3)
+
+        def product(bank, left, right, b, j):
+            rows = slice(j * P, (j + 1) * P)
+            nc.tensor.matmul_mx(
+                out=bank[:],
+                lhsT=left[0][:, b, rows].bitcast(E4M3),
+                lhsT_scale=left[1][:, b, rows],
+                rhs=right[0][:, b, :].bitcast(E5M2),
+                rhs_scale=right[1][:, b, :],
+                start=True,
+                stop=True,
+            )
+
+        dx_tiles = {}
+
+        def make_dx(b, j):
+            bank = ps_dx.tile([P, N], F32, name="dx_bank")
+            product(bank, w_mx, dzn_mx, b, j)
+            dx = stage.tile([P, N], F32, name="dx")
+            nc.scalar.copy(dx[:], bank[:])
+            dx_tiles[b, j] = dx
+
+        def scatter_dx(j):
+            for b in range(B):
+                nc.vector.tensor_copy(gx[j][:].indirect(lists[b]), dx_tiles[b, j][:])
+            nc.sync.dma_start(out_1[j * P:(j + 1) * P, :], gx[j][:])
+
+        def make_gw(b, j):
+            bank = ps_gw.tile([P, DV], F32, name="gw_bank")
+            product(bank, x_mx, dzs_mx, b, j)
+            gw = stage.tile([P, DV], F32, name="gw")
+            nc.scalar.copy(
+                gw[:].rearrange("d (p v e) -> d p v e", v=2, e=2),
+                bank[:].rearrange("d (v p e) -> d p v e", v=2, e=2),
+            )
+            nc.sync.dma_start(out_0[b, j * P:(j + 1) * P, :], gw[:])
+
+        def finish_gw(half):
+            for b in range(B):
+                quantize(x_mx, b, slice(half * HALF, (half + 1) * HALF), xs[:, b, half * 1024:(half + 1) * 1024], E4M3)
+            for b in range(B):
+                for j in (2 * half, 2 * half + 1):
+                    make_gw(b, j)
+
+        nc.vector.tensor_copy(tsg[:], ts_win[:].indirect(offsets[:]))
+        nc.scalar.activation(neg_ts[:], tsg[:], ACT.Copy, scale=-1.0)
+
+        gather_h(0)
+        gather_h(1)
+        for b in range(B):
+            square_h(b)
+        gather_dy(0)
+        gather_dy(1)
+        for b in range(B):
+            form_dz(0, b)
+        prepare_x(0)
+        gather_h(2)
+        gather_h(3)
+        for b in range(B):
+            turn_dz(0, b)
+        for b in range(B):
+            square_h(b)
+        prepare_w(0, 0)
+        gather_dy(2)
+        for b in range(B):
+            gather_dy(3, b)
+            form_dz(1, b)
+            join_pairs(b)
+        quantize(dzn_mx, 0, slice(0, N), dzn[:, 0, :], E5M2)
+        make_dx(0, 0)
+        prepare_w(1, 0)
+        quantize(dzn_mx, 1, slice(0, N), dzn[:, 1, :], E5M2)
+        make_dx(1, 0)
+        make_dx(0, 1)
+        make_dx(1, 1)
+        prepare_x(1)
+        for b in range(B):
+            prepare_w(b, 1)
+        for b in range(B):
+            turn_dz(1, b)
+            quantize(dzs_mx, b, slice(0, DV), dzs[:, b, :], E5M2)
+        scatter_dx(0)
+        for b in range(B):
+            make_dx(b, 2)
+        finish_gw(0)
+        prepare_x(2)
+        scatter_dx(1)
+        for b in range(B):
+            make_dx(b, 3)
+        prepare_x(3)
+        finish_gw(1)
+        scatter_dx(2)
+        scatter_dx(3)

@@ -5,6 +5,7 @@ from concourse.masks import make_identity
 
 B, N, T, D, DV = 2, 512, 2048, 512, 512
 FLOPS = 2 * 2 * B * N * D * DV
+BYTES = 4 * (D * T + 2 * DV * T + T + B * DV * D + B * D * DV + D * T) + 2 * 128 * B * N // 16
 
 F32 = mybir.dt.float32
 BF16 = mybir.dt.bfloat16
@@ -26,11 +27,12 @@ def tile_attend_gex_tnh_wx_kernel(tc, xT, dyT, hT, ts, wm, offs, out_0, out_1):
     nc = tc.nc
     with ExitStack() as ctx:
         keep = ctx.enter_context(tc.tile_pool(name="keep", bufs=1))
-        loads = ctx.enter_context(tc.tile_pool(name="loads", bufs=8))
+        loads = ctx.enter_context(tc.tile_pool(name="loads", bufs=11))
         ring = ctx.enter_context(tc.tile_pool(name="ring", bufs=2))
-        stage = ctx.enter_context(tc.tile_pool(name="stage", bufs=4))
+        stage = ctx.enter_context(tc.tile_pool(name="stage", bufs=7))
         ps_turn = ctx.enter_context(tc.psum_pool(name="ps_turn", bufs=3))
-        ps_dx = ctx.enter_context(tc.psum_pool(name="ps_dx", bufs=3))
+        ps_dx = ctx.enter_context(tc.psum_pool(name="ps_dx", bufs=2))
+        ps_chain = ctx.enter_context(tc.psum_pool(name="ps_chain", bufs=1))
         ps_gw = ctx.enter_context(tc.psum_pool(name="ps_gw", bufs=2))
 
         offsets = keep.tile([P, S // 16], U16, name="offsets")
@@ -46,56 +48,59 @@ def tile_attend_gex_tnh_wx_kernel(tc, xT, dyT, hT, ts, wm, offs, out_0, out_1):
             nc.sync.dma_start(win[:], src)
             return win
 
-        def load_w(b, half):
-            w_raw = ring.tile([P, 4, HALF], F32, name="w_raw", bufs=4)
-            src = wm[b].rearrange("(p t) d -> p t d", t=4)
-            nc.sync.dma_start(w_raw[:], src[:, :, half * HALF:(half + 1) * HALF])
-            return w_raw
-
         h_win, dy_win, x_win, w_raws = {}, {}, {}, {}
-        ts_win = load(ts)
+        ts_row = keep.tile([P, T // P], F32, name="ts_row")
+        nc.sync.dma_start(ts_row[:], ts[0].rearrange("(p c) -> p c", p=P))
         h_win[0] = load(h_planes[:, 0, :])
         h_win[1] = load(h_planes[:, 1, :])
         dy_win[0] = load(dy_planes[:, 0, :])
+        w_raws[0] = load(wm[0].rearrange("(p t) d -> p (t d)", t=4))
         dy_win[1] = load(dy_planes[:, 1, :])
-        x_win[0] = load(xT[0:P, :])
+        x_win[0] = load(xT[0 * P:1 * P, :])
         h_win[2] = load(h_planes[:, 2, :])
         h_win[3] = load(h_planes[:, 3, :])
-        w_raws[0, 0] = load_w(0, 0)
         dy_win[2] = load(dy_planes[:, 2, :])
+        w_raws[1] = load(wm[1].rearrange("(p t) d -> p (t d)", t=4))
         dy_win[3] = load(dy_planes[:, 3, :])
-        w_raws[1, 0] = load_w(1, 0)
-        x_win[1] = load(xT[P:2 * P, :])
-        w_raws[0, 1] = load_w(0, 1)
-        w_raws[1, 1] = load_w(1, 1)
+        x_win[1] = load(xT[1 * P:2 * P, :])
         x_win[2] = load(xT[2 * P:3 * P, :])
         x_win[3] = load(xT[3 * P:4 * P, :])
 
         ident = keep.tile([P, P], F32, name="ident")
         make_identity(nc, ident[:])
-        gx = [keep.tile([P, T], F32, name=f"gx{j}") for j in range(4)]
-        for j in range(4):
+        minus_one = keep.tile([P, S], F32, name="minus_one")
+        nc.gpsimd.memset(minus_one[:], -1.0)
+        ts_win = keep.tile([P, T], F32, name="hsq")
+        for g in range(4):
+            bank = ps_turn.tile([P, 4, P], F32, name="turn")
+            for c in range(4):
+                column = ts_row[:, 4 * g + c:4 * g + c + 1]
+                nc.tensor.transpose(bank[:, c, :], column.to_broadcast([P, P]), ident[:])
+            nc.scalar.copy(
+                ts_win[:].rearrange("p (k c) -> p k c", c=16)[:, :, 4 * g:4 * g + 4],
+                bank[:].rearrange("p c k -> p k c"),
+            )
+        gx = [keep.tile([P, T], F32, name=f"gx{j}") for j in range(2)]
+        for j in range(2):
             nc.vector.memset(gx[j][:], 0.0)
+        for j in range(2, 4):
+            gx.append(loads.tile([P, T], F32, name="win"))
+            nc.gpsimd.memset(gx[j][:], 0.0)
 
-        def mx_tiles(name):
-            codes = keep.tile([P, B, 512], U32, name=name + "_codes", align_bytes=64)
-            scales = keep.tile([P, B, 512], U8, name=name + "_scales", align_bytes=64)
+        def quantize(name, src, words, fmt, codes=None):
+            if codes is None:
+                codes = keep.tile([P, words], U32, name=name + "_codes", align_bytes=64)
+            scales = keep.tile([P, words], U8, name=name + "_scales", align_bytes=64)
+            nc.vector.quantize_mx(out=codes[:].bitcast(fmt), scales=scales[:], in_=src)
             return codes, scales
 
-        w_mx, dzn_mx, x_mx, dzs_mx = mx_tiles("w"), mx_tiles("dzn"), mx_tiles("x"), mx_tiles("dzs")
-
-        def quantize(mx, b, cols, src, fmt):
-            nc.vector.quantize_mx(out=mx[0][:, b, cols].bitcast(fmt), scales=mx[1][:, b, cols], in_=src)
-
-        tsg = keep.tile([P, S], F32, name="tsg")
-        neg_ts = keep.tile([P, S], F32, name="neg_ts")
+        neg_ts = keep.tile([P, S], F32, name="neg_ts", align_bytes=64)
         hg = keep.tile([P, 2, S], F32, name="hg")
         hsq = keep.tile([P, S, 2], F32, name="hsq")
         dyts = keep.tile([P, 2, S], F32, name="dyts")
         dz_pairs = keep.tile([P, 2, 2 * S], BF16, name="dz_pairs", align_bytes=64)
         dz_words = dz_pairs[:].bitcast(F32)
-        dzn = keep.tile([P, B, 4 * N], BF16, name="dzn", align_bytes=64)
-        dzs = keep.tile([P, B, 4 * DV], BF16, name="dzs", align_bytes=64)
+        dzn = [keep.tile([P, 4 * N], BF16, name=f"dzn{b}", align_bytes=64) for b in range(B)]
         xs = keep.tile([P, B, 4 * D], BF16, name="xs", align_bytes=64)
 
         def gather_h(t):
@@ -121,11 +126,11 @@ def tile_attend_gex_tnh_wx_kernel(tc, xT, dyT, hT, ts, wm, offs, out_0, out_1):
 
         def join_pairs(b):
             nc.scalar.copy(
-                dzn[:, b, :].bitcast(F32).rearrange("p (i v) -> p i v", v=2),
+                dzn[b][:].bitcast(F32).rearrange("p (i v) -> p i v", v=2),
                 dz_words[:, :, slots[b]].rearrange("p v i -> p i v"),
             )
 
-        def turn_dz(v, b):
+        def turn_dz(dzs, v, b):
             bank = ps_turn.tile([P, 4, P], F32, name="turn")
             for s in range(4):
                 nc.tensor.transpose(bank[:, s, :], dz_words[:, v, b * N + s:(b + 1) * N:4], ident[:])
@@ -134,8 +139,8 @@ def tile_attend_gex_tnh_wx_kernel(tc, xT, dyT, hT, ts, wm, offs, out_0, out_1):
                 bank[:].bitcast(BF16).rearrange("q s c -> q c s"),
             )
 
-        def prepare_x(j):
-            x_bf = ring.tile([P, T], BF16, name="x_bf")
+        def prepare_x(j, pool=ps_turn, name="turn"):
+            x_bf = keep.tile([P, T], BF16, name="dzs" if j == 0 else f"x_bf{j % 2}", align_bytes=64)
             for half in range(2):
                 cols = slice(half * T // 2, (half + 1) * T // 2)
                 nc.scalar.copy(x_bf[:, cols], x_win[j][:, cols])
@@ -145,7 +150,7 @@ def tile_attend_gex_tnh_wx_kernel(tc, xT, dyT, hT, ts, wm, offs, out_0, out_1):
                     xg[:, b, :].rearrange("p (u q e) -> p q u e", u=2, e=2), x_bf[:].indirect(lists[b]), ACT.Copy
                 )
             words = xg[:].bitcast(F32)
-            bank = ps_turn.tile([P, 4, P], F32, name="turn")
+            bank = pool.tile([P, 4, P], F32, name=name)
             for b in range(B):
                 for u in range(2):
                     nc.tensor.transpose(bank[:, 2 * b + u, :], words[:, b, u * P:(u + 1) * P], ident[:])
@@ -154,62 +159,53 @@ def tile_attend_gex_tnh_wx_kernel(tc, xT, dyT, hT, ts, wm, offs, out_0, out_1):
                 bank[:].rearrange("q (b u) d -> q b d u", u=2),
             )
 
-        def prepare_w(b, half):
-            w_bf = ring.tile([P, HALF * 4], BF16, name="w_bf", align_bytes=64)
-            nc.scalar.copy(
-                w_bf[:].rearrange("p (c i t) -> p c t i", i=4, t=4),
-                w_raws[b, half][:].rearrange("p t (c i) -> p c t i", i=4),
-            )
-            quantize(w_mx, b, slice(half * HALF, (half + 1) * HALF), w_bf[:], E4M3)
+        def cast_w(b):
+            w_bf = keep.tile([P, D * 4], BF16, name=f"w_bf{b}", align_bytes=64)
+            rows = w_raws[b][:].rearrange("p (t d) -> p t d", t=4)
+            for j in range(4):
+                nc.scalar.copy(
+                    w_bf[:, j * 4 * P:(j + 1) * 4 * P].rearrange("p (c i t) -> p c t i", i=4, t=4),
+                    rows[:, :, j * P:(j + 1) * P].rearrange("p t (c i) -> p c t i", i=4),
+                )
+            return w_bf
 
-        def product(bank, left, right, b, j):
-            rows = slice(j * P, (j + 1) * P)
+        def product(bank, left, first, right):
             nc.tensor.matmul_mx(
                 out=bank[:],
-                lhsT=left[0][:, b, rows].bitcast(E4M3),
-                lhsT_scale=left[1][:, b, rows],
-                rhs=right[0][:, b, :].bitcast(E5M2),
-                rhs_scale=right[1][:, b, :],
+                lhsT=left[0][:, first:first + P].bitcast(E4M3),
+                lhsT_scale=left[1][:, first:first + P],
+                rhs=right[0][:].bitcast(E5M2),
+                rhs_scale=right[1][:],
                 start=True,
                 stop=True,
             )
 
-        dx_tiles = {}
+        w_mx, x_mx, dzn_mx, dzs_mx, dx_tiles = {}, {}, {}, {}, {}
 
-        def make_dx(b, j):
-            bank = ps_dx.tile([P, N], F32, name="dx_bank")
-            product(bank, w_mx, dzn_mx, b, j)
-            dx = stage.tile([P, N], F32, name="dx")
-            nc.scalar.copy(dx[:], bank[:])
+        def make_dx(b, j, dx, pool=ps_dx, name="dx_bank"):
+            bank = pool.tile([P, N], F32, name=name)
+            product(bank, w_mx[b], j * P, dzn_mx[b])
+            nc.scalar.copy(dx, bank[:])
             dx_tiles[b, j] = dx
 
-        def scatter_dx(j):
-            for b in range(B):
-                nc.vector.tensor_copy(gx[j][:].indirect(lists[b]), dx_tiles[b, j][:])
-            nc.sync.dma_start(out_1[j * P:(j + 1) * P, :], gx[j][:])
+        def scatter_dx(b, j):
+            nc.vector.tensor_copy(gx[j][:].indirect(lists[b]), dx_tiles[b, j])
+            if b == B - 1:
+                nc.sync.dma_start(out_1[j * P:(j + 1) * P, :], gx[j][:])
 
         def make_gw(b, j):
             bank = ps_gw.tile([P, DV], F32, name="gw_bank")
-            product(bank, x_mx, dzs_mx, b, j)
+            product(bank, x_mx[b], j * P, dzs_mx[b])
             gw = stage.tile([P, DV], F32, name="gw")
             nc.scalar.copy(
                 gw[:].rearrange("d (p v e) -> d p v e", v=2, e=2),
                 bank[:].rearrange("d (v p e) -> d p v e", v=2, e=2),
             )
-            nc.sync.dma_start(out_0[b, j * P:(j + 1) * P, :], gw[:])
-
-        def finish_gw(half):
-            for b in range(B):
-                quantize(x_mx, b, slice(half * HALF, (half + 1) * HALF), xs[:, b, half * 1024:(half + 1) * 1024], E4M3)
-            for b in range(B):
-                for j in (2 * half, 2 * half + 1):
-                    make_gw(b, j)
-
-        nc.vector.tensor_copy(tsg[:], ts_win[:].indirect(offsets[:]))
-        nc.scalar.activation(neg_ts[:], tsg[:], ACT.Copy, scale=-1.0)
+            nc.scalar.dma_start(out_0[b, j * P:(j + 1) * P, :], gw[:])
 
         gather_h(0)
         gather_h(1)
+        nc.vector.tensor_tensor(neg_ts[:], ts_win[:].indirect(offsets[:]), minus_one[:], ALU.mult)
         for b in range(B):
             square_h(b)
         gather_dy(0)
@@ -217,40 +213,42 @@ def tile_attend_gex_tnh_wx_kernel(tc, xT, dyT, hT, ts, wm, offs, out_0, out_1):
         for b in range(B):
             form_dz(0, b)
         prepare_x(0)
+        dzs = keep.tile([P, B, 4 * DV], BF16, name="dzs", align_bytes=64)
         gather_h(2)
         gather_h(3)
         for b in range(B):
-            turn_dz(0, b)
-        for b in range(B):
             square_h(b)
-        prepare_w(0, 0)
+        w_bf = [cast_w(b) for b in range(B)]
+        for b in range(B):
+            turn_dz(dzs, 0, b)
         gather_dy(2)
         for b in range(B):
             gather_dy(3, b)
             form_dz(1, b)
             join_pairs(b)
-        quantize(dzn_mx, 0, slice(0, N), dzn[:, 0, :], E5M2)
-        make_dx(0, 0)
-        prepare_w(1, 0)
-        quantize(dzn_mx, 1, slice(0, N), dzn[:, 1, :], E5M2)
-        make_dx(1, 0)
-        make_dx(0, 1)
-        make_dx(1, 1)
+        dx_early = keep.tile([P, 6, N], F32, name="dx_early")
+        for b in range(B):
+            w_codes = keep.tile([P, D], U32, name=("neg_ts", "dzn0")[b], align_bytes=64)
+            w_mx[b] = quantize(f"w{b}", w_bf[b][:], D, E4M3, w_codes)
+            dzn_mx[b] = quantize(f"dzn{b}", dzn[b][:], N, E5M2)
+        early = [(0, 0), (0, 1), (1, 0), (0, 2), (1, 1), (1, 2)]
+        for k, (b, j) in enumerate(early):
+            make_dx(b, j, dx_early[:, k, :])
+        for b, j in early:
+            scatter_dx(b, j)
         prepare_x(1)
-        for b in range(B):
-            prepare_w(b, 1)
-        for b in range(B):
-            turn_dz(1, b)
-            quantize(dzs_mx, b, slice(0, DV), dzs[:, b, :], E5M2)
-        scatter_dx(0)
-        for b in range(B):
-            make_dx(b, 2)
-        finish_gw(0)
         prepare_x(2)
-        scatter_dx(1)
         for b in range(B):
-            make_dx(b, 3)
-        prepare_x(3)
-        finish_gw(1)
-        scatter_dx(2)
-        scatter_dx(3)
+            turn_dz(dzs, 1, b)
+        prepare_x(3, ps_chain, "last")
+        dx_late = keep.tile([P, 2, N], F32, name="dx_late")
+        for b in range(B):
+            dzs_mx[b] = quantize(f"dzs{b}", dzs[:, b, :], DV, E5M2)
+        for b in range(B):
+            x_mx[b] = quantize(f"x{b}", xs[:, b, :], D, E4M3)
+            make_dx(b, 3, dx_late[:, b, :], ps_chain, "last")
+        for b in range(B):
+            for j in range(4):
+                make_gw(b, j)
+        for b in range(B):
+            scatter_dx(b, 3)

@@ -27,7 +27,7 @@ def tile_attend_gex_tnh_wx_kernel(tc, xT, dyT, hT, ts, wm, offs, out_0, out_1):
     nc = tc.nc
     with ExitStack() as ctx:
         keep = ctx.enter_context(tc.tile_pool(name="keep", bufs=1))
-        loads = ctx.enter_context(tc.tile_pool(name="loads", bufs=11))
+        loads = ctx.enter_context(tc.tile_pool(name="loads", bufs=9))
         ring = ctx.enter_context(tc.tile_pool(name="ring", bufs=2))
         stage = ctx.enter_context(tc.tile_pool(name="stage", bufs=7))
         ps_turn = ctx.enter_context(tc.psum_pool(name="ps_turn", bufs=3))
@@ -43,8 +43,8 @@ def tile_attend_gex_tnh_wx_kernel(tc, xT, dyT, hT, ts, wm, offs, out_0, out_1):
         h_planes = hT.rearrange("(p t) c -> p t c", t=4)
         dy_planes = dyT.rearrange("(p t) c -> p t c", t=4)
 
-        def load(src):
-            win = loads.tile([P, T], F32, name="win")
+        def load(src, pool=loads, name="win"):
+            win = pool.tile([P, T], F32, name=name)
             nc.sync.dma_start(win[:], src)
             return win
 
@@ -53,15 +53,19 @@ def tile_attend_gex_tnh_wx_kernel(tc, xT, dyT, hT, ts, wm, offs, out_0, out_1):
         nc.sync.dma_start(ts_row[:], ts[0].rearrange("(p c) -> p c", p=P))
         h_win[0] = load(h_planes[:, 0, :])
         h_win[1] = load(h_planes[:, 1, :])
-        dy_win[0] = load(dy_planes[:, 0, :])
+        dy_win[0] = load(dy_planes[:, 0, :], keep, "gx2")
         w_raws[0] = load(wm[0].rearrange("(p t) d -> p (t d)", t=4))
-        dy_win[1] = load(dy_planes[:, 1, :])
+        dy_win[1] = load(dy_planes[:, 1, :], keep, "gx3")
         x_win[0] = load(xT[0 * P:1 * P, :])
         h_win[2] = load(h_planes[:, 2, :])
         h_win[3] = load(h_planes[:, 3, :])
         dy_win[2] = load(dy_planes[:, 2, :])
-        w_raws[1] = load(wm[1].rearrange("(p t) d -> p (t d)", t=4))
+        w_raws[1] = loads.tile([P, T], F32, name="win")
+        w1_rows = w_raws[1][:].rearrange("p (t d) -> p t d", t=4)
+        w1_src = wm[1].rearrange("(p t) d -> p t d", t=4)
+        nc.sync.dma_start(w1_rows[:, :, :HALF], w1_src[:, :, :HALF])
         dy_win[3] = load(dy_planes[:, 3, :])
+        nc.sync.dma_start(w1_rows[:, :, HALF:], w1_src[:, :, HALF:])
         x_win[1] = load(xT[1 * P:2 * P, :])
         x_win[2] = load(xT[2 * P:3 * P, :])
         x_win[3] = load(xT[3 * P:4 * P, :])
@@ -83,9 +87,6 @@ def tile_attend_gex_tnh_wx_kernel(tc, xT, dyT, hT, ts, wm, offs, out_0, out_1):
         gx = [keep.tile([P, T], F32, name=f"gx{j}") for j in range(2)]
         for j in range(2):
             nc.vector.memset(gx[j][:], 0.0)
-        for j in range(2, 4):
-            gx.append(loads.tile([P, T], F32, name="win"))
-            nc.gpsimd.memset(gx[j][:], 0.0)
 
         def quantize(name, src, words, fmt, codes=None):
             if codes is None:
@@ -130,8 +131,8 @@ def tile_attend_gex_tnh_wx_kernel(tc, xT, dyT, hT, ts, wm, offs, out_0, out_1):
                 dz_words[:, :, slots[b]].rearrange("p v i -> p i v"),
             )
 
-        def turn_dz(dzs, v, b):
-            bank = ps_turn.tile([P, 4, P], F32, name="turn")
+        def turn_dz(dzs, v, b, pool=ps_turn, name="turn"):
+            bank = pool.tile([P, 4, P], F32, name=name)
             for s in range(4):
                 nc.tensor.transpose(bank[:, s, :], dz_words[:, v, b * N + s:(b + 1) * N:4], ident[:])
             nc.scalar.copy(
@@ -140,10 +141,13 @@ def tile_attend_gex_tnh_wx_kernel(tc, xT, dyT, hT, ts, wm, offs, out_0, out_1):
             )
 
         def prepare_x(j, pool=ps_turn, name="turn"):
-            x_bf = keep.tile([P, T], BF16, name="dzs" if j == 0 else f"x_bf{j % 2}", align_bytes=64)
+            x_bf = keep.tile([P, T], BF16, name=("dzs", "dzn1", "w_bf1", "w_bf0")[j], align_bytes=64)
             for half in range(2):
                 cols = slice(half * T // 2, (half + 1) * T // 2)
-                nc.scalar.copy(x_bf[:, cols], x_win[j][:, cols])
+                if 2 * j + half < 5:
+                    nc.scalar.copy(x_bf[:, cols], x_win[j][:, cols])
+                else:
+                    nc.gpsimd.tensor_copy(x_bf[:, cols], x_win[j][:, cols])
             xg = ring.tile([P, B, N], BF16, name="xg")
             for b in range(B):
                 nc.scalar.activation(
@@ -208,8 +212,10 @@ def tile_attend_gex_tnh_wx_kernel(tc, xT, dyT, hT, ts, wm, offs, out_0, out_1):
         nc.vector.tensor_tensor(neg_ts[:], ts_win[:].indirect(offsets[:]), minus_one[:], ALU.mult)
         for b in range(B):
             square_h(b)
-        gather_dy(0)
-        gather_dy(1)
+        for t in range(2):
+            gather_dy(t)
+            gx.append(keep.tile([P, T], F32, name=f"gx{2 + t}"))
+            nc.gpsimd.memset(gx[2 + t][:], 0.0)
         for b in range(B):
             form_dz(0, b)
         prepare_x(0)
@@ -239,7 +245,7 @@ def tile_attend_gex_tnh_wx_kernel(tc, xT, dyT, hT, ts, wm, offs, out_0, out_1):
         prepare_x(1)
         prepare_x(2)
         for b in range(B):
-            turn_dz(dzs, 1, b)
+            turn_dz(dzs, 1, b, ps_dx, "dx_bank")
         prepare_x(3, ps_chain, "last")
         dx_late = keep.tile([P, 2, N], F32, name="dx_late")
         for b in range(B):

@@ -27,13 +27,14 @@ def tile_attend_gex_tnh_wx_kernel(tc, xT, dyT, hT, ts, wm, offs, out_0, out_1):
     nc = tc.nc
     with ExitStack() as ctx:
         keep = ctx.enter_context(tc.tile_pool(name="keep", bufs=1))
-        loads = ctx.enter_context(tc.tile_pool(name="loads", bufs=9))
         ring = ctx.enter_context(tc.tile_pool(name="ring", bufs=2))
-        stage = ctx.enter_context(tc.tile_pool(name="stage", bufs=7))
         ps_turn = ctx.enter_context(tc.psum_pool(name="ps_turn", bufs=3))
         ps_dx = ctx.enter_context(tc.psum_pool(name="ps_dx", bufs=2))
         ps_chain = ctx.enter_context(tc.psum_pool(name="ps_chain", bufs=1))
         ps_gw = ctx.enter_context(tc.psum_pool(name="ps_gw", bufs=2))
+
+        def sb(name, shape, dtype):
+            return keep.tile(shape, dtype, name=name, align_bytes=64)
 
         offsets = keep.tile([P, S // 16], U16, name="offsets")
         nc.sync.dma_start(offsets[:], offs)
@@ -43,38 +44,28 @@ def tile_attend_gex_tnh_wx_kernel(tc, xT, dyT, hT, ts, wm, offs, out_0, out_1):
         h_planes = hT.rearrange("(p t) c -> p t c", t=4)
         dy_planes = dyT.rearrange("(p t) c -> p t c", t=4)
 
-        def load(src, pool=loads, name="win"):
-            win = pool.tile([P, T], F32, name=name)
+        def load(src, name):
+            win = sb(name, [P, T], F32)
             nc.sync.dma_start(win[:], src)
             return win
 
-        h_win, dy_win, x_win, w_raws = {}, {}, {}, {}
-        ts_row = keep.tile([P, T // P], F32, name="ts_row")
+        h_win, dy_win, x_raw = {}, {}, {}
+        ts_row = sb("ts_row", [P, T // P], F32)
         nc.sync.dma_start(ts_row[:], ts[0].rearrange("(p c) -> p c", p=P))
-        h_win[0] = load(h_planes[:, 0, :])
-        h_win[1] = load(h_planes[:, 1, :])
-        dy_win[0] = load(dy_planes[:, 0, :], keep, "gx2")
-        w_raws[0] = load(wm[0].rearrange("(p t) d -> p (t d)", t=4))
-        dy_win[1] = load(dy_planes[:, 1, :], keep, "gx3")
-        x_win[0] = load(xT[0 * P:1 * P, :])
-        h_win[2] = load(h_planes[:, 2, :])
-        h_win[3] = load(h_planes[:, 3, :])
-        dy_win[2] = load(dy_planes[:, 2, :])
-        w_raws[1] = loads.tile([P, T], F32, name="win")
-        w1_rows = w_raws[1][:].rearrange("p (t d) -> p t d", t=4)
-        w1_src = wm[1].rearrange("(p t) d -> p t d", t=4)
-        nc.sync.dma_start(w1_rows[:, :, :HALF], w1_src[:, :, :HALF])
-        dy_win[3] = load(dy_planes[:, 3, :])
-        nc.sync.dma_start(w1_rows[:, :, HALF:], w1_src[:, :, HALF:])
-        x_win[1] = load(xT[1 * P:2 * P, :])
-        x_win[2] = load(xT[2 * P:3 * P, :])
-        x_win[3] = load(xT[3 * P:4 * P, :])
+        h_win[0] = load(h_planes[:, 0, :], "buf_a")
+        h_win[1] = load(h_planes[:, 1, :], "buf_b")
+        dy_win[0] = load(dy_planes[:, 0, :], "gx2")
+        dy_win[1] = load(dy_planes[:, 1, :], "gx3")
+        x_raw[0] = load(xT[0 * P:1 * P, :], "buf_c")
+        h_win[2] = load(h_planes[:, 2, :], "buf_d")
+        w0_raw = load(wm[0].rearrange("(p t) d -> p (t d)", t=4), "w0_raw")
+        dy_win[2] = load(dy_planes[:, 2, :], "buf_f")
+        h_win[3] = load(h_planes[:, 3, :], "buf_e")
+        dy_win[3] = load(dy_planes[:, 3, :], "buf_g")
 
-        ident = keep.tile([P, P], F32, name="ident")
+        ident = sb("ident", [P, P], F32)
         make_identity(nc, ident[:])
-        minus_one = keep.tile([P, S], F32, name="minus_one")
-        nc.gpsimd.memset(minus_one[:], -1.0)
-        ts_win = keep.tile([P, T], F32, name="hsq")
+        ts_win = sb("ts_win", [P, T], F32)
         for g in range(4):
             bank = ps_turn.tile([P, 4, P], F32, name="turn")
             for c in range(4):
@@ -84,70 +75,80 @@ def tile_attend_gex_tnh_wx_kernel(tc, xT, dyT, hT, ts, wm, offs, out_0, out_1):
                 ts_win[:].rearrange("p (k c) -> p k c", c=16)[:, :, 4 * g:4 * g + 4],
                 bank[:].rearrange("p c k -> p k c"),
             )
-        gx = [keep.tile([P, T], F32, name=f"gx{j}") for j in range(2)]
+        gx = [sb(f"gx{j}", [P, T], F32) for j in range(2)]
         for j in range(2):
             nc.vector.memset(gx[j][:], 0.0)
 
         def quantize(name, src, words, fmt, codes=None):
             if codes is None:
-                codes = keep.tile([P, words], U32, name=name + "_codes", align_bytes=64)
-            scales = keep.tile([P, words], U8, name=name + "_scales", align_bytes=64)
-            nc.vector.quantize_mx(out=codes[:].bitcast(fmt), scales=scales[:], in_=src)
+                codes = sb(name + "_codes", [P, words], U32)[:]
+            scales = sb(name + "_scales", [P, words], U8)
+            nc.vector.quantize_mx(out=codes.bitcast(fmt), scales=scales[:], in_=src)
             return codes, scales
 
-        neg_ts = keep.tile([P, S], F32, name="neg_ts", align_bytes=64)
-        hg = keep.tile([P, 2, S], F32, name="hg")
-        hsq = keep.tile([P, S, 2], F32, name="hsq")
-        dyts = keep.tile([P, 2, S], F32, name="dyts")
-        dz_pairs = keep.tile([P, 2, 2 * S], BF16, name="dz_pairs", align_bytes=64)
-        dz_words = dz_pairs[:].bitcast(F32)
-        dzn = [keep.tile([P, 4 * N], BF16, name=f"dzn{b}", align_bytes=64) for b in range(B)]
-        xs = keep.tile([P, B, 4 * D], BF16, name="xs", align_bytes=64)
+        def product(bank, left, first, right):
+            nc.tensor.matmul_mx(
+                out=bank[:],
+                lhsT=left[0][:, first:first + P].bitcast(E4M3),
+                lhsT_scale=left[1][:, first:first + P],
+                rhs=right[0].bitcast(E5M2),
+                rhs_scale=right[1][:],
+                start=True,
+                stop=True,
+            )
+
+        tsg = sb("tsg", [P, S], F32)
+        hg = sb("hg", [P, 2, S], F32)
+        dy01 = sb("dy01", [P, 2, S], F32)
+        dy23 = sb("dy23", [P, 2, N], F32)
+        dz0 = sb("dz0", [P, 2, 2 * N], BF16)
+        dz0_words = dz0[:].bitcast(F32)
+        dzs = {0: sb("dzs0", [P, 4 * DV], BF16), 1: sb("dzs1", [P, 4 * DV], BF16)}
+        dzn = {0: sb("dzn0", [P, 4 * N], BF16), 1: sb("dzn1", [P, 4 * N], BF16)}
 
         def gather_h(t):
             nc.vector.tensor_copy(hg[:, t % 2, :], h_win[t][:].indirect(offsets[:]))
 
-        def square_h(b):
-            nc.scalar.activation(hsq[:, slots[b], :], hg[:, :, slots[b]].rearrange("p e i -> p i e"), ACT.Square)
+        def square_h(hsq, pair):
+            nc.scalar.activation(hsq, hg[:, :, slots[0]].rearrange("p e i -> p i e"), ACT.Square)
+            nc.scalar.activation(pair, hg[:, :, slots[1]], ACT.Square)
+            nc.scalar.activation(pair, pair, ACT.Copy, bias=-1.0)
 
-        def gather_dy(t, b=None):
+        def gather_dy(t, out, b=None):
             cols = slice(0, S) if b is None else slots[b]
             entries = offsets[:] if b is None else lists[b]
-            nc.vector.tensor_tensor(dyts[:, t % 2, cols], dy_win[t][:].indirect(entries), neg_ts[:, cols], ALU.mult)
+            nc.vector.tensor_tensor(out, dy_win[t][:].indirect(entries), tsg[:, cols], ALU.mult)
 
-        def form_dz(v, b):
+        def form_dz0(v, hsq, dyts, part):
             nc.vector.scalar_tensor_tensor(
-                out=dz_pairs[:, v, 2 * b * N:2 * (b + 1) * N].rearrange("p (i e) -> p i e", e=2),
-                in0=hsq[:, slots[b], :],
+                out=dz0[:, v, :].rearrange("p (i e) -> p i e", e=2)[:, part, :],
+                in0=hsq[:, part, :],
                 scalar=1.0,
-                in1=dyts[:, :, slots[b]].rearrange("p e i -> p i e"),
+                in1=dyts.rearrange("p e i -> p i e")[:, part, :],
                 op0=ALU.subtract,
                 op1=ALU.mult,
             )
 
-        def join_pairs(b):
-            nc.scalar.copy(
-                dzn[b][:].bitcast(F32).rearrange("p (i v) -> p i v", v=2),
-                dz_words[:, :, slots[b]].rearrange("p v i -> p i v"),
-            )
-
-        def turn_dz(dzs, v, b, pool=ps_turn, name="turn"):
-            bank = pool.tile([P, 4, P], F32, name=name)
+        def turn_dz0(v):
+            bank = ps_turn.tile([P, 4, P], F32, name="turn")
             for s in range(4):
-                nc.tensor.transpose(bank[:, s, :], dz_words[:, v, b * N + s:(b + 1) * N:4], ident[:])
+                nc.tensor.transpose(bank[:, s, :], dz0_words[:, v, s:N:4], ident[:])
             nc.scalar.copy(
-                dzs[:, b, v * 1024:(v + 1) * 1024].rearrange("q (c s) -> q c s", s=4),
+                dzs[0][:, v * 1024:(v + 1) * 1024].rearrange("q (c s) -> q c s", s=4),
                 bank[:].bitcast(BF16).rearrange("q s c -> q c s"),
             )
 
-        def prepare_x(j, pool=ps_turn, name="turn"):
-            x_bf = keep.tile([P, T], BF16, name=("dzs", "dzn1", "w_bf1", "w_bf0")[j], align_bytes=64)
+        def cast_x(j, name, engine):
+            x_bf = sb(name, [P, T], BF16)
             for half in range(2):
                 cols = slice(half * T // 2, (half + 1) * T // 2)
-                if 2 * j + half < 5:
-                    nc.scalar.copy(x_bf[:, cols], x_win[j][:, cols])
+                if engine == "scalar":
+                    nc.scalar.copy(x_bf[:, cols], x_raw[j][:, cols])
                 else:
-                    nc.gpsimd.tensor_copy(x_bf[:, cols], x_win[j][:, cols])
+                    nc.gpsimd.tensor_copy(x_bf[:, cols], x_raw[j][:, cols])
+            return x_bf
+
+        def turn_x(x_bf, xs, pool, name):
             xg = ring.tile([P, B, N], BF16, name="xg")
             for b in range(B):
                 nc.scalar.activation(
@@ -159,13 +160,12 @@ def tile_attend_gex_tnh_wx_kernel(tc, xT, dyT, hT, ts, wm, offs, out_0, out_1):
                 for u in range(2):
                     nc.tensor.transpose(bank[:, 2 * b + u, :], words[:, b, u * P:(u + 1) * P], ident[:])
             nc.scalar.copy(
-                xs[:].bitcast(F32)[:, :, 2 * j * P:2 * (j + 1) * P].rearrange("q b (d u) -> q b d u", u=2),
+                xs.bitcast(F32).rearrange("q (b d u) -> q b d u", b=B, u=2),
                 bank[:].rearrange("q (b u) d -> q b d u", u=2),
             )
 
-        def cast_w(b):
-            w_bf = keep.tile([P, D * 4], BF16, name=f"w_bf{b}", align_bytes=64)
-            rows = w_raws[b][:].rearrange("p (t d) -> p t d", t=4)
+        def cast_w(raw, w_bf):
+            rows = raw[:].rearrange("p (t d) -> p t d", t=4)
             for j in range(4):
                 nc.scalar.copy(
                     w_bf[:, j * 4 * P:(j + 1) * 4 * P].rearrange("p (c i t) -> p c t i", i=4, t=4),
@@ -173,88 +173,145 @@ def tile_attend_gex_tnh_wx_kernel(tc, xT, dyT, hT, ts, wm, offs, out_0, out_1):
                 )
             return w_bf
 
-        def product(bank, left, first, right):
-            nc.tensor.matmul_mx(
-                out=bank[:],
-                lhsT=left[0][:, first:first + P].bitcast(E4M3),
-                lhsT_scale=left[1][:, first:first + P],
-                rhs=right[0][:].bitcast(E5M2),
-                rhs_scale=right[1][:],
-                start=True,
-                stop=True,
-            )
-
         w_mx, x_mx, dzn_mx, dzs_mx, dx_tiles = {}, {}, {}, {}, {}
 
-        def make_dx(b, j, dx, pool=ps_dx, name="dx_bank"):
-            bank = pool.tile([P, N], F32, name=name)
-            product(bank, w_mx[b], j * P, dzn_mx[b])
-            nc.scalar.copy(dx, bank[:])
+        def make_dx(b, j, name, pool=ps_dx, bank_name="dx_bank"):
+            bank = pool.tile([P, N], F32, name=bank_name)
+            left, first = w_mx[b, j]
+            product(bank, left, first, dzn_mx[b])
+            dx = sb(name, [P, N], F32)
+            nc.scalar.mul(dx[:], bank[:], -1.0)
             dx_tiles[b, j] = dx
 
         def scatter_dx(b, j):
-            nc.vector.tensor_copy(gx[j][:].indirect(lists[b]), dx_tiles[b, j])
+            nc.vector.tensor_copy(gx[j][:].indirect(lists[b]), dx_tiles[b, j][:])
             if b == B - 1:
                 nc.sync.dma_start(out_1[j * P:(j + 1) * P, :], gx[j][:])
 
-        def make_gw(b, j):
+        def make_gw(b, j, gw):
             bank = ps_gw.tile([P, DV], F32, name="gw_bank")
-            product(bank, x_mx[b], j * P, dzs_mx[b])
-            gw = stage.tile([P, DV], F32, name="gw")
-            nc.scalar.copy(
-                gw[:].rearrange("d (p v e) -> d p v e", v=2, e=2),
+            left, first = x_mx[b, j]
+            product(bank, left, first, dzs_mx[b])
+            nc.scalar.mul(
+                gw.rearrange("d (p v e) -> d p v e", v=2, e=2),
                 bank[:].rearrange("d (v p e) -> d p v e", v=2, e=2),
+                -1.0,
             )
-            nc.scalar.dma_start(out_0[b, j * P:(j + 1) * P, :], gw[:])
+            nc.scalar.dma_start(out_0[b, j * P:(j + 1) * P, :], gw)
 
         gather_h(0)
         gather_h(1)
-        nc.vector.tensor_tensor(neg_ts[:], ts_win[:].indirect(offsets[:]), minus_one[:], ALU.mult)
         for b in range(B):
-            square_h(b)
+            nc.vector.tensor_copy(tsg[:, slots[b]], ts_win[:].indirect(lists[b]))
+        hsq0 = sb("ts_row", [P, N, 2], F32)
+        hm0 = sb("ts_win", [P, 2, N], F32)
+        square_h(hsq0[:], hm0[:])
         for t in range(2):
-            gather_dy(t)
-            gx.append(keep.tile([P, T], F32, name=f"gx{2 + t}"))
+            for b in range(B):
+                gather_dy(t, dy01[:, t, slots[b]], b)
+            gx.append(sb(f"gx{2 + t}", [P, T], F32))
             nc.gpsimd.memset(gx[2 + t][:], 0.0)
-        for b in range(B):
-            form_dz(0, b)
-        prepare_x(0)
-        dzs = keep.tile([P, B, 4 * DV], BF16, name="dzs", align_bytes=64)
+        form_dz0(0, hsq0[:], dy01[:, :, slots[0]], slice(0, N))
+        w1_raw = load(wm[1].rearrange("(p t) d -> p (t d)", t=4), "buf_a")
+        x_raw[1] = load(xT[1 * P:2 * P, :], "buf_b")
+        x0_bf = cast_x(0, "x0_bf", "scalar")
+        xs0 = sb("xs0", [P, B * 4 * P], BF16)
+        turn_x(x0_bf, xs0[:], ps_turn, "turn")
+        x_raw[2] = load(xT[2 * P:3 * P, :], "buf_c")
         gather_h(2)
+        x_raw[3] = load(xT[3 * P:4 * P, :], "buf_d")
+        w0_bf = cast_w(w0_raw, sb("w0_bf", [P, D * 4], BF16)[:])
+        gather_dy(2, dy23[:, 0, :], 0)
         gather_h(3)
+        squares = sb("w0_raw", [P, B, 2 * N], F32)
+        hsq1 = squares[:, 0, :].rearrange("p (i e) -> p i e", e=2)
+        hm1 = squares[:, 1, :].rearrange("p (e i) -> p e i", e=2)
+        turn_dz0(0)
+        square_h(hsq1, hm1)
+        gather_dy(3, dy23[:, 1, :], 0)
+        dy3_late = sb("dy3_late", [P, N], F32)
+        gather_dy(3, dy3_late[:], 1)
+        for half in range(2):
+            part = slice(half * N // 2, (half + 1) * N // 2)
+            form_dz0(1, hsq1, dy23[:], part)
+            nc.scalar.copy(
+                dzn[0][:].bitcast(F32).rearrange("p (i v) -> p i v", v=2)[:, part, :],
+                dz0_words.rearrange("p v i -> p i v")[:, part, :],
+            )
+        early_codes = sb("buf_g", [P, D + B * P], U32)
+        w0_mx = quantize("w0", w0_bf, D, E4M3, early_codes[:, :D])
+        for j in range(4):
+            w_mx[0, j] = (w0_mx, j * P)
+        x0_mx = quantize("x0", xs0[:], B * P, E4M3, early_codes[:, D:])
         for b in range(B):
-            square_h(b)
-        w_bf = [cast_w(b) for b in range(B)]
+            x_mx[b, 0] = (x0_mx, b * P)
+        dzn_mx[0] = quantize("dzn0", dzn[0][:], N, E5M2)
+        turn_dz0(1)
+        late = sb("dz0", [P, 3 * D], F32)
+        dy2_late = late[:, :N]
+        gather_dy(2, dy2_late, 1)
+        for j in range(3):
+            make_dx(0, j, f"dx0{j}")
+        dzs_mx[0] = quantize("dzs0", dzs[0][:], DV, E5M2)
+        for j in range(3):
+            scatter_dx(0, j)
+        w1_bf = cast_w(w1_raw, late[:, N:].bitcast(BF16))
+        gw_first = sb("gw_first", [P, B, DV], F32)
+        make_gw(0, 0, gw_first[:, 0, :])
+
+        dz1 = sb("dzs0", [P, 4, N], BF16)
+        dyts1 = [dy01[:, 0, slots[1]], dy01[:, 1, slots[1]], dy2_late, dy3_late[:]]
+        for t in range(4):
+            nc.gpsimd.tensor_tensor(dz1[:, t, :], (hm0[:], hm1)[t // 2][:, t % 2, :], dyts1[t], ALU.mult)
+        nc.scalar.copy(
+            dzn[1][:].rearrange("p (c i t) -> p c t i", i=4, t=4),
+            dz1[:].rearrange("p t (c i) -> p c t i", i=4),
+        )
+        dz1_words = dz1[:].bitcast(F32)
+        for v in range(2):
+            bank = ps_turn.tile([P, 4, P], F32, name="turn")
+            for e in range(2):
+                for u in range(2):
+                    nc.tensor.transpose(bank[:, 2 * e + u, :], dz1_words[:, 2 * v + e, u:N // 2:2], ident[:])
+            nc.scalar.copy(
+                dzs[1][:].bitcast(F32)[:, v * 512:(v + 1) * 512].rearrange("q (p g) -> q p g", g=4),
+                bank[:].rearrange("q g p -> q p g"),
+            )
+        x1_bf = cast_x(1, "w0_raw", "gpsimd")
+        x2_bf = cast_x(2, "buf_b", "gpsimd")
+        w1_mx = quantize("w1", w1_bf, D, E4M3, sb("dy3_late", [P, D], U32)[:])
+        dzn_mx[1] = quantize("dzn1", dzn[1][:], N, E5M2)
+        dzs_mx[1] = quantize("dzs1", dzs[1][:], DV, E5M2)
+        for j in range(4):
+            w_mx[1, j] = (w1_mx, j * P)
+        make_dx(0, 3, "dzs0")
+        scatter_dx(0, 3)
+        xs12 = sb("xs12", [P, 2, B * 4 * P], BF16)
+        turn_x(x1_bf, xs12[:, 0, :], ps_turn, "turn")
+        make_dx(1, 0, "dx10")
+        scatter_dx(1, 0)
+        x3_bf = cast_x(3, "dzs1", "gpsimd")
+        turn_x(x2_bf, xs12[:, 1, :], ps_chain, "last")
+        make_gw(1, 0, gw_first[:, 1, :])
+        x12_mx = quantize("x12", xs12[:].rearrange("q j c -> q (j c)"), 2 * B * P, E4M3)
+        for j in range(2):
+            for b in range(B):
+                x_mx[b, 1 + j] = (x12_mx, (j * B + b) * P)
+        make_dx(1, 1, "dx11", ps_chain, "last")
+        scatter_dx(1, 1)
+        xs3 = sb("xs3", [P, B * 4 * P], BF16)
+        turn_x(x3_bf, xs3[:], ps_chain, "last")
+        x3_mx = quantize("x3", xs3[:], B * P, E4M3)
         for b in range(B):
-            turn_dz(dzs, 0, b)
-        gather_dy(2)
+            x_mx[b, 3] = (x3_mx, b * P)
+        for j in (2, 3):
+            make_dx(1, j, f"dx1{j}", ps_chain, "last")
+        gw_mid = sb("buf_d", [P, 4, DV], F32)
+        for j in range(2):
+            for b in range(B):
+                make_gw(b, 1 + j, gw_mid[:, j * B + b, :])
+        gw_last = sb("gw_last", [P, B, DV], F32)
         for b in range(B):
-            gather_dy(3, b)
-            form_dz(1, b)
-            join_pairs(b)
-        dx_early = keep.tile([P, 6, N], F32, name="dx_early")
-        for b in range(B):
-            w_codes = keep.tile([P, D], U32, name=("neg_ts", "dzn0")[b], align_bytes=64)
-            w_mx[b] = quantize(f"w{b}", w_bf[b][:], D, E4M3, w_codes)
-            dzn_mx[b] = quantize(f"dzn{b}", dzn[b][:], N, E5M2)
-        early = [(0, 0), (0, 1), (1, 0), (0, 2), (1, 1), (1, 2)]
-        for k, (b, j) in enumerate(early):
-            make_dx(b, j, dx_early[:, k, :])
-        for b, j in early:
-            scatter_dx(b, j)
-        prepare_x(1)
-        prepare_x(2)
-        for b in range(B):
-            turn_dz(dzs, 1, b, ps_dx, "dx_bank")
-        prepare_x(3, ps_chain, "last")
-        dx_late = keep.tile([P, 2, N], F32, name="dx_late")
-        for b in range(B):
-            dzs_mx[b] = quantize(f"dzs{b}", dzs[:, b, :], DV, E5M2)
-        for b in range(B):
-            x_mx[b] = quantize(f"x{b}", xs[:, b, :], D, E4M3)
-            make_dx(b, 3, dx_late[:, b, :], ps_chain, "last")
-        for b in range(B):
-            for j in range(4):
-                make_gw(b, j)
-        for b in range(B):
-            scatter_dx(b, 3)
+            make_gw(b, 3, gw_last[:, b, :])
+        for j in (2, 3):
+            scatter_dx(1, j)

@@ -27,7 +27,6 @@ def tile_attend_gex_tnh_wx_kernel(tc, xT, dyT, hT, ts, wm, offs, out_0, out_1):
     nc = tc.nc
     with ExitStack() as ctx:
         keep = ctx.enter_context(tc.tile_pool(name="keep", bufs=1))
-        ring = ctx.enter_context(tc.tile_pool(name="ring", bufs=2))
         ps_turn = ctx.enter_context(tc.psum_pool(name="ps_turn", bufs=3))
         ps_dx = ctx.enter_context(tc.psum_pool(name="ps_dx", bufs=2))
         ps_chain = ctx.enter_context(tc.psum_pool(name="ps_chain", bufs=1))
@@ -37,7 +36,6 @@ def tile_attend_gex_tnh_wx_kernel(tc, xT, dyT, hT, ts, wm, offs, out_0, out_1):
             return keep.tile(shape, dtype, name=name, align_bytes=64)
 
         offsets = keep.tile([P, S // 16], U16, name="offsets")
-        nc.sync.dma_start(offsets[:], offs)
         lists = [offsets[:, b * COLS:(b + 1) * COLS] for b in range(B)]
         slots = [slice(b * N, (b + 1) * N) for b in range(B)]
 
@@ -50,6 +48,7 @@ def tile_attend_gex_tnh_wx_kernel(tc, xT, dyT, hT, ts, wm, offs, out_0, out_1):
             return win
 
         h_win, dy_win, x_raw = {}, {}, {}
+        nc.sync.dma_start(offsets[:], offs)
         ts_row = sb("ts_row", [P, T // P], F32)
         nc.sync.dma_start(ts_row[:], ts[0].rearrange("(p c) -> p c", p=P))
         h_win[0] = load(h_planes[:, 0, :], "buf_a")
@@ -59,8 +58,8 @@ def tile_attend_gex_tnh_wx_kernel(tc, xT, dyT, hT, ts, wm, offs, out_0, out_1):
         x_raw[0] = load(xT[0 * P:1 * P, :], "buf_c")
         h_win[2] = load(h_planes[:, 2, :], "buf_d")
         w0_raw = load(wm[0].rearrange("(p t) d -> p (t d)", t=4), "w0_raw")
-        dy_win[2] = load(dy_planes[:, 2, :], "buf_f")
         h_win[3] = load(h_planes[:, 3, :], "buf_e")
+        dy_win[2] = load(dy_planes[:, 2, :], "buf_f")
         dy_win[3] = load(dy_planes[:, 3, :], "buf_g")
 
         ident = sb("ident", [P, P], F32)
@@ -99,42 +98,45 @@ def tile_attend_gex_tnh_wx_kernel(tc, xT, dyT, hT, ts, wm, offs, out_0, out_1):
 
         tsg = sb("tsg", [P, S], F32)
         hg = sb("hg", [P, 2, S], F32)
-        dy01 = sb("dy01", [P, 2, S], F32)
-        dy23 = sb("dy23", [P, 2, N], F32)
-        dz0 = sb("dz0", [P, 2, 2 * N], BF16)
-        dz0_words = dz0[:].bitcast(F32)
+        dyts = [sb(f"dyts{v}", [P, 2, S], F32) for v in range(2)]
+        dz = {0: sb("dz0", [P, 2, 2 * N], BF16)}
         dzs = {0: sb("dzs0", [P, 4 * DV], BF16), 1: sb("dzs1", [P, 4 * DV], BF16)}
         dzn = {0: sb("dzn0", [P, 4 * N], BF16), 1: sb("dzn1", [P, 4 * N], BF16)}
+        halves = [slice(0, N // 2), slice(N // 2, N)]
 
         def gather_h(t):
             nc.vector.tensor_copy(hg[:, t % 2, :], h_win[t][:].indirect(offsets[:]))
 
-        def square_h(hsq, pair):
-            nc.scalar.activation(hsq, hg[:, :, slots[0]].rearrange("p e i -> p i e"), ACT.Square)
-            nc.scalar.activation(pair, hg[:, :, slots[1]], ACT.Square)
-            nc.scalar.activation(pair, pair, ACT.Copy, bias=-1.0)
+        def square_h(b, hsq):
+            nc.scalar.activation(hsq, hg[:, :, slots[b]].rearrange("p e i -> p i e"), ACT.Square)
 
-        def gather_dy(t, out, b=None):
+        def gather_dy(t, b=None):
             cols = slice(0, S) if b is None else slots[b]
             entries = offsets[:] if b is None else lists[b]
-            nc.vector.tensor_tensor(out, dy_win[t][:].indirect(entries), tsg[:, cols], ALU.mult)
+            nc.vector.tensor_tensor(dyts[t // 2][:, t % 2, cols], dy_win[t][:].indirect(entries), tsg[:, cols], ALU.mult)
 
-        def form_dz0(v, hsq, dyts, part):
+        def form_dz(v, b, hsq, part=slice(0, N)):
             nc.vector.scalar_tensor_tensor(
-                out=dz0[:, v, :].rearrange("p (i e) -> p i e", e=2)[:, part, :],
+                out=dz[b][:, v, :].rearrange("p (i e) -> p i e", e=2)[:, part, :],
                 in0=hsq[:, part, :],
                 scalar=1.0,
-                in1=dyts.rearrange("p e i -> p i e")[:, part, :],
+                in1=dyts[v][:, :, slots[b]].rearrange("p e i -> p i e")[:, part, :],
                 op0=ALU.subtract,
                 op1=ALU.mult,
             )
 
-        def turn_dz0(v):
-            bank = ps_turn.tile([P, 4, P], F32, name="turn")
-            for s in range(4):
-                nc.tensor.transpose(bank[:, s, :], dz0_words[:, v, s:N:4], ident[:])
+        def join_pairs(b, part=slice(0, N)):
             nc.scalar.copy(
-                dzs[0][:, v * 1024:(v + 1) * 1024].rearrange("q (c s) -> q c s", s=4),
+                dzn[b][:].bitcast(F32).rearrange("p (i v) -> p i v", v=2)[:, part, :],
+                dz[b][:].bitcast(F32).rearrange("p v i -> p i v")[:, part, :],
+            )
+
+        def turn_dz(v, b, pool=ps_turn, name="turn"):
+            bank = pool.tile([P, 4, P], F32, name=name)
+            for s in range(4):
+                nc.tensor.transpose(bank[:, s, :], dz[b][:].bitcast(F32)[:, v, s:N:4], ident[:])
+            nc.scalar.copy(
+                dzs[b][:, v * 1024:(v + 1) * 1024].rearrange("q (c s) -> q c s", s=4),
                 bank[:].bitcast(BF16).rearrange("q s c -> q c s"),
             )
 
@@ -148,8 +150,8 @@ def tile_attend_gex_tnh_wx_kernel(tc, xT, dyT, hT, ts, wm, offs, out_0, out_1):
                     nc.gpsimd.tensor_copy(x_bf[:, cols], x_raw[j][:, cols])
             return x_bf
 
-        def turn_x(x_bf, xs, pool, name):
-            xg = ring.tile([P, B, N], BF16, name="xg")
+        def turn_x(x_bf, xs, pool, name, xg_name):
+            xg = sb(xg_name, [P, B, N], BF16)
             for b in range(B):
                 nc.scalar.activation(
                     xg[:, b, :].rearrange("p (u q e) -> p q u e", u=2, e=2), x_bf[:].indirect(lists[b]), ACT.Copy
@@ -175,16 +177,21 @@ def tile_attend_gex_tnh_wx_kernel(tc, xT, dyT, hT, ts, wm, offs, out_0, out_1):
 
         w_mx, x_mx, dzn_mx, dzs_mx, dx_tiles = {}, {}, {}, {}, {}
 
-        def make_dx(b, j, name, pool=ps_dx, bank_name="dx_bank"):
+        def make_dx(b, j, name, pool=ps_dx, bank_name="dx_bank", parts=1):
             bank = pool.tile([P, N], F32, name=bank_name)
             left, first = w_mx[b, j]
             product(bank, left, first, dzn_mx[b])
             dx = sb(name, [P, N], F32)
-            nc.scalar.mul(dx[:], bank[:], -1.0)
+            for part in range(parts):
+                cols = slice(part * N // parts, (part + 1) * N // parts)
+                nc.scalar.mul(dx[:, cols], bank[:, cols], -1.0)
             dx_tiles[b, j] = dx
 
-        def scatter_dx(b, j):
-            nc.vector.tensor_copy(gx[j][:].indirect(lists[b]), dx_tiles[b, j][:])
+        def scatter_dx(b, j, parts=1):
+            for part in range(parts):
+                cols = slice(part * N // parts, (part + 1) * N // parts)
+                entries = offsets[:, b * COLS + part * COLS // parts:b * COLS + (part + 1) * COLS // parts]
+                nc.vector.tensor_copy(gx[j][:].indirect(entries), dx_tiles[b, j][:, cols])
             if b == B - 1:
                 nc.sync.dma_start(out_1[j * P:(j + 1) * P, :], gx[j][:])
 
@@ -203,109 +210,89 @@ def tile_attend_gex_tnh_wx_kernel(tc, xT, dyT, hT, ts, wm, offs, out_0, out_1):
         gather_h(1)
         for b in range(B):
             nc.vector.tensor_copy(tsg[:, slots[b]], ts_win[:].indirect(lists[b]))
-        hsq0 = sb("ts_row", [P, N, 2], F32)
-        hm0 = sb("ts_win", [P, 2, N], F32)
-        square_h(hsq0[:], hm0[:])
+        hsq = {(0, 0): sb("ts_row", [P, N, 2], F32)[:], (0, 1): sb("ts_win", [P, N, 2], F32)[:]}
+        for b in range(B):
+            square_h(b, hsq[0, b])
         for t in range(2):
             for b in range(B):
-                gather_dy(t, dy01[:, t, slots[b]], b)
+                gather_dy(t, b)
             gx.append(sb(f"gx{2 + t}", [P, T], F32))
             nc.gpsimd.memset(gx[2 + t][:], 0.0)
-        form_dz0(0, hsq0[:], dy01[:, :, slots[0]], slice(0, N))
+        form_dz(0, 0, hsq[0, 0])
         w1_raw = load(wm[1].rearrange("(p t) d -> p (t d)", t=4), "buf_a")
         x_raw[1] = load(xT[1 * P:2 * P, :], "buf_b")
         x0_bf = cast_x(0, "x0_bf", "scalar")
         xs0 = sb("xs0", [P, B * 4 * P], BF16)
-        turn_x(x0_bf, xs0[:], ps_turn, "turn")
+        turn_x(x0_bf, xs0[:], ps_turn, "turn", "xg0")
         x_raw[2] = load(xT[2 * P:3 * P, :], "buf_c")
         gather_h(2)
         x_raw[3] = load(xT[3 * P:4 * P, :], "buf_d")
         w0_bf = cast_w(w0_raw, sb("w0_bf", [P, D * 4], BF16)[:])
-        gather_dy(2, dy23[:, 0, :], 0)
         gather_h(3)
-        squares = sb("w0_raw", [P, B, 2 * N], F32)
-        hsq1 = squares[:, 0, :].rearrange("p (i e) -> p i e", e=2)
-        hm1 = squares[:, 1, :].rearrange("p (e i) -> p e i", e=2)
-        turn_dz0(0)
-        square_h(hsq1, hm1)
-        gather_dy(3, dy23[:, 1, :], 0)
-        dy3_late = sb("dy3_late", [P, N], F32)
-        gather_dy(3, dy3_late[:], 1)
-        for half in range(2):
-            part = slice(half * N // 2, (half + 1) * N // 2)
-            form_dz0(1, hsq1, dy23[:], part)
-            nc.scalar.copy(
-                dzn[0][:].bitcast(F32).rearrange("p (i v) -> p i v", v=2)[:, part, :],
-                dz0_words.rearrange("p v i -> p i v")[:, part, :],
-            )
+        squares = sb("w0_raw", [P, B, N, 2], F32)
+        turn_dz(0, 0)
+        for b in range(B):
+            hsq[1, b] = squares[:, b, :, :]
+            square_h(b, hsq[1, b])
+        gather_dy(2)
+        for b in range(B):
+            gather_dy(3, b)
+        for part in halves:
+            form_dz(1, 0, hsq[1, 0], part)
+            join_pairs(0, part)
         early_codes = sb("buf_g", [P, D + B * P], U32)
         w0_mx = quantize("w0", w0_bf, D, E4M3, early_codes[:, :D])
         for j in range(4):
             w_mx[0, j] = (w0_mx, j * P)
+        dzn_mx[0] = quantize("dzn0", dzn[0][:], N, E5M2)
+        turn_dz(1, 0)
+        dz[1] = sb("dz0", [P, 2, 2 * N], BF16)
+        for v in range(2):
+            form_dz(v, 1, hsq[v, 1])
         x0_mx = quantize("x0", xs0[:], B * P, E4M3, early_codes[:, D:])
         for b in range(B):
             x_mx[b, 0] = (x0_mx, b * P)
-        dzn_mx[0] = quantize("dzn0", dzn[0][:], N, E5M2)
-        turn_dz0(1)
-        late = sb("dz0", [P, 3 * D], F32)
-        dy2_late = late[:, :N]
-        gather_dy(2, dy2_late, 1)
         for j in range(3):
             make_dx(0, j, f"dx0{j}")
         dzs_mx[0] = quantize("dzs0", dzs[0][:], DV, E5M2)
         for j in range(3):
             scatter_dx(0, j)
-        w1_bf = cast_w(w1_raw, late[:, N:].bitcast(BF16))
+        x1_bf = cast_x(1, "dzs0", "gpsimd")
+        x2_bf = cast_x(2, "buf_b", "gpsimd")
+        x3_bf = cast_x(3, "buf_c", "gpsimd")
+        join_pairs(1)
+        turn_dz(0, 1)
+        turn_dz(1, 1, ps_chain, "last")
+        w1_bf = cast_w(w1_raw, sb("dz0", [P, D * 4], BF16)[:])
         gw_first = sb("gw_first", [P, B, DV], F32)
         make_gw(0, 0, gw_first[:, 0, :])
-
-        dz1 = sb("dzs0", [P, 4, N], BF16)
-        dyts1 = [dy01[:, 0, slots[1]], dy01[:, 1, slots[1]], dy2_late, dy3_late[:]]
-        for t in range(4):
-            nc.gpsimd.tensor_tensor(dz1[:, t, :], (hm0[:], hm1)[t // 2][:, t % 2, :], dyts1[t], ALU.mult)
-        nc.scalar.copy(
-            dzn[1][:].rearrange("p (c i t) -> p c t i", i=4, t=4),
-            dz1[:].rearrange("p t (c i) -> p c t i", i=4),
-        )
-        dz1_words = dz1[:].bitcast(F32)
-        for v in range(2):
-            bank = ps_turn.tile([P, 4, P], F32, name="turn")
-            for e in range(2):
-                for u in range(2):
-                    nc.tensor.transpose(bank[:, 2 * e + u, :], dz1_words[:, 2 * v + e, u:N // 2:2], ident[:])
-            nc.scalar.copy(
-                dzs[1][:].bitcast(F32)[:, v * 512:(v + 1) * 512].rearrange("q (p g) -> q p g", g=4),
-                bank[:].rearrange("q g p -> q p g"),
-            )
-        x1_bf = cast_x(1, "w0_raw", "gpsimd")
-        x2_bf = cast_x(2, "buf_b", "gpsimd")
-        w1_mx = quantize("w1", w1_bf, D, E4M3, sb("dy3_late", [P, D], U32)[:])
-        dzn_mx[1] = quantize("dzn1", dzn[1][:], N, E5M2)
-        dzs_mx[1] = quantize("dzs1", dzs[1][:], DV, E5M2)
+        late_codes = sb("buf_a", [P, 3, N], U32)
+        dzn_mx[1] = quantize("dzn1", dzn[1][:], N, E5M2, late_codes[:, 0, :])
+        dzs_mx[1] = quantize("dzs1", dzs[1][:], DV, E5M2, late_codes[:, 1, :])
+        w1_mx = quantize("w1", w1_bf, D, E4M3, late_codes[:, 2, :])
         for j in range(4):
             w_mx[1, j] = (w1_mx, j * P)
-        make_dx(0, 3, "dzs0")
-        scatter_dx(0, 3)
         xs12 = sb("xs12", [P, 2, B * 4 * P], BF16)
-        turn_x(x1_bf, xs12[:, 0, :], ps_turn, "turn")
-        make_dx(1, 0, "dx10")
+        make_dx(0, 3, "dx03", ps_chain, "last")
+        scatter_dx(0, 3)
+        turn_x(x1_bf, xs12[:, 0, :], ps_turn, "turn", "xg0")
+        turn_x(x2_bf, xs12[:, 1, :], ps_chain, "last", "xg2")
+        make_dx(1, 0, "buf_b")
         scatter_dx(1, 0)
-        x3_bf = cast_x(3, "dzs1", "gpsimd")
-        turn_x(x2_bf, xs12[:, 1, :], ps_chain, "last")
         make_gw(1, 0, gw_first[:, 1, :])
         x12_mx = quantize("x12", xs12[:].rearrange("q j c -> q (j c)"), 2 * B * P, E4M3)
         for j in range(2):
             for b in range(B):
                 x_mx[b, 1 + j] = (x12_mx, (j * B + b) * P)
-        make_dx(1, 1, "dx11", ps_chain, "last")
-        scatter_dx(1, 1)
+        for j in (1, 2):
+            make_dx(1, j, f"dx1{j}", ps_chain, "last")
+            scatter_dx(1, j)
         xs3 = sb("xs3", [P, B * 4 * P], BF16)
-        turn_x(x3_bf, xs3[:], ps_chain, "last")
+        turn_x(x3_bf, xs3[:], ps_chain, "last", "buf_d")
         x3_mx = quantize("x3", xs3[:], B * P, E4M3)
         for b in range(B):
             x_mx[b, 3] = (x3_mx, b * P)
-        for j in (2, 3):
-            make_dx(1, j, f"dx1{j}", ps_chain, "last")
+        make_dx(1, 3, "dx13", ps_chain, "last")
         gw_mid = sb("buf_d", [P, 4, DV], F32)
         for j in range(2):
             for b in range(B):
@@ -313,5 +300,4 @@ def tile_attend_gex_tnh_wx_kernel(tc, xT, dyT, hT, ts, wm, offs, out_0, out_1):
         gw_last = sb("gw_last", [P, B, DV], F32)
         for b in range(B):
             make_gw(b, 3, gw_last[:, b, :])
-        for j in (2, 3):
-            scatter_dx(1, j)
+        scatter_dx(1, 3)

@@ -252,46 +252,48 @@ def tile_attend_gex_tnh_wx_kernel(tc, xT, dyT, hT, ts, wm, offs, out_0, out_1):
         x0_mx = quantize("x0", xs0[:], B * P, E4M3, early_codes[:, D:])
         for b in range(B):
             x_mx[b, 0] = (x0_mx, b * P)
-        for j in range(3):
+        for j in range(2):
             make_dx(0, j, f"dx0{j}")
         dzs_mx[0] = quantize("dzs0", dzs[0][:], DV, E5M2)
-        for j in range(3):
+        for j in range(2):
             scatter_dx(0, j)
         x1_bf = cast_x(1, "dzs0", "gpsimd")
         x2_bf = cast_x(2, "buf_b", "gpsimd")
-        x3_bf = cast_x(3, "buf_c", "gpsimd")
         join_pairs(1)
         turn_dz(0, 1)
         turn_dz(1, 1, ps_chain, "last")
         w1_bf = cast_w(w1_raw, sb("dz0", [P, D * 4], BF16)[:])
-        gw_first = sb("gw_first", [P, B, DV], F32)
-        make_gw(0, 0, gw_first[:, 0, :])
         late_codes = sb("buf_a", [P, 3, N], U32)
+        w1_mx = quantize("w1", w1_bf, D, E4M3, late_codes[:, 2, :])
         dzn_mx[1] = quantize("dzn1", dzn[1][:], N, E5M2, late_codes[:, 0, :])
         dzs_mx[1] = quantize("dzs1", dzs[1][:], DV, E5M2, late_codes[:, 1, :])
-        w1_mx = quantize("w1", w1_bf, D, E4M3, late_codes[:, 2, :])
         for j in range(4):
             w_mx[1, j] = (w1_mx, j * P)
+        make_dx(0, 2, "dx02", ps_chain, "last")
+        scatter_dx(0, 2)
+        x3_bf = cast_x(3, "dzs1", "gpsimd")
+        gw_first = sb("gw_first", [P, B, DV], F32)
+        make_gw(0, 0, gw_first[:, 0, :])
         xs12 = sb("xs12", [P, 2, B * 4 * P], BF16)
-        make_dx(0, 3, "dx03", ps_chain, "last")
-        scatter_dx(0, 3)
         turn_x(x1_bf, xs12[:, 0, :], ps_turn, "turn", "xg0")
-        turn_x(x2_bf, xs12[:, 1, :], ps_chain, "last", "xg2")
-        make_dx(1, 0, "buf_b")
+        make_dx(1, 0, "dzs0")
         scatter_dx(1, 0)
-        make_gw(1, 0, gw_first[:, 1, :])
+        turn_x(x2_bf, xs12[:, 1, :], ps_chain, "last", "xg2")
         x12_mx = quantize("x12", xs12[:].rearrange("q j c -> q (j c)"), 2 * B * P, E4M3)
         for j in range(2):
             for b in range(B):
                 x_mx[b, 1 + j] = (x12_mx, (j * B + b) * P)
-        for j in (1, 2):
-            make_dx(1, j, f"dx1{j}", ps_chain, "last")
-            scatter_dx(1, j)
+        make_dx(1, 1, "buf_b")
+        scatter_dx(1, 1)
+        make_dx(0, 3, "dx03", ps_chain, "last")
+        scatter_dx(0, 3)
+        make_gw(1, 0, gw_first[:, 1, :])
         xs3 = sb("xs3", [P, B * 4 * P], BF16)
         turn_x(x3_bf, xs3[:], ps_chain, "last", "buf_d")
         x3_mx = quantize("x3", xs3[:], B * P, E4M3)
         for b in range(B):
             x_mx[b, 3] = (x3_mx, b * P)
+        make_dx(1, 2, "dzs1")
         make_dx(1, 3, "dx13", ps_chain, "last")
         gw_mid = sb("buf_d", [P, 4, DV], F32)
         for j in range(2):
@@ -300,4 +302,5 @@ def tile_attend_gex_tnh_wx_kernel(tc, xT, dyT, hT, ts, wm, offs, out_0, out_1):
         gw_last = sb("gw_last", [P, B, DV], F32)
         for b in range(B):
             make_gw(b, 3, gw_last[:, b, :])
-        scatter_dx(1, 3)
+        for j in (2, 3):
+            scatter_dx(1, j)

@@ -20,7 +20,7 @@ ACT = mybir.ActivationFunctionType
 P = 128
 S = B * N
 COLS = N // 16
-HALF = D // 2
+BLOCKS = D // P
 
 
 def tile_attend_gex_tnh_wx_kernel(tc, xT, dyT, hT, ts, wm, offs, out_0, out_1):
@@ -32,41 +32,44 @@ def tile_attend_gex_tnh_wx_kernel(tc, xT, dyT, hT, ts, wm, offs, out_0, out_1):
         ps_chain = ctx.enter_context(tc.psum_pool(name="ps_chain", bufs=1))
         ps_gw = ctx.enter_context(tc.psum_pool(name="ps_gw", bufs=2))
 
-        def sb(name, shape, dtype):
-            return keep.tile(shape, dtype, name=name, align_bytes=64)
+        def sb(buffer, shape, dtype):
+            return keep.tile(shape, dtype, name=buffer, align_bytes=64)
+
+        def psum(pool, shape):
+            return pool.tile(shape, F32, name="bank")
+
+        def load(src, buffer):
+            raw = sb(buffer, [P, T], F32)
+            nc.sync.dma_start(raw[:], src)
+            return raw
 
         offsets = keep.tile([P, S // 16], U16, name="offsets")
         lists = [offsets[:, b * COLS:(b + 1) * COLS] for b in range(B)]
         slots = [slice(b * N, (b + 1) * N) for b in range(B)]
-
         h_planes = hT.rearrange("(p t) c -> p t c", t=4)
         dy_planes = dyT.rearrange("(p t) c -> p t c", t=4)
+        w_rows = [wm[b].rearrange("(p t) d -> p (t d)", t=4) for b in range(B)]
 
-        def load(src, name):
-            win = sb(name, [P, T], F32)
-            nc.sync.dma_start(win[:], src)
-            return win
-
-        h_win, dy_win, x_raw = {}, {}, {}
+        h_win, dy_win, x_raw, w_raw = {}, {}, {}, {}
         nc.sync.dma_start(offsets[:], offs)
         ts_row = sb("ts_row", [P, T // P], F32)
         nc.sync.dma_start(ts_row[:], ts[0].rearrange("(p c) -> p c", p=P))
-        h_win[0] = load(h_planes[:, 0, :], "buf_a")
-        h_win[1] = load(h_planes[:, 1, :], "buf_b")
-        dy_win[0] = load(dy_planes[:, 0, :], "gx2")
-        dy_win[1] = load(dy_planes[:, 1, :], "gx3")
-        x_raw[0] = load(xT[0 * P:1 * P, :], "buf_c")
-        h_win[2] = load(h_planes[:, 2, :], "buf_d")
-        w0_raw = load(wm[0].rearrange("(p t) d -> p (t d)", t=4), "w0_raw")
-        h_win[3] = load(h_planes[:, 3, :], "buf_e")
-        dy_win[2] = load(dy_planes[:, 2, :], "buf_f")
-        dy_win[3] = load(dy_planes[:, 3, :], "buf_g")
+        h_win[0] = load(h_planes[:, 0, :], "h0")
+        h_win[1] = load(h_planes[:, 1, :], "h1")
+        dy_win[0] = load(dy_planes[:, 0, :], "dy0")
+        dy_win[1] = load(dy_planes[:, 1, :], "dy1")
+        x_raw[0] = load(xT[0 * P:1 * P, :], "x0")
+        h_win[2] = load(h_planes[:, 2, :], "h2")
+        w_raw[0] = load(w_rows[0], "w0")
+        h_win[3] = load(h_planes[:, 3, :], "h3")
+        dy_win[2] = load(dy_planes[:, 2, :], "dy2")
+        dy_win[3] = load(dy_planes[:, 3, :], "dy3")
 
         ident = sb("ident", [P, P], F32)
         make_identity(nc, ident[:])
         ts_win = sb("ts_win", [P, T], F32)
         for g in range(4):
-            bank = ps_turn.tile([P, 4, P], F32, name="turn")
+            bank = psum(ps_turn, [P, 4, P])
             for c in range(4):
                 column = ts_row[:, 4 * g + c:4 * g + c + 1]
                 nc.tensor.transpose(bank[:, c, :], column.to_broadcast([P, P]), ident[:])
@@ -74,90 +77,86 @@ def tile_attend_gex_tnh_wx_kernel(tc, xT, dyT, hT, ts, wm, offs, out_0, out_1):
                 ts_win[:].rearrange("p (k c) -> p k c", c=16)[:, :, 4 * g:4 * g + 4],
                 bank[:].rearrange("p c k -> p k c"),
             )
-        gx = [sb(f"gx{j}", [P, T], F32) for j in range(2)]
-        for j in range(2):
+
+        gx = [sb(f"gx{j}", [P, T], F32) for j in range(BLOCKS)]
+        for j in range(BLOCKS):
             nc.vector.memset(gx[j][:], 0.0)
 
-        def quantize(name, src, words, fmt, codes=None):
-            if codes is None:
-                codes = sb(name + "_codes", [P, words], U32)[:]
-            scales = sb(name + "_scales", [P, words], U8)
+        ts_g = sb("ts_g", [P, S], F32)
+        h_g = sb("h_g", [P, 2, S], F32)
+        dy_g = [sb(f"dy_g{v}", [P, 2, S], F32) for v in range(2)]
+        dz = {0: sb("dz0", [P, 2, 2 * N], BF16)}
+        dzn = [sb(f"dzn{b}", [P, 4 * N], BF16) for b in range(B)]
+        dzs, h_sq = {}, {}
+        w_mx, x_mx, dzn_mx, dzs_mx, dx_tiles = {}, {}, {}, {}, {}
+
+        def quantize(name, src, codes, fmt):
+            scales = sb(name + "_scales", [P, codes.shape[1]], U8)
             nc.vector.quantize_mx(out=codes.bitcast(fmt), scales=scales[:], in_=src)
             return codes, scales
 
-        def product(bank, left, first, right):
+        def product(bank, stationary, moving):
+            (codes, scales), first = stationary
             nc.tensor.matmul_mx(
                 out=bank[:],
-                lhsT=left[0][:, first:first + P].bitcast(E4M3),
-                lhsT_scale=left[1][:, first:first + P],
-                rhs=right[0].bitcast(E5M2),
-                rhs_scale=right[1][:],
+                lhsT=codes[:, first:first + P].bitcast(E4M3),
+                lhsT_scale=scales[:, first:first + P],
+                rhs=moving[0].bitcast(E5M2),
+                rhs_scale=moving[1][:],
                 start=True,
                 stop=True,
             )
 
-        tsg = sb("tsg", [P, S], F32)
-        hg = sb("hg", [P, 2, S], F32)
-        dyts = [sb(f"dyts{v}", [P, 2, S], F32) for v in range(2)]
-        dz = {0: sb("dz0", [P, 2, 2 * N], BF16)}
-        dzs = {0: sb("dzs0", [P, 4 * DV], BF16), 1: sb("dzs1", [P, 4 * DV], BF16)}
-        dzn = {0: sb("dzn0", [P, 4 * N], BF16), 1: sb("dzn1", [P, 4 * N], BF16)}
-        halves = [slice(0, N // 2), slice(N // 2, N)]
-
         def gather_h(t):
-            nc.vector.tensor_copy(hg[:, t % 2, :], h_win[t][:].indirect(offsets[:]))
+            nc.vector.tensor_copy(h_g[:, t % 2, :], h_win[t][:].indirect(offsets[:]))
 
-        def square_h(b, hsq):
-            nc.scalar.activation(hsq, hg[:, :, slots[b]].rearrange("p e i -> p i e"), ACT.Square)
+        def square_h(v, b, squares):
+            nc.scalar.activation(squares, h_g[:, :, slots[b]].rearrange("p e i -> p i e"), ACT.Square)
+            h_sq[v, b] = squares
 
-        def gather_dy(t, b=None):
-            cols = slice(0, S) if b is None else slots[b]
-            entries = offsets[:] if b is None else lists[b]
-            nc.vector.tensor_tensor(dyts[t // 2][:, t % 2, cols], dy_win[t][:].indirect(entries), tsg[:, cols], ALU.mult)
+        def gather_dy(t, entries, cols, factor):
+            nc.vector.tensor_tensor(dy_g[t // 2][:, t % 2, cols], dy_win[t][:].indirect(entries), factor, ALU.mult)
 
-        def form_dz(v, b, hsq, part=slice(0, N)):
+        def form_dz(v, b, part):
             nc.vector.scalar_tensor_tensor(
                 out=dz[b][:, v, :].rearrange("p (i e) -> p i e", e=2)[:, part, :],
-                in0=hsq[:, part, :],
+                in0=h_sq[v, b][:, part, :],
                 scalar=1.0,
-                in1=dyts[v][:, :, slots[b]].rearrange("p e i -> p i e")[:, part, :],
+                in1=dy_g[v][:, :, slots[b]].rearrange("p e i -> p i e")[:, part, :],
                 op0=ALU.subtract,
                 op1=ALU.mult,
             )
 
-        def join_pairs(b, part=slice(0, N)):
+        def join_pairs(b, part):
             nc.scalar.copy(
                 dzn[b][:].bitcast(F32).rearrange("p (i v) -> p i v", v=2)[:, part, :],
                 dz[b][:].bitcast(F32).rearrange("p v i -> p i v")[:, part, :],
             )
 
-        def turn_dz(v, b, pool=ps_turn, name="turn"):
-            bank = pool.tile([P, 4, P], F32, name=name)
+        def turn_dz(v, b, pool):
+            bank = psum(pool, [P, 4, P])
             for s in range(4):
                 nc.tensor.transpose(bank[:, s, :], dz[b][:].bitcast(F32)[:, v, s:N:4], ident[:])
             nc.scalar.copy(
-                dzs[b][:, v * 1024:(v + 1) * 1024].rearrange("q (c s) -> q c s", s=4),
+                dzs[b][:, v * 2 * N:(v + 1) * 2 * N].rearrange("q (c s) -> q c s", s=4),
                 bank[:].bitcast(BF16).rearrange("q s c -> q c s"),
             )
 
-        def cast_x(j, name, engine):
-            x_bf = sb(name, [P, T], BF16)
+        def cast_x(j, buffer, copy):
+            x_bf = sb(buffer, [P, T], BF16)
             for half in range(2):
                 cols = slice(half * T // 2, (half + 1) * T // 2)
-                if engine == "scalar":
-                    nc.scalar.copy(x_bf[:, cols], x_raw[j][:, cols])
-                else:
-                    nc.gpsimd.tensor_copy(x_bf[:, cols], x_raw[j][:, cols])
+                copy(x_bf[:, cols], x_raw[j][:, cols])
             return x_bf
 
-        def turn_x(x_bf, xs, pool, name, xg_name):
-            xg = sb(xg_name, [P, B, N], BF16)
+        def turn_x(x_bf, xs, pool, buffer):
+            x_g = sb(buffer, [P, B, N], BF16)
             for b in range(B):
                 nc.scalar.activation(
-                    xg[:, b, :].rearrange("p (u q e) -> p q u e", u=2, e=2), x_bf[:].indirect(lists[b]), ACT.Copy
+                    x_g[:, b, :].rearrange("p (u q e) -> p q u e", u=2, e=2), x_bf[:].indirect(lists[b]), ACT.Copy
                 )
-            words = xg[:].bitcast(F32)
-            bank = pool.tile([P, 4, P], F32, name=name)
+            words = x_g[:].bitcast(F32)
+            bank = psum(pool, [P, 4, P])
             for b in range(B):
                 for u in range(2):
                     nc.tensor.transpose(bank[:, 2 * b + u, :], words[:, b, u * P:(u + 1) * P], ident[:])
@@ -166,39 +165,41 @@ def tile_attend_gex_tnh_wx_kernel(tc, xT, dyT, hT, ts, wm, offs, out_0, out_1):
                 bank[:].rearrange("q (b u) d -> q b d u", u=2),
             )
 
-        def cast_w(raw, w_bf):
-            rows = raw[:].rearrange("p (t d) -> p t d", t=4)
-            for j in range(4):
+        def quantize_x(name, xs, blocks, codes):
+            operand = quantize(name, xs, codes, E4M3)
+            for k, j in enumerate(blocks):
+                for b in range(B):
+                    x_mx[b, j] = (operand, (k * B + b) * P)
+
+        def cast_w(b, buffer):
+            w_bf = sb(buffer, [P, D * 4], BF16)
+            rows = w_raw[b][:].rearrange("p (t d) -> p t d", t=4)
+            for j in range(BLOCKS):
                 nc.scalar.copy(
                     w_bf[:, j * 4 * P:(j + 1) * 4 * P].rearrange("p (c i t) -> p c t i", i=4, t=4),
                     rows[:, :, j * P:(j + 1) * P].rearrange("p t (c i) -> p c t i", i=4),
                 )
             return w_bf
 
-        w_mx, x_mx, dzn_mx, dzs_mx, dx_tiles = {}, {}, {}, {}, {}
+        def quantize_w(b, w_bf, codes):
+            operand = quantize(f"w{b}", w_bf[:], codes, E4M3)
+            for j in range(BLOCKS):
+                w_mx[b, j] = (operand, j * P)
 
-        def make_dx(b, j, name, pool=ps_dx, bank_name="dx_bank", parts=1):
-            bank = pool.tile([P, N], F32, name=bank_name)
-            left, first = w_mx[b, j]
-            product(bank, left, first, dzn_mx[b])
-            dx = sb(name, [P, N], F32)
-            for part in range(parts):
-                cols = slice(part * N // parts, (part + 1) * N // parts)
-                nc.scalar.mul(dx[:, cols], bank[:, cols], -1.0)
-            dx_tiles[b, j] = dx
+        def make_dx(b, j, buffer, pool):
+            bank = psum(pool, [P, N])
+            product(bank, w_mx[b, j], dzn_mx[b])
+            dx_tiles[b, j] = sb(buffer, [P, N], F32)
+            nc.scalar.mul(dx_tiles[b, j][:], bank[:], -1.0)
 
-        def scatter_dx(b, j, parts=1):
-            for part in range(parts):
-                cols = slice(part * N // parts, (part + 1) * N // parts)
-                entries = offsets[:, b * COLS + part * COLS // parts:b * COLS + (part + 1) * COLS // parts]
-                nc.vector.tensor_copy(gx[j][:].indirect(entries), dx_tiles[b, j][:, cols])
+        def scatter_dx(b, j):
+            nc.vector.tensor_copy(gx[j][:].indirect(lists[b]), dx_tiles[b, j][:])
             if b == B - 1:
                 nc.sync.dma_start(out_1[j * P:(j + 1) * P, :], gx[j][:])
 
         def make_gw(b, j, gw):
-            bank = ps_gw.tile([P, DV], F32, name="gw_bank")
-            left, first = x_mx[b, j]
-            product(bank, left, first, dzs_mx[b])
+            bank = psum(ps_gw, [P, DV])
+            product(bank, x_mx[b, j], dzs_mx[b])
             nc.scalar.mul(
                 gw.rearrange("d (p v e) -> d p v e", v=2, e=2),
                 bank[:].rearrange("d (v p e) -> d p v e", v=2, e=2),
@@ -206,99 +207,124 @@ def tile_attend_gex_tnh_wx_kernel(tc, xT, dyT, hT, ts, wm, offs, out_0, out_1):
             )
             nc.scalar.dma_start(out_0[b, j * P:(j + 1) * P, :], gw)
 
+        whole = slice(0, N)
+
         gather_h(0)
         gather_h(1)
         for b in range(B):
-            nc.vector.tensor_copy(tsg[:, slots[b]], ts_win[:].indirect(lists[b]))
-        hsq = {(0, 0): sb("ts_row", [P, N, 2], F32)[:], (0, 1): sb("ts_win", [P, N, 2], F32)[:]}
-        for b in range(B):
-            square_h(b, hsq[0, b])
+            nc.vector.tensor_copy(ts_g[:, slots[b]], ts_win[:].indirect(lists[b]))
+        square = sb("ts_row", [P, 2, N], F32)
+        nc.scalar.activation(square[:], h_g[:, :, slots[1]], ACT.Square)
+        slope = sb("slope", [P, 2, N], F32)
+        nc.scalar.activation(slope[:], square[:], ACT.Copy, bias=-1.0)
+        square_h(0, 0, sb("ts_row", [P, N, 2], F32)[:])
+        bank = psum(ps_gw, [P, 4, P])
+        for s in range(4):
+            nc.tensor.transpose(bank[:, s, :], ts_g[:, N + s:S:4], ident[:])
+        ts_cols = sb("ts_cols", [P, 4, 1], F32)
+        nc.scalar.copy(ts_cols[:], bank[:, :, 0:1])
         for t in range(2):
-            for b in range(B):
-                gather_dy(t, b)
-            gx.append(sb(f"gx{2 + t}", [P, T], F32))
-            nc.gpsimd.memset(gx[2 + t][:], 0.0)
-        form_dz(0, 0, hsq[0, 0])
-        w1_raw = load(wm[1].rearrange("(p t) d -> p (t d)", t=4), "buf_a")
-        x_raw[1] = load(xT[1 * P:2 * P, :], "buf_b")
-        x0_bf = cast_x(0, "x0_bf", "scalar")
+            gather_dy(t, lists[0], slots[0], ts_g[:, slots[0]])
+            gather_dy(t, lists[1], slots[1], slope[:, t, :])
+        form_dz(0, 0, whole)
+
+        w_raw[1] = load(w_rows[1], "h0")
+        x_raw[1] = load(xT[1 * P:2 * P, :], "h1")
+        x0_bf = cast_x(0, "x0_bf", nc.scalar.copy)
         xs0 = sb("xs0", [P, B * 4 * P], BF16)
-        turn_x(x0_bf, xs0[:], ps_turn, "turn", "xg0")
-        x_raw[2] = load(xT[2 * P:3 * P, :], "buf_c")
+        turn_x(x0_bf, xs0[:], ps_turn, "x_g0")
+        x_raw[2] = load(xT[2 * P:3 * P, :], "x0")
         gather_h(2)
-        x_raw[3] = load(xT[3 * P:4 * P, :], "buf_d")
-        w0_bf = cast_w(w0_raw, sb("w0_bf", [P, D * 4], BF16)[:])
+        x_raw[3] = load(xT[3 * P:4 * P, :], "h2")
         gather_h(3)
-        squares = sb("w0_raw", [P, B, N, 2], F32)
-        turn_dz(0, 0)
+
+        turned = sb("x0_bf", [P, 4, 2 * P], BF16)
+        for upper in range(2):
+            bank = psum(ps_turn, [P, 2, 2, P])
+            for s in range(2):
+                for e in range(2):
+                    nc.tensor.transpose(bank[:, s, e, :], dy_g[0][:, e, N + 2 * upper + s:S:4], ident[:])
+            for s in range(2):
+                nc.scalar.activation(
+                    turned[:, 2 * upper + s, :].rearrange("q (p e) -> q p e", e=2),
+                    bank[:, s, :, :].rearrange("q e p -> q p e"),
+                    ACT.Copy,
+                    scale=ts_cols[:, 2 * upper + s, :],
+                )
+        turned_back = psum(ps_gw, [P, 4, P])
+        for s in range(4):
+            nc.tensor.transpose(turned_back[:, s, :], turned[:].bitcast(F32)[:, s, :], ident[:])
+
+        w0_bf = cast_w(0, "w0_bf")
+        squares = sb("w0", [P, B, N, 2], F32)
         for b in range(B):
-            hsq[1, b] = squares[:, b, :, :]
-            square_h(b, hsq[1, b])
-        gather_dy(2)
+            square_h(1, b, squares[:, b, :, :])
+        dzs[0] = sb("h3", [P, 4 * DV], BF16)
+        turn_dz(0, 0, ps_turn)
+        gather_dy(2, offsets[:], slice(0, S), ts_g[:])
         for b in range(B):
-            gather_dy(3, b)
-        for part in halves:
-            form_dz(1, 0, hsq[1, 0], part)
+            gather_dy(3, lists[b], slots[b], ts_g[:, slots[b]])
+        for part in (slice(0, N // 2), slice(N // 2, N)):
+            form_dz(1, 0, part)
             join_pairs(0, part)
-        early_codes = sb("buf_g", [P, D + B * P], U32)
-        w0_mx = quantize("w0", w0_bf, D, E4M3, early_codes[:, :D])
-        for j in range(4):
-            w_mx[0, j] = (w0_mx, j * P)
-        dzn_mx[0] = quantize("dzn0", dzn[0][:], N, E5M2)
-        turn_dz(1, 0)
+
+        early_codes = sb("dy3", [P, D + B * P], U32)
+        quantize_w(0, w0_bf, early_codes[:, :D])
+        dzn_mx[0] = quantize("dzn0", dzn[0][:], sb("dzn0_codes", [P, N], U32)[:], E5M2)
+        turn_dz(1, 0, ps_turn)
         dz[1] = sb("dz0", [P, 2, 2 * N], BF16)
-        for v in range(2):
-            form_dz(v, 1, hsq[v, 1])
-        x0_mx = quantize("x0", xs0[:], B * P, E4M3, early_codes[:, D:])
-        for b in range(B):
-            x_mx[b, 0] = (x0_mx, b * P)
+        form_dz(1, 1, whole)
+        quantize_x("x0", xs0[:], [0], early_codes[:, D:])
         for j in range(2):
-            make_dx(0, j, f"dx0{j}")
-        dzs_mx[0] = quantize("dzs0", dzs[0][:], DV, E5M2)
+            make_dx(0, j, f"dx0{j}", ps_dx)
+        nc.scalar.copy(
+            dz[1][:].bitcast(F32)[:, 0, :].rearrange("p (q s) -> p q s", s=4),
+            turned_back[:].rearrange("p s q -> p q s"),
+        )
+        dzs_mx[0] = quantize("dzs0", dzs[0][:], sb("dzs0_codes", [P, DV], U32)[:], E5M2)
+
         for j in range(2):
             scatter_dx(0, j)
-        x1_bf = cast_x(1, "dzs0", "gpsimd")
-        x2_bf = cast_x(2, "buf_b", "gpsimd")
-        join_pairs(1)
-        turn_dz(0, 1)
-        turn_dz(1, 1, ps_chain, "last")
-        w1_bf = cast_w(w1_raw, sb("dz0", [P, D * 4], BF16)[:])
-        late_codes = sb("buf_a", [P, 3, N], U32)
-        w1_mx = quantize("w1", w1_bf, D, E4M3, late_codes[:, 2, :])
-        dzn_mx[1] = quantize("dzn1", dzn[1][:], N, E5M2, late_codes[:, 0, :])
-        dzs_mx[1] = quantize("dzs1", dzs[1][:], DV, E5M2, late_codes[:, 1, :])
-        for j in range(4):
-            w_mx[1, j] = (w1_mx, j * P)
-        make_dx(0, 2, "dx02", ps_chain, "last")
+        x1_bf = cast_x(1, "h3", nc.gpsimd.tensor_copy)
+        x2_bf = cast_x(2, "h1", nc.gpsimd.tensor_copy)
+        join_pairs(1, whole)
+        dzs[1] = sb("xs0", [P, 4 * DV], BF16)
+        nc.scalar.copy(
+            dzs[1][:, :2 * N].rearrange("q (c i s) -> q c s i", i=4, s=4),
+            turned[:].rearrange("q s (c i) -> q c s i", i=4),
+        )
+        turn_dz(1, 1, ps_chain)
+        w1_bf = cast_w(1, "dz0")
+        late_codes = sb("h0", [P, 3, N], U32)
+        quantize_w(1, w1_bf, late_codes[:, 2, :])
+        dzn_mx[1] = quantize("dzn1", dzn[1][:], late_codes[:, 0, :], E5M2)
+        dzs_mx[1] = quantize("dzs1", dzs[1][:], late_codes[:, 1, :], E5M2)
+
+        make_dx(0, 2, "dx02", ps_chain)
         scatter_dx(0, 2)
-        x3_bf = cast_x(3, "dzs1", "gpsimd")
+        x3_bf = cast_x(3, "xs0", nc.gpsimd.tensor_copy)
         gw_first = sb("gw_first", [P, B, DV], F32)
         make_gw(0, 0, gw_first[:, 0, :])
         xs12 = sb("xs12", [P, 2, B * 4 * P], BF16)
-        turn_x(x1_bf, xs12[:, 0, :], ps_turn, "turn", "xg0")
-        make_dx(1, 0, "dzs0")
+        turn_x(x1_bf, xs12[:, 0, :], ps_turn, "x_g0")
+        make_dx(1, 0, "h3", ps_dx)
         scatter_dx(1, 0)
-        turn_x(x2_bf, xs12[:, 1, :], ps_chain, "last", "xg2")
-        x12_mx = quantize("x12", xs12[:].rearrange("q j c -> q (j c)"), 2 * B * P, E4M3)
-        for j in range(2):
-            for b in range(B):
-                x_mx[b, 1 + j] = (x12_mx, (j * B + b) * P)
-        make_dx(1, 1, "buf_b")
+        turn_x(x2_bf, xs12[:, 1, :], ps_chain, "x_g2")
+        quantize_x("x12", xs12[:].rearrange("q j c -> q (j c)"), [1, 2], sb("x12_codes", [P, 2 * B * P], U32)[:])
+        make_dx(1, 1, "h1", ps_dx)
         scatter_dx(1, 1)
-        make_dx(0, 3, "dx03", ps_chain, "last")
+        make_dx(0, 3, "dx03", ps_chain)
         scatter_dx(0, 3)
         make_gw(1, 0, gw_first[:, 1, :])
         xs3 = sb("xs3", [P, B * 4 * P], BF16)
-        turn_x(x3_bf, xs3[:], ps_chain, "last", "buf_d")
-        x3_mx = quantize("x3", xs3[:], B * P, E4M3)
-        for b in range(B):
-            x_mx[b, 3] = (x3_mx, b * P)
-        make_dx(1, 2, "dzs1")
-        make_dx(1, 3, "dx13", ps_chain, "last")
-        gw_mid = sb("buf_d", [P, 4, DV], F32)
-        for j in range(2):
+        turn_x(x3_bf, xs3[:], ps_chain, "h2")
+        quantize_x("x3", xs3[:], [3], sb("x3_codes", [P, B * P], U32)[:])
+        make_dx(1, 2, "xs0", ps_dx)
+        make_dx(1, 3, "dx13", ps_chain)
+        gw_mid = sb("h2", [P, 2 * B, DV], F32)
+        for j in (1, 2):
             for b in range(B):
-                make_gw(b, 1 + j, gw_mid[:, j * B + b, :])
+                make_gw(b, j, gw_mid[:, (j - 1) * B + b, :])
         gw_last = sb("gw_last", [P, B, DV], F32)
         for b in range(B):
             make_gw(b, 3, gw_last[:, b, :])

@@ -17,6 +17,7 @@ E5M2 = mybir.dt.float8_e5m2_x4
 ALU = mybir.AluOpType
 ACT = mybir.ActivationFunctionType
 
+K = 1024
 P = 128
 S = B * N
 COLS = N // 16
@@ -27,12 +28,15 @@ def tile_attend_gex_tnh_wx_kernel(tc, xT, dyT, hT, ts, wm, offs, out_0, out_1):
     nc = tc.nc
     with ExitStack() as ctx:
         keep = ctx.enter_context(tc.tile_pool(name="keep", bufs=1))
+        relay = ctx.enter_context(tc.tile_pool(name="relay", bufs=1))
         ps_turn = ctx.enter_context(tc.psum_pool(name="ps_turn", bufs=3))
         ps_dx = ctx.enter_context(tc.psum_pool(name="ps_dx", bufs=2))
         ps_chain = ctx.enter_context(tc.psum_pool(name="ps_chain", bufs=1))
         ps_gw = ctx.enter_context(tc.psum_pool(name="ps_gw", bufs=2))
 
         def sb(buffer, shape, dtype):
+            if isinstance(buffer, tuple):
+                return relay.tile(shape, dtype, name=buffer[0], offset=buffer[1], align_bytes=64)
             return keep.tile(shape, dtype, name=buffer, align_bytes=64)
 
         def psum(pool, shape):
@@ -48,40 +52,37 @@ def tile_attend_gex_tnh_wx_kernel(tc, xT, dyT, hT, ts, wm, offs, out_0, out_1):
         slots = [slice(b * N, (b + 1) * N) for b in range(B)]
         h_planes = hT.rearrange("(p t) c -> p t c", t=4)
         dy_planes = dyT.rearrange("(p t) c -> p t c", t=4)
-        w_rows = [wm[b].rearrange("(p t) d -> p (t d)", t=4) for b in range(B)]
+        w_planes = [wm[b].rearrange("(p t) d -> p t d", t=4) for b in range(B)]
+
+        def load_w(b, half, buffer):
+            raw = sb(buffer, [P, 4, D // 2], F32)
+            nc.sync.dma_start(raw[:], w_planes[b][:, :, half * D // 2:(half + 1) * D // 2])
+            return raw[:]
 
         h_win, dy_win, x_raw, w_raw = {}, {}, {}, {}
         nc.sync.dma_start(offsets[:], offs)
-        ts_row = sb("ts_row", [P, T // P], F32)
-        nc.sync.dma_start(ts_row[:], ts[0].rearrange("(p c) -> p c", p=P))
-        h_win[0] = load(h_planes[:, 0, :], "h0")
+        ts_win = sb("ts_win", [P, T], F32)
+        nc.sync.dma_start(ts_win[P - 1:P, :], ts[0:1, :])
+        h_win[0] = load(h_planes[:, 0, :], ("h0", 22 * K))
         h_win[1] = load(h_planes[:, 1, :], "h1")
         dy_win[0] = load(dy_planes[:, 0, :], "dy0")
         dy_win[1] = load(dy_planes[:, 1, :], "dy1")
-        x_raw[0] = load(xT[0 * P:1 * P, :], "x0")
+        x_raw[0] = load(xT[0 * P:1 * P, :], ("x0", 4096))
         h_win[2] = load(h_planes[:, 2, :], "h2")
-        w_raw[0] = load(w_rows[0], "w0")
-        h_win[3] = load(h_planes[:, 3, :], "h3")
+        w_raw[0, 0] = load_w(0, 0, "w0")
+        h_win[3] = load(h_planes[:, 3, :], ("h3", 34 * K))
         dy_win[2] = load(dy_planes[:, 2, :], "dy2")
         dy_win[3] = load(dy_planes[:, 3, :], "dy3")
+        w_raw[0, 1] = load_w(0, 1, "w0_late")
 
         ident = sb("ident", [P, P], F32)
         make_identity(nc, ident[:])
-        ts_win = sb("ts_win", [P, T], F32)
-        for g in range(4):
-            bank = psum(ps_turn, [P, 4, P])
-            for c in range(4):
-                column = ts_row[:, 4 * g + c:4 * g + c + 1]
-                nc.tensor.transpose(bank[:, c, :], column.to_broadcast([P, P]), ident[:])
-            nc.scalar.copy(
-                ts_win[:].rearrange("p (k c) -> p k c", c=16)[:, :, 4 * g:4 * g + 4],
-                bank[:].rearrange("p c k -> p k c"),
-            )
-
-        gx = [sb(f"gx{j}", [P, T], F32) for j in range(BLOCKS)]
-        for j in range(BLOCKS):
+        nc.vector.memset(ts_win[:P - 1, :], 0.0)
+        gx = {j: sb(f"gx{j}", [P, T], F32) for j in range(2)}
+        for j in range(2):
             nc.vector.memset(gx[j][:], 0.0)
 
+        ts_row = sb("ts_row", [P, S], F32)
         ts_g = sb("ts_g", [P, S], F32)
         h_g = sb("h_g", [P, 2, S], F32)
         dy_g = [sb(f"dy_g{v}", [P, 2, S], F32) for v in range(2)]
@@ -171,20 +172,17 @@ def tile_attend_gex_tnh_wx_kernel(tc, xT, dyT, hT, ts, wm, offs, out_0, out_1):
                 for b in range(B):
                     x_mx[b, j] = (operand, (k * B + b) * P)
 
-        def cast_w(b, buffer):
-            w_bf = sb(buffer, [P, D * 4], BF16)
-            rows = w_raw[b][:].rearrange("p (t d) -> p t d", t=4)
-            for j in range(BLOCKS):
+        def cast_w(b, half, w_bf):
+            for j in range(2):
                 nc.scalar.copy(
                     w_bf[:, j * 4 * P:(j + 1) * 4 * P].rearrange("p (c i t) -> p c t i", i=4, t=4),
-                    rows[:, :, j * P:(j + 1) * P].rearrange("p t (c i) -> p c t i", i=4),
+                    w_raw[b, half][:, :, j * P:(j + 1) * P].rearrange("p t (c i) -> p c t i", i=4),
                 )
-            return w_bf
 
-        def quantize_w(b, w_bf, codes):
-            operand = quantize(f"w{b}", w_bf[:], codes, E4M3)
-            for j in range(BLOCKS):
-                w_mx[b, j] = (operand, j * P)
+        def quantize_w(name, w_bf, blocks, codes):
+            operand = quantize(name, w_bf, codes, E4M3)
+            for k, block in enumerate(blocks):
+                w_mx[block] = (operand, k * P)
 
         def make_dx(b, j, buffer, pool):
             bank = psum(pool, [P, N])
@@ -209,31 +207,43 @@ def tile_attend_gex_tnh_wx_kernel(tc, xT, dyT, hT, ts, wm, offs, out_0, out_1):
 
         whole = slice(0, N)
 
-        gather_h(0)
-        gather_h(1)
+        nc.vector.tensor_copy(ts_row[:], ts_win[:].indirect(offsets[:]))
+        def spread_ts(b):
+            bank = psum(ps_dx, [P, 4, P])
+            for s in range(4):
+                nc.tensor.transpose(bank[:, s, :], ts_cols[b][:, s, :].to_broadcast([P, P]), ident[:])
+            return bank[:]
+
+        ts_cols = [sb(f"ts_cols{b}", [P, 4, 1], F32) for b in range(B)]
         for b in range(B):
-            nc.vector.tensor_copy(ts_g[:, slots[b]], ts_win[:].indirect(lists[b]))
-        square = sb("ts_row", [P, 2, N], F32)
-        nc.scalar.activation(square[:], h_g[:, :, slots[1]], ACT.Square)
+            bank = psum(ps_turn, [P, 4, P])
+            for s in range(4):
+                cols = slice(s * P, (s + 1) * P) if b == 0 else slice(N + s, S, 4)
+                nc.tensor.transpose(bank[:, s, :], ts_row[:, cols], ident[:])
+            nc.scalar.copy(ts_cols[b][:], bank[:, :, P - 1:P])
+            if b == 0:
+                nc.scalar.copy(ts_g[:, slots[0]], spread_ts(0).rearrange("p s q -> p (s q)"))
+
         slope = sb("slope", [P, 2, N], F32)
-        nc.scalar.activation(slope[:], square[:], ACT.Copy, bias=-1.0)
-        square_h(0, 0, sb("ts_row", [P, N, 2], F32)[:])
-        bank = psum(ps_gw, [P, 4, P])
-        for s in range(4):
-            nc.tensor.transpose(bank[:, s, :], ts_g[:, N + s:S:4], ident[:])
-        ts_cols = sb("ts_cols", [P, 4, 1], F32)
-        nc.scalar.copy(ts_cols[:], bank[:, :, 0:1])
+        for t in range(2):
+            gather_h(t)
+            square = sb("ts_cols0", [P, N], F32)
+            nc.scalar.activation(square[:], h_g[:, t, slots[1]], ACT.Square)
+            nc.scalar.activation(slope[:, t, :], square[:], ACT.Copy, bias=-1.0)
+        square_h(0, 0, sb("ts_cols0", [P, N, 2], F32)[:])
+        nc.scalar.copy(ts_g[:, slots[1]].rearrange("p (q s) -> p q s", s=4), spread_ts(1).rearrange("p s q -> p q s"))
         for t in range(2):
             gather_dy(t, lists[0], slots[0], ts_g[:, slots[0]])
             gather_dy(t, lists[1], slots[1], slope[:, t, :])
         form_dz(0, 0, whole)
 
-        w_raw[1] = load(w_rows[1], "h0")
+        for half in range(2):
+            w_raw[1, half] = load_w(1, half, (f"w1_{half}", (22 + 4 * half) * K))
         x_raw[1] = load(xT[1 * P:2 * P, :], "h1")
         x0_bf = cast_x(0, "x0_bf", nc.scalar.copy)
         xs0 = sb("xs0", [P, B * 4 * P], BF16)
         turn_x(x0_bf, xs0[:], ps_turn, "x_g0")
-        x_raw[2] = load(xT[2 * P:3 * P, :], "x0")
+        x_raw[2] = load(xT[2 * P:3 * P, :], ("x2", 4096))
         gather_h(2)
         x_raw[3] = load(xT[3 * P:4 * P, :], "h2")
         gather_h(3)
@@ -249,32 +259,38 @@ def tile_attend_gex_tnh_wx_kernel(tc, xT, dyT, hT, ts, wm, offs, out_0, out_1):
                     turned[:, 2 * upper + s, :].rearrange("q (p e) -> q p e", e=2),
                     bank[:, s, :, :].rearrange("q e p -> q p e"),
                     ACT.Copy,
-                    scale=ts_cols[:, 2 * upper + s, :],
+                    scale=ts_cols[1][:, 2 * upper + s, :],
                 )
         turned_back = psum(ps_gw, [P, 4, P])
         for s in range(4):
             nc.tensor.transpose(turned_back[:, s, :], turned[:].bitcast(F32)[:, s, :], ident[:])
 
-        w0_bf = cast_w(0, "w0_bf")
+        w0_bf = sb("w0_bf", [P, 2 * D], BF16)
+        cast_w(0, 0, w0_bf[:])
         squares = sb("w0", [P, B, N, 2], F32)
         for b in range(B):
             square_h(1, b, squares[:, b, :, :])
-        dzs[0] = sb("h3", [P, 4 * DV], BF16)
+        dzs[0] = sb(("dzs0", 36 * K), [P, 4 * DV], BF16)
         turn_dz(0, 0, ps_turn)
+        dzs[1] = sb(("dzs1", 30 * K), [P, 4 * DV], BF16)
+        nc.scalar.copy(
+            dzs[1][:, :2 * N].rearrange("q (c i s) -> q c s i", i=4, s=4),
+            turned[:].rearrange("q s (c i) -> q c s i", i=4),
+        )
         gather_dy(2, offsets[:], slice(0, S), ts_g[:])
         for b in range(B):
             gather_dy(3, lists[b], slots[b], ts_g[:, slots[b]])
-        for part in (slice(0, N // 2), slice(N // 2, N)):
+        for part in (slice(k * N // 4, (k + 1) * N // 4) for k in range(4)):
             form_dz(1, 0, part)
             join_pairs(0, part)
 
-        early_codes = sb("dy3", [P, D + B * P], U32)
-        quantize_w(0, w0_bf, early_codes[:, :D])
+        early_codes = sb("dy3", [P, D // 2 + B * P], U32)
+        quantize_w("w0", w0_bf[:], [(0, 0), (0, 1)], early_codes[:, :D // 2])
         dzn_mx[0] = quantize("dzn0", dzn[0][:], sb("dzn0_codes", [P, N], U32)[:], E5M2)
         turn_dz(1, 0, ps_turn)
         dz[1] = sb("dz0", [P, 2, 2 * N], BF16)
         form_dz(1, 1, whole)
-        quantize_x("x0", xs0[:], [0], early_codes[:, D:])
+        quantize_x("x0", xs0[:], [0], early_codes[:, D // 2:])
         for j in range(2):
             make_dx(0, j, f"dx0{j}", ps_dx)
         nc.scalar.copy(
@@ -285,41 +301,47 @@ def tile_attend_gex_tnh_wx_kernel(tc, xT, dyT, hT, ts, wm, offs, out_0, out_1):
 
         for j in range(2):
             scatter_dx(0, j)
-        x1_bf = cast_x(1, "h3", nc.gpsimd.tensor_copy)
-        x2_bf = cast_x(2, "h1", nc.gpsimd.tensor_copy)
+        x1_bf = cast_x(1, ("x1_bf", 34 * K), nc.gpsimd.tensor_copy)
+        gx[2] = sb("h1", [P, T], F32)
+        nc.gpsimd.memset(gx[2][:], 0.0)
         join_pairs(1, whole)
-        dzs[1] = sb("xs0", [P, 4 * DV], BF16)
-        nc.scalar.copy(
-            dzs[1][:, :2 * N].rearrange("q (c i s) -> q c s i", i=4, s=4),
-            turned[:].rearrange("q s (c i) -> q c s i", i=4),
-        )
         turn_dz(1, 1, ps_chain)
-        w1_bf = cast_w(1, "dz0")
-        late_codes = sb("h0", [P, 3, N], U32)
-        quantize_w(1, w1_bf, late_codes[:, 2, :])
+        w0_late = sb(("w0_late_bf", 38 * K), [P, 2 * D], BF16)
+        cast_w(0, 1, w0_late[:])
+        w1_bf = sb("dz0", [P, 2 * D], BF16)
+        cast_w(1, 0, w1_bf[:])
+        late_codes = sb(("late_codes", 17 * K), [P, 3, N], U32)
+        quantize_w("w0_late", w0_late[:], [(0, 2), (0, 3)], late_codes[:, 2, D // 2:])
+        quantize_w("w1", w1_bf[:], [(1, 0), (1, 1)], late_codes[:, 2, :D // 2])
         dzn_mx[1] = quantize("dzn1", dzn[1][:], late_codes[:, 0, :], E5M2)
         dzs_mx[1] = quantize("dzs1", dzs[1][:], late_codes[:, 1, :], E5M2)
 
         make_dx(0, 2, "dx02", ps_chain)
         scatter_dx(0, 2)
-        x3_bf = cast_x(3, "xs0", nc.gpsimd.tensor_copy)
+        x2_bf = cast_x(2, ("x2_bf", 30 * K), nc.gpsimd.tensor_copy)
+        gx[3] = sb(("gx3", 8192), [P, T], F32)
+        nc.gpsimd.memset(gx[3][:], 0.0)
+        x3_bf = cast_x(3, ("x3_bf", 1024), nc.gpsimd.tensor_copy)
         gw_first = sb("gw_first", [P, B, DV], F32)
         make_gw(0, 0, gw_first[:, 0, :])
         xs12 = sb("xs12", [P, 2, B * 4 * P], BF16)
         turn_x(x1_bf, xs12[:, 0, :], ps_turn, "x_g0")
-        make_dx(1, 0, "h3", ps_dx)
+        make_dx(1, 0, ("dx10", 34 * K), ps_dx)
         scatter_dx(1, 0)
         turn_x(x2_bf, xs12[:, 1, :], ps_chain, "x_g2")
         quantize_x("x12", xs12[:].rearrange("q j c -> q (j c)"), [1, 2], sb("x12_codes", [P, 2 * B * P], U32)[:])
-        make_dx(1, 1, "h1", ps_dx)
+        make_dx(1, 1, ("dx11", 30 * K), ps_dx)
         scatter_dx(1, 1)
+        w1_late = sb(("w1_late_bf", 32 * K), [P, 2 * D], BF16)
+        cast_w(1, 1, w1_late[:])
+        quantize_w("w1_late", w1_late[:], [(1, 2), (1, 3)], sb("w1_late_codes", [P, D // 2], U32)[:])
         make_dx(0, 3, "dx03", ps_chain)
         scatter_dx(0, 3)
         make_gw(1, 0, gw_first[:, 1, :])
         xs3 = sb("xs3", [P, B * 4 * P], BF16)
         turn_x(x3_bf, xs3[:], ps_chain, "h2")
         quantize_x("x3", xs3[:], [3], sb("x3_codes", [P, B * P], U32)[:])
-        make_dx(1, 2, "xs0", ps_dx)
+        make_dx(1, 2, ("dx12", 1024), ps_dx)
         make_dx(1, 3, "dx13", ps_chain)
         gw_mid = sb("h2", [P, 2 * B, DV], F32)
         for j in (1, 2):

@@ -61,7 +61,7 @@ def tile_attend_gex_tnh_wx_kernel(tc, xT, dyT, hT, ts, wm, offs, out_0, out_1):
 
         h_win, dy_win, x_raw, w_raw = {}, {}, {}, {}
         nc.sync.dma_start(offsets[:], offs)
-        ts_win = sb("ts_win", [P, T], F32)
+        ts_win = sb(("ts_win", 48 * K), [P, T], F32)
         nc.sync.dma_start(ts_win[P - 1:P, :], ts[0:1, :])
         h_win[0] = load(h_planes[:, 0, :], ("h0", 22 * K))
         h_win[1] = load(h_planes[:, 1, :], "h1")
@@ -69,25 +69,22 @@ def tile_attend_gex_tnh_wx_kernel(tc, xT, dyT, hT, ts, wm, offs, out_0, out_1):
         dy_win[1] = load(dy_planes[:, 1, :], "dy1")
         x_raw[0] = load(xT[0 * P:1 * P, :], ("x0", 4096))
         h_win[2] = load(h_planes[:, 2, :], "h2")
-        w_raw[0, 0] = load_w(0, 0, "w0")
         h_win[3] = load(h_planes[:, 3, :], ("h3", 34 * K))
         dy_win[2] = load(dy_planes[:, 2, :], "dy2")
         dy_win[3] = load(dy_planes[:, 3, :], "dy3")
+        w_raw[0, 0] = load_w(0, 0, "dzn0")
         w_raw[0, 1] = load_w(0, 1, "w0_late")
 
         ident = sb("ident", [P, P], F32)
         make_identity(nc, ident[:])
         nc.vector.memset(ts_win[:P - 1, :], 0.0)
-        gx = {j: sb(f"gx{j}", [P, T], F32) for j in range(2)}
-        for j in range(2):
-            nc.vector.memset(gx[j][:], 0.0)
 
         ts_row = sb("ts_row", [P, S], F32)
         ts_g = sb("ts_g", [P, S], F32)
         h_g = sb("h_g", [P, 2, S], F32)
         dy_g = [sb(f"dy_g{v}", [P, 2, S], F32) for v in range(2)]
         dz = {0: sb("dz0", [P, 2, 2 * N], BF16)}
-        dzn = [sb(f"dzn{b}", [P, 4 * N], BF16) for b in range(B)]
+        dzn = {1: sb("dzn1", [P, 4 * N], BF16)}
         dzs, h_sq = {}, {}
         w_mx, x_mx, dzn_mx, dzs_mx, dx_tiles = {}, {}, {}, {}, {}
 
@@ -208,6 +205,10 @@ def tile_attend_gex_tnh_wx_kernel(tc, xT, dyT, hT, ts, wm, offs, out_0, out_1):
         whole = slice(0, N)
 
         nc.vector.tensor_copy(ts_row[:], ts_win[:].indirect(offsets[:]))
+        gx = {j: sb((f"gx{j}", (44 + 8 * j) * K), [P, T], F32) for j in range(2)}
+        for j in range(2):
+            nc.gpsimd.memset(gx[j][:], 0.0)
+
         def spread_ts(b):
             bank = psum(ps_dx, [P, 4, P])
             for s in range(4):
@@ -224,6 +225,8 @@ def tile_attend_gex_tnh_wx_kernel(tc, xT, dyT, hT, ts, wm, offs, out_0, out_1):
             if b == 0:
                 nc.scalar.copy(ts_g[:, slots[0]], spread_ts(0).rearrange("p s q -> p (s q)"))
 
+        gx[2] = sb("ts_row", [P, T], F32)
+        nc.gpsimd.memset(gx[2][:], 0.0)
         slope = sb("slope", [P, 2, N], F32)
         for t in range(2):
             gather_h(t)
@@ -236,12 +239,14 @@ def tile_attend_gex_tnh_wx_kernel(tc, xT, dyT, hT, ts, wm, offs, out_0, out_1):
             gather_dy(t, lists[0], slots[0], ts_g[:, slots[0]])
             gather_dy(t, lists[1], slots[1], slope[:, t, :])
         form_dz(0, 0, whole)
+        gx[3] = sb("ts_cols0", [P, T], F32)
+        nc.gpsimd.memset(gx[3][:], 0.0)
 
         for half in range(2):
             w_raw[1, half] = load_w(1, half, (f"w1_{half}", (22 + 4 * half) * K))
         x_raw[1] = load(xT[1 * P:2 * P, :], "h1")
         x0_bf = cast_x(0, "x0_bf", nc.scalar.copy)
-        xs0 = sb("xs0", [P, B * 4 * P], BF16)
+        xs0 = sb(("xs0", 30 * K), [P, B * 4 * P], BF16)
         turn_x(x0_bf, xs0[:], ps_turn, "x_g0")
         x_raw[2] = load(xT[2 * P:3 * P, :], ("x2", 4096))
         gather_h(2)
@@ -265,21 +270,16 @@ def tile_attend_gex_tnh_wx_kernel(tc, xT, dyT, hT, ts, wm, offs, out_0, out_1):
         for s in range(4):
             nc.tensor.transpose(turned_back[:, s, :], turned[:].bitcast(F32)[:, s, :], ident[:])
 
-        w0_bf = sb("w0_bf", [P, 2 * D], BF16)
-        cast_w(0, 0, w0_bf[:])
-        squares = sb("w0", [P, B, N, 2], F32)
-        for b in range(B):
-            square_h(1, b, squares[:, b, :, :])
-        dzs[0] = sb(("dzs0", 36 * K), [P, 4 * DV], BF16)
+        for b, buffer in enumerate(("squares", ("squares1", 38 * K))):
+            square_h(1, b, sb(buffer, [P, N, 2], F32)[:])
+        dzs[0] = sb(("dzs0", 34 * K), [P, 4 * DV], BF16)
         turn_dz(0, 0, ps_turn)
-        dzs[1] = sb(("dzs1", 30 * K), [P, 4 * DV], BF16)
-        nc.scalar.copy(
-            dzs[1][:, :2 * N].rearrange("q (c i s) -> q c s i", i=4, s=4),
-            turned[:].rearrange("q s (c i) -> q c s i", i=4),
-        )
         gather_dy(2, offsets[:], slice(0, S), ts_g[:])
         for b in range(B):
             gather_dy(3, lists[b], slots[b], ts_g[:, slots[b]])
+        w0_bf = sb("w0_bf", [P, 2 * D], BF16)
+        cast_w(0, 0, w0_bf[:])
+        dzn[0] = sb("dzn0", [P, 4 * N], BF16)
         for part in (slice(k * N // 4, (k + 1) * N // 4) for k in range(4)):
             form_dz(1, 0, part)
             join_pairs(0, part)
@@ -291,48 +291,49 @@ def tile_attend_gex_tnh_wx_kernel(tc, xT, dyT, hT, ts, wm, offs, out_0, out_1):
         dz[1] = sb("dz0", [P, 2, 2 * N], BF16)
         form_dz(1, 1, whole)
         quantize_x("x0", xs0[:], [0], early_codes[:, D // 2:])
-        for j in range(2):
-            make_dx(0, j, f"dx0{j}", ps_dx)
+        make_dx(0, 0, "dx00", ps_dx)
+        dzs_mx[0] = quantize("dzs0", dzs[0][:], sb("dzs0_codes", [P, DV], U32)[:], E5M2)
+
+        scatter_dx(0, 0)
+        x1_bf = cast_x(1, ("x1_bf", 36 * K), nc.gpsimd.tensor_copy)
+        w0_late = sb(("w0_late_bf", 40 * K), [P, 2 * D], BF16)
+        cast_w(0, 1, w0_late[:])
+        quantize_w("w0_late", w0_late[:], [(0, 2), (0, 3)], sb("w0_late_codes", [P, D // 2], U32)[:])
+        make_dx(0, 1, "w0_late", ps_dx)
+        scatter_dx(0, 1)
+        x2_bf = cast_x(2, ("x2_bf", 40 * K), nc.gpsimd.tensor_copy)
         nc.scalar.copy(
             dz[1][:].bitcast(F32)[:, 0, :].rearrange("p (q s) -> p q s", s=4),
             turned_back[:].rearrange("p s q -> p q s"),
         )
-        dzs_mx[0] = quantize("dzs0", dzs[0][:], sb("dzs0_codes", [P, DV], U32)[:], E5M2)
-
-        for j in range(2):
-            scatter_dx(0, j)
-        x1_bf = cast_x(1, ("x1_bf", 34 * K), nc.gpsimd.tensor_copy)
-        gx[2] = sb("h1", [P, T], F32)
-        nc.gpsimd.memset(gx[2][:], 0.0)
         join_pairs(1, whole)
+        dzs[1] = sb("dy_g1", [P, 4 * DV], BF16)
+        nc.scalar.copy(
+            dzs[1][:, :2 * N].rearrange("q (c i s) -> q c s i", i=4, s=4),
+            turned[:].rearrange("q s (c i) -> q c s i", i=4),
+        )
         turn_dz(1, 1, ps_chain)
-        w0_late = sb(("w0_late_bf", 38 * K), [P, 2 * D], BF16)
-        cast_w(0, 1, w0_late[:])
         w1_bf = sb("dz0", [P, 2 * D], BF16)
         cast_w(1, 0, w1_bf[:])
         late_codes = sb(("late_codes", 17 * K), [P, 3, N], U32)
-        quantize_w("w0_late", w0_late[:], [(0, 2), (0, 3)], late_codes[:, 2, D // 2:])
         quantize_w("w1", w1_bf[:], [(1, 0), (1, 1)], late_codes[:, 2, :D // 2])
         dzn_mx[1] = quantize("dzn1", dzn[1][:], late_codes[:, 0, :], E5M2)
         dzs_mx[1] = quantize("dzs1", dzs[1][:], late_codes[:, 1, :], E5M2)
 
         make_dx(0, 2, "dx02", ps_chain)
         scatter_dx(0, 2)
-        x2_bf = cast_x(2, ("x2_bf", 30 * K), nc.gpsimd.tensor_copy)
-        gx[3] = sb(("gx3", 8192), [P, T], F32)
-        nc.gpsimd.memset(gx[3][:], 0.0)
-        x3_bf = cast_x(3, ("x3_bf", 1024), nc.gpsimd.tensor_copy)
+        x3_bf = cast_x(3, "dy_g1", nc.gpsimd.tensor_copy)
         gw_first = sb("gw_first", [P, B, DV], F32)
         make_gw(0, 0, gw_first[:, 0, :])
         xs12 = sb("xs12", [P, 2, B * 4 * P], BF16)
         turn_x(x1_bf, xs12[:, 0, :], ps_turn, "x_g0")
-        make_dx(1, 0, ("dx10", 34 * K), ps_dx)
+        make_dx(1, 0, ("dx10", 36 * K), ps_dx)
         scatter_dx(1, 0)
         turn_x(x2_bf, xs12[:, 1, :], ps_chain, "x_g2")
         quantize_x("x12", xs12[:].rearrange("q j c -> q (j c)"), [1, 2], sb("x12_codes", [P, 2 * B * P], U32)[:])
-        make_dx(1, 1, ("dx11", 30 * K), ps_dx)
+        make_dx(1, 1, ("dx11", 40 * K), ps_dx)
         scatter_dx(1, 1)
-        w1_late = sb(("w1_late_bf", 32 * K), [P, 2 * D], BF16)
+        w1_late = sb(("w1_late_bf", 42 * K), [P, 2 * D], BF16)
         cast_w(1, 1, w1_late[:])
         quantize_w("w1_late", w1_late[:], [(1, 2), (1, 3)], sb("w1_late_codes", [P, D // 2], U32)[:])
         make_dx(0, 3, "dx03", ps_chain)
@@ -341,7 +342,7 @@ def tile_attend_gex_tnh_wx_kernel(tc, xT, dyT, hT, ts, wm, offs, out_0, out_1):
         xs3 = sb("xs3", [P, B * 4 * P], BF16)
         turn_x(x3_bf, xs3[:], ps_chain, "h2")
         quantize_x("x3", xs3[:], [3], sb("x3_codes", [P, B * P], U32)[:])
-        make_dx(1, 2, ("dx12", 1024), ps_dx)
+        make_dx(1, 2, "dy_g1", ps_dx)
         make_dx(1, 3, "dx13", ps_chain)
         gw_mid = sb("h2", [P, 2 * B, DV], F32)
         for j in (1, 2):

@@ -20,8 +20,8 @@ ACT = mybir.ActivationFunctionType
 K = 1024
 P = 128
 S = B * N
-COLS = N // 16
 BLOCKS = D // P
+PIECE = 256
 
 
 def tile_attend_gex_tnh_wx_kernel(tc, xT, dyT, hT, ts, wm, offs, out_0, out_1):
@@ -30,8 +30,7 @@ def tile_attend_gex_tnh_wx_kernel(tc, xT, dyT, hT, ts, wm, offs, out_0, out_1):
         keep = ctx.enter_context(tc.tile_pool(name="keep", bufs=1))
         relay = ctx.enter_context(tc.tile_pool(name="relay", bufs=1))
         ps_turn = ctx.enter_context(tc.psum_pool(name="ps_turn", bufs=3))
-        ps_dx = ctx.enter_context(tc.psum_pool(name="ps_dx", bufs=2))
-        ps_chain = ctx.enter_context(tc.psum_pool(name="ps_chain", bufs=1))
+        ps_dx = ctx.enter_context(tc.psum_pool(name="ps_dx", bufs=3))
         ps_gw = ctx.enter_context(tc.psum_pool(name="ps_gw", bufs=2))
 
         def sb(buffer, shape, dtype):
@@ -48,308 +47,194 @@ def tile_attend_gex_tnh_wx_kernel(tc, xT, dyT, hT, ts, wm, offs, out_0, out_1):
             return raw
 
         offsets = keep.tile([P, S // 16], U16, name="offsets")
-        lists = [offsets[:, b * COLS:(b + 1) * COLS] for b in range(B)]
+
+        def entries(first, last):
+            return offsets[:, first // 16:last // 16]
+
         slots = [slice(b * N, (b + 1) * N) for b in range(B)]
+        lists = [entries(b * N, (b + 1) * N) for b in range(B)]
         h_planes = hT.rearrange("(p t) c -> p t c", t=4)
         dy_planes = dyT.rearrange("(p t) c -> p t c", t=4)
-        w_planes = [wm[b].rearrange("(p t) d -> p t d", t=4) for b in range(B)]
 
-        def load_w(b, half, buffer):
-            raw = sb(buffer, [P, 4, D // 2], F32)
-            nc.sync.dma_start(raw[:], w_planes[b][:, :, half * D // 2:(half + 1) * D // 2])
-            return raw[:]
-
-        h_win, dy_win, x_raw, w_raw = {}, {}, {}, {}
         nc.sync.dma_start(offsets[:], offs)
-        ts_win = sb(("ts_win", 48 * K), [P, T], F32)
+        ts_win = sb(("ts_win", 64 * K), [P, T], F32)
         nc.sync.dma_start(ts_win[P - 1:P, :], ts[0:1, :])
-        h_win[0] = load(h_planes[:, 0, :], ("h0", 22 * K))
-        h_win[1] = load(h_planes[:, 1, :], "h1")
-        dy_win[0] = load(dy_planes[:, 0, :], "dy0")
-        dy_win[1] = load(dy_planes[:, 1, :], "dy1")
-        x_raw[0] = load(xT[0 * P:1 * P, :], ("x0", 4096))
-        h_win[2] = load(h_planes[:, 2, :], "h2")
-        h_win[3] = load(h_planes[:, 3, :], ("h3", 34 * K))
-        dy_win[2] = load(dy_planes[:, 2, :], "dy2")
-        dy_win[3] = load(dy_planes[:, 3, :], "dy3")
-        w_raw[0, 0] = load_w(0, 0, "dzn0")
-        w_raw[0, 1] = load_w(0, 1, "w0_late")
+        h_win, dy_win = {}, {}
+        for t in range(4):
+            h_win[t] = load(h_planes[:, t, :], (f"h{t}", 16 * t * K))
+            dy_win[t] = load(dy_planes[:, t, :], (f"dy{t}", (16 * t + 8) * K))
+        w_raw = {}
+        for b in range(B):
+            w_raw[b] = sb((f"w_raw{b}", (72 + 24 * b) * K), [P, 4, D], F32)
+            nc.sync.dma_start(w_raw[b][:], wm[b].rearrange("(p t) d -> p t d", t=4))
 
         ident = sb("ident", [P, P], F32)
         make_identity(nc, ident[:])
         nc.vector.memset(ts_win[:P - 1, :], 0.0)
+        gx = [sb(f"gx{j}", [P, T], F32) for j in range(BLOCKS)]
+        for j in range(BLOCKS):
+            nc.gpsimd.memset(gx[j][:], 0.0)
 
-        ts_row = sb("ts_row", [P, S], F32)
+        ts_row = sb(("ts_row", 104 * K), [P, S], F32)
         ts_g = sb("ts_g", [P, S], F32)
-        h_g = sb("h_g", [P, 2, S], F32)
-        dy_g = [sb(f"dy_g{v}", [P, 2, S], F32) for v in range(2)]
-        dz = {0: sb("dz0", [P, 2, 2 * N], BF16)}
-        dzn = {1: sb("dzn1", [P, 4 * N], BF16)}
-        dzs, h_sq = {}, {}
-        w_mx, x_mx, dzn_mx, dzs_mx, dx_tiles = {}, {}, {}, {}, {}
+        dz = [sb(f"dz{b}", [P, 4, N], BF16) for b in range(B)]
+        dzs, dzs_mx = {}, {}
 
-        def quantize(name, src, codes, fmt):
-            scales = sb(name + "_scales", [P, codes.shape[1]], U8)
-            nc.vector.quantize_mx(out=codes.bitcast(fmt), scales=scales[:], in_=src)
+        def quantize(name, src, fmt, place=None):
+            codes = sb((name + "_codes", place) if place else name + "_codes", [P, src.shape[1] // 4], U32)
+            scales = sb(name + "_scales", [P, src.shape[1] // 4], U8)
+            nc.vector.quantize_mx(out=codes[:].bitcast(fmt), scales=scales[:], in_=src)
             return codes, scales
 
-        def product(bank, stationary, moving):
-            (codes, scales), first = stationary
+        def product(bank, stationary, first, moving, cols):
             nc.tensor.matmul_mx(
-                out=bank[:],
-                lhsT=codes[:, first:first + P].bitcast(E4M3),
-                lhsT_scale=scales[:, first:first + P],
-                rhs=moving[0].bitcast(E5M2),
-                rhs_scale=moving[1][:],
+                out=bank,
+                lhsT=stationary[0][:, first:first + P].bitcast(E4M3),
+                lhsT_scale=stationary[1][:, first:first + P],
+                rhs=moving[0][:, cols].bitcast(E5M2),
+                rhs_scale=moving[1][:, cols],
                 start=True,
                 stop=True,
             )
 
-        def gather_h(t):
-            nc.vector.tensor_copy(h_g[:, t % 2, :], h_win[t][:].indirect(offsets[:]))
-
-        def square_h(v, b, squares):
-            nc.scalar.activation(squares, h_g[:, :, slots[b]].rearrange("p e i -> p i e"), ACT.Square)
-            h_sq[v, b] = squares
-
-        def gather_dy(t, entries, cols, factor):
-            nc.vector.tensor_tensor(dy_g[t // 2][:, t % 2, cols], dy_win[t][:].indirect(entries), factor, ALU.mult)
-
-        def form_dz(v, b, part):
-            nc.vector.scalar_tensor_tensor(
-                out=dz[b][:, v, :].rearrange("p (i e) -> p i e", e=2)[:, part, :],
-                in0=h_sq[v, b][:, part, :],
-                scalar=1.0,
-                in1=dy_g[v][:, :, slots[b]].rearrange("p e i -> p i e")[:, part, :],
-                op0=ALU.subtract,
-                op1=ALU.mult,
-            )
-
-        def join_pairs(b, part):
-            nc.scalar.copy(
-                dzn[b][:].bitcast(F32).rearrange("p (i v) -> p i v", v=2)[:, part, :],
-                dz[b][:].bitcast(F32).rearrange("p v i -> p i v")[:, part, :],
-            )
-
-        def turn_dz(v, b, pool):
-            bank = psum(pool, [P, 4, P])
-            for s in range(4):
-                nc.tensor.transpose(bank[:, s, :], dz[b][:].bitcast(F32)[:, v, s:N:4], ident[:])
-            nc.scalar.copy(
-                dzs[b][:, v * 2 * N:(v + 1) * 2 * N].rearrange("q (c s) -> q c s", s=4),
-                bank[:].bitcast(BF16).rearrange("q s c -> q c s"),
-            )
-
-        def cast_x(j, buffer, copy):
-            x_bf = sb(buffer, [P, T], BF16)
-            for half in range(2):
-                cols = slice(half * T // 2, (half + 1) * T // 2)
-                copy(x_bf[:, cols], x_raw[j][:, cols])
-            return x_bf
-
-        def turn_x(x_bf, xs, pool, buffer):
-            x_g = sb(buffer, [P, B, N], BF16)
-            for b in range(B):
-                nc.scalar.activation(
-                    x_g[:, b, :].rearrange("p (u q e) -> p q u e", u=2, e=2), x_bf[:].indirect(lists[b]), ACT.Copy
-                )
-            words = x_g[:].bitcast(F32)
-            bank = psum(pool, [P, 4, P])
-            for b in range(B):
-                for u in range(2):
-                    nc.tensor.transpose(bank[:, 2 * b + u, :], words[:, b, u * P:(u + 1) * P], ident[:])
-            nc.scalar.copy(
-                xs.bitcast(F32).rearrange("q (b d u) -> q b d u", b=B, u=2),
-                bank[:].rearrange("q (b u) d -> q b d u", u=2),
-            )
-
-        def quantize_x(name, xs, blocks, codes):
-            operand = quantize(name, xs, codes, E4M3)
-            for k, j in enumerate(blocks):
-                for b in range(B):
-                    x_mx[b, j] = (operand, (k * B + b) * P)
-
-        def cast_w(b, half, w_bf):
-            for j in range(2):
-                nc.scalar.copy(
-                    w_bf[:, j * 4 * P:(j + 1) * 4 * P].rearrange("p (c i t) -> p c t i", i=4, t=4),
-                    w_raw[b, half][:, :, j * P:(j + 1) * P].rearrange("p t (c i) -> p c t i", i=4),
-                )
-
-        def quantize_w(name, w_bf, blocks, codes):
-            operand = quantize(name, w_bf, codes, E4M3)
-            for k, block in enumerate(blocks):
-                w_mx[block] = (operand, k * P)
-
-        def make_dx(b, j, buffer, pool):
-            bank = psum(pool, [P, N])
-            product(bank, w_mx[b, j], dzn_mx[b])
-            dx_tiles[b, j] = sb(buffer, [P, N], F32)
-            nc.scalar.mul(dx_tiles[b, j][:], bank[:], -1.0)
-
-        def scatter_dx(b, j):
-            nc.vector.tensor_copy(gx[j][:].indirect(lists[b]), dx_tiles[b, j][:])
-            if b == B - 1:
-                nc.sync.dma_start(out_1[j * P:(j + 1) * P, :], gx[j][:])
-
-        def make_gw(b, j, gw):
-            bank = psum(ps_gw, [P, DV])
-            product(bank, x_mx[b, j], dzs_mx[b])
-            nc.scalar.mul(
-                gw.rearrange("d (p v e) -> d p v e", v=2, e=2),
-                bank[:].rearrange("d (v p e) -> d p v e", v=2, e=2),
-                -1.0,
-            )
-            nc.scalar.dma_start(out_0[b, j * P:(j + 1) * P, :], gw)
-
-        whole = slice(0, N)
-
-        nc.vector.tensor_copy(ts_row[:], ts_win[:].indirect(offsets[:]))
-        gx = {j: sb((f"gx{j}", (44 + 8 * j) * K), [P, T], F32) for j in range(2)}
-        for j in range(2):
-            nc.gpsimd.memset(gx[j][:], 0.0)
-
-        def spread_ts(b):
-            bank = psum(ps_dx, [P, 4, P])
-            for s in range(4):
-                nc.tensor.transpose(bank[:, s, :], ts_cols[b][:, s, :].to_broadcast([P, P]), ident[:])
-            return bank[:]
-
-        ts_cols = [sb(f"ts_cols{b}", [P, 4, 1], F32) for b in range(B)]
         for b in range(B):
+            nc.vector.tensor_copy(ts_row[:, slots[b]], ts_win[:].indirect(lists[b]))
             bank = psum(ps_turn, [P, 4, P])
             for s in range(4):
-                cols = slice(s * P, (s + 1) * P) if b == 0 else slice(N + s, S, 4)
-                nc.tensor.transpose(bank[:, s, :], ts_row[:, cols], ident[:])
-            nc.scalar.copy(ts_cols[b][:], bank[:, :, P - 1:P])
-            if b == 0:
-                nc.scalar.copy(ts_g[:, slots[0]], spread_ts(0).rearrange("p s q -> p (s q)"))
+                nc.tensor.transpose(bank[:, s, :], ts_row[:, b * N + s * P:b * N + (s + 1) * P], ident[:])
+            ts_cols = sb((f"ts_cols{b}", 108 * K + 64 * b), [P, 4, 1], F32)
+            nc.scalar.copy(ts_cols[:], bank[:, :, P - 1:P])
+            bank = psum(ps_dx, [P, 4, P])
+            for s in range(4):
+                nc.tensor.transpose(bank[:, s, :], ts_cols[:, s, :].to_broadcast([P, P]), ident[:])
+            nc.scalar.mul(ts_g[:, slots[b]], bank[:].rearrange("p s q -> p (s q)"), -1.0)
 
-        gx[2] = sb("ts_row", [P, T], F32)
-        nc.gpsimd.memset(gx[2][:], 0.0)
-        slope = sb("slope", [P, 2, N], F32)
-        for t in range(2):
-            gather_h(t)
-            square = sb("ts_cols0", [P, N], F32)
-            nc.scalar.activation(square[:], h_g[:, t, slots[1]], ACT.Square)
-            nc.scalar.activation(slope[:, t, :], square[:], ACT.Copy, bias=-1.0)
-        square_h(0, 0, sb("ts_cols0", [P, N, 2], F32)[:])
-        nc.scalar.copy(ts_g[:, slots[1]].rearrange("p (q s) -> p q s", s=4), spread_ts(1).rearrange("p s q -> p q s"))
-        for t in range(2):
-            gather_dy(t, lists[0], slots[0], ts_g[:, slots[0]])
-            gather_dy(t, lists[1], slots[1], slope[:, t, :])
-        form_dz(0, 0, whole)
-        gx[3] = sb("ts_cols0", [P, T], F32)
-        nc.gpsimd.memset(gx[3][:], 0.0)
-
-        for half in range(2):
-            w_raw[1, half] = load_w(1, half, (f"w1_{half}", (22 + 4 * half) * K))
-        x_raw[1] = load(xT[1 * P:2 * P, :], "h1")
-        x0_bf = cast_x(0, "x0_bf", nc.scalar.copy)
-        xs0 = sb(("xs0", 30 * K), [P, B * 4 * P], BF16)
-        turn_x(x0_bf, xs0[:], ps_turn, "x_g0")
-        x_raw[2] = load(xT[2 * P:3 * P, :], ("x2", 4096))
-        gather_h(2)
-        x_raw[3] = load(xT[3 * P:4 * P, :], "h2")
-        gather_h(3)
-
-        turned = sb("x0_bf", [P, 4, 2 * P], BF16)
-        for upper in range(2):
-            bank = psum(ps_turn, [P, 2, 2, P])
-            for s in range(2):
-                for e in range(2):
-                    nc.tensor.transpose(bank[:, s, e, :], dy_g[0][:, e, N + 2 * upper + s:S:4], ident[:])
-            for s in range(2):
-                nc.scalar.activation(
-                    turned[:, 2 * upper + s, :].rearrange("q (p e) -> q p e", e=2),
-                    bank[:, s, :, :].rearrange("q e p -> q p e"),
-                    ACT.Copy,
-                    scale=ts_cols[1][:, 2 * upper + s, :],
-                )
-        turned_back = psum(ps_gw, [P, 4, P])
-        for s in range(4):
-            nc.tensor.transpose(turned_back[:, s, :], turned[:].bitcast(F32)[:, s, :], ident[:])
-
-        for b, buffer in enumerate(("squares", ("squares1", 38 * K))):
-            square_h(1, b, sb(buffer, [P, N, 2], F32)[:])
-        dzs[0] = sb(("dzs0", 34 * K), [P, 4 * DV], BF16)
-        turn_dz(0, 0, ps_turn)
-        gather_dy(2, offsets[:], slice(0, S), ts_g[:])
-        for b in range(B):
-            gather_dy(3, lists[b], slots[b], ts_g[:, slots[b]])
-        w0_bf = sb("w0_bf", [P, 2 * D], BF16)
-        cast_w(0, 0, w0_bf[:])
-        dzn[0] = sb("dzn0", [P, 4 * N], BF16)
-        for part in (slice(k * N // 4, (k + 1) * N // 4) for k in range(4)):
-            form_dz(1, 0, part)
-            join_pairs(0, part)
-
-        early_codes = sb("dy3", [P, D // 2 + B * P], U32)
-        quantize_w("w0", w0_bf[:], [(0, 0), (0, 1)], early_codes[:, :D // 2])
-        dzn_mx[0] = quantize("dzn0", dzn[0][:], sb("dzn0_codes", [P, N], U32)[:], E5M2)
-        turn_dz(1, 0, ps_turn)
-        dz[1] = sb("dz0", [P, 2, 2 * N], BF16)
-        form_dz(1, 1, whole)
-        quantize_x("x0", xs0[:], [0], early_codes[:, D // 2:])
-        make_dx(0, 0, "dx00", ps_dx)
-        dzs_mx[0] = quantize("dzs0", dzs[0][:], sb("dzs0_codes", [P, DV], U32)[:], E5M2)
-
-        scatter_dx(0, 0)
-        x1_bf = cast_x(1, ("x1_bf", 36 * K), nc.gpsimd.tensor_copy)
-        w0_late = sb(("w0_late_bf", 40 * K), [P, 2 * D], BF16)
-        cast_w(0, 1, w0_late[:])
-        quantize_w("w0_late", w0_late[:], [(0, 2), (0, 3)], sb("w0_late_codes", [P, D // 2], U32)[:])
-        make_dx(0, 1, "w0_late", ps_dx)
-        scatter_dx(0, 1)
-        x2_bf = cast_x(2, ("x2_bf", 40 * K), nc.gpsimd.tensor_copy)
-        nc.scalar.copy(
-            dz[1][:].bitcast(F32)[:, 0, :].rearrange("p (q s) -> p q s", s=4),
-            turned_back[:].rearrange("p s q -> p q s"),
-        )
-        join_pairs(1, whole)
-        dzs[1] = sb("dy_g1", [P, 4 * DV], BF16)
-        nc.scalar.copy(
-            dzs[1][:, :2 * N].rearrange("q (c i s) -> q c s i", i=4, s=4),
-            turned[:].rearrange("q s (c i) -> q c s i", i=4),
-        )
-        turn_dz(1, 1, ps_chain)
-        w1_bf = sb("dz0", [P, 2 * D], BF16)
-        cast_w(1, 0, w1_bf[:])
-        late_codes = sb(("late_codes", 17 * K), [P, 3, N], U32)
-        quantize_w("w1", w1_bf[:], [(1, 0), (1, 1)], late_codes[:, 2, :D // 2])
-        dzn_mx[1] = quantize("dzn1", dzn[1][:], late_codes[:, 0, :], E5M2)
-        dzs_mx[1] = quantize("dzs1", dzs[1][:], late_codes[:, 1, :], E5M2)
-
-        make_dx(0, 2, "dx02", ps_chain)
-        scatter_dx(0, 2)
-        x3_bf = cast_x(3, "dy_g1", nc.gpsimd.tensor_copy)
-        gw_first = sb("gw_first", [P, B, DV], F32)
-        make_gw(0, 0, gw_first[:, 0, :])
-        xs12 = sb("xs12", [P, 2, B * 4 * P], BF16)
-        turn_x(x1_bf, xs12[:, 0, :], ps_turn, "x_g0")
-        make_dx(1, 0, ("dx10", 36 * K), ps_dx)
-        scatter_dx(1, 0)
-        turn_x(x2_bf, xs12[:, 1, :], ps_chain, "x_g2")
-        quantize_x("x12", xs12[:].rearrange("q j c -> q (j c)"), [1, 2], sb("x12_codes", [P, 2 * B * P], U32)[:])
-        make_dx(1, 1, ("dx11", 40 * K), ps_dx)
-        scatter_dx(1, 1)
-        w1_late = sb(("w1_late_bf", 42 * K), [P, 2 * D], BF16)
-        cast_w(1, 1, w1_late[:])
-        quantize_w("w1_late", w1_late[:], [(1, 2), (1, 3)], sb("w1_late_codes", [P, D // 2], U32)[:])
-        make_dx(0, 3, "dx03", ps_chain)
-        scatter_dx(0, 3)
-        make_gw(1, 0, gw_first[:, 1, :])
-        xs3 = sb("xs3", [P, B * 4 * P], BF16)
-        turn_x(x3_bf, xs3[:], ps_chain, "h2")
-        quantize_x("x3", xs3[:], [3], sb("x3_codes", [P, B * P], U32)[:])
-        make_dx(1, 2, "dy_g1", ps_dx)
-        make_dx(1, 3, "dx13", ps_chain)
-        gw_mid = sb("h2", [P, 2 * B, DV], F32)
-        for j in (1, 2):
+        def turn_dz(t):
+            bank = psum(ps_turn, [P, B, 2, P])
             for b in range(B):
-                make_gw(b, j, gw_mid[:, (j - 1) * B + b, :])
-        gw_last = sb("gw_last", [P, B, DV], F32)
-        for b in range(B):
-            make_gw(b, 3, gw_last[:, b, :])
-        for j in (2, 3):
-            scatter_dx(1, j)
+                words = dz[b][:, t, :].bitcast(F32)
+                for u in range(2):
+                    nc.tensor.transpose(bank[:, b, u, :], words[:, u:N // 2:2], ident[:])
+            dzs[t] = sb((f"dzs{t}", (16, 32, 48, 72)[t] * K), [P, B * 4 * P], BF16)
+            nc.scalar.copy(
+                dzs[t][:].bitcast(F32).rearrange("q (b p u) -> q b p u", b=B, u=2),
+                bank[:].rearrange("q b u p -> q b p u"),
+            )
+
+        def quantize_dzs(t, place):
+            dzs_mx[t] = quantize(f"dzs{t}", dzs[t][:], E5M2, place)
+
+        for t in range(4):
+            h_g = sb("h_g", [P, S], F32)
+            if t == 0:
+                nc.vector.tensor_copy(h_g[:], h_win[t][:].indirect(offsets[:]))
+            else:
+                nc.scalar.activation(h_g[:], h_win[t][:].indirect(offsets[:]), ACT.Copy)
+            if t > 0:
+                turn_dz(t - 1)
+            h_sq = sb((f"h_sq{t}", (108, 104)[t % 2] * K), [P, S], F32)
+            nc.scalar.activation(h_sq[:], h_g[:], ACT.Square)
+            dy_g = [sb(f"dy_g{b}", [P, N], F32) for b in range(B)]
+            for b in range(B):
+                nc.vector.tensor_tensor(dy_g[b][:], dy_win[t][:].indirect(lists[b]), ts_g[:, slots[b]], ALU.mult)
+            for b in range(B):
+                nc.vector.scalar_tensor_tensor(
+                    out=dz[b][:, t, :],
+                    in0=h_sq[:, slots[b]],
+                    scalar=1.0,
+                    in1=dy_g[b][:],
+                    op0=ALU.subtract,
+                    op1=ALU.mult,
+                )
+            if t > 0:
+                quantize_dzs(t - 1, (16 * t + 8) * K)
+
+        x_raw = [load(xT[j * P:(j + 1) * P, :], (f"x{j}", (0, 8, 16, 32)[j] * K)) for j in range(BLOCKS)]
+
+        def interleave(copy, dst, src):
+            copy(
+                dst.rearrange("p (c i t) -> p c t i", i=4, t=4),
+                src.rearrange("p t (c i) -> p c t i", i=4),
+            )
+
+        w_mx, dzn_mx = {}, {}
+
+        def cast_w(b):
+            w_bf = sb(("h_g", ("w_bf1", 74 * K))[b], [P, 4 * D], BF16)
+            interleave(nc.scalar.copy, w_bf[:], w_raw[b][:])
+            return w_bf
+
+        def join(b):
+            dzn = sb(f"dzn{b}", [P, 4 * N], BF16)
+            interleave(nc.vector.tensor_copy, dzn[:], dz[b][:])
+            return dzn
+
+        w_bf0 = cast_w(0)
+        turn_dz(3)
+        w_bf1 = cast_w(1)
+        dzn0 = join(0)
+        w_mx[0] = quantize("w0", w_bf0[:], E4M3)
+        dzn_mx[0] = quantize("dzn0", dzn0[:], E5M2)
+        dzn1 = join(1)
+        dzn_mx[1] = quantize("dzn1", dzn1[:], E5M2)
+        w_mx[1] = quantize("w1", w_bf1[:], E4M3)
+
+        dx = [sb((f"dx{j}", (50, 58, 42, 26)[j] * K), [P, S], F32) for j in range(BLOCKS)]
+        x_bank, x_mx = {}, {}
+
+        def make_dx(b, j):
+            bank = psum(ps_dx, [P, N])
+            product(bank[:], w_mx[b], j * P, dzn_mx[b], slice(0, N))
+            nc.scalar.copy(dx[j][:, slots[b]], bank[:])
+
+        def scatter_vector(j, first, last):
+            nc.vector.tensor_copy(gx[j][:].indirect(entries(first, last)), dx[j][:, first:last])
+            if last == S:
+                nc.sync.dma_start(out_1[j * P:(j + 1) * P, :], gx[j][:])
+
+        def scatter_scalar(j):
+            nc.scalar.activation(gx[j][:].indirect(entries(0, PIECE)), dx[j][:, :PIECE], ACT.Copy)
+
+        def gather_x(j):
+            x_g = sb((f"x_g{j}", 96 * K), [P, S], BF16)
+            nc.scalar.activation(x_g[:], x_raw[j][:].indirect(offsets[:]), ACT.Copy)
+            words = x_g[:].bitcast(F32)
+            x_bank[j] = psum(ps_turn, [P, B, 2, P])
+            for b in range(B):
+                for u in range(2):
+                    nc.tensor.transpose(x_bank[j][:, b, u, :], words[:, b * N // 2 + u:(b + 1) * N // 2:2], ident[:])
+
+        def quantize_x(j):
+            xs = sb((f"xs{j}", (64 + 2 * j) * K), [P, B * 4 * P], BF16)
+            nc.scalar.copy(
+                xs[:].bitcast(F32).rearrange("q (b d u) -> q b d u", b=B, u=2),
+                x_bank[j][:].rearrange("q b u d -> q b d u"),
+            )
+            x_mx[j] = quantize(f"x{j}", xs[:], E4M3)
+
+        def make_gw(b, j, copy):
+            bank = psum(ps_gw, [P, 4, P])
+            for t in range(4):
+                product(bank[:, t, :], x_mx[j], b * P, dzs_mx[t], slice(b * P, (b + 1) * P))
+            gw = sb((f"gw{b}{j}", (80 + 2 * (B * j + b)) * K), [P, DV], F32)
+            copy(gw[:].rearrange("d (p t) -> d p t", t=4), bank[:].rearrange("d t p -> d p t"))
+            nc.sync.dma_start(out_0[b, j * P:(j + 1) * P, :], gw[:])
+
+        make_dx(0, 0)
+        scatter_vector(0, 0, N)
+        quantize_dzs(3, None)
+        gather_x(0)
+        make_dx(1, 0)
+        scatter_vector(0, N, S)
+        for j in range(1, BLOCKS):
+            make_dx(0, j)
+            quantize_x(j - 1)
+            scatter_scalar(j)
+            make_dx(1, j)
+            scatter_vector(j, PIECE, S)
+            gather_x(j)
+            for b in range(B):
+                make_gw(b, j - 1, nc.scalar.copy)
+        quantize_x(BLOCKS - 1)
+        make_gw(0, BLOCKS - 1, nc.scalar.copy)
+        make_gw(1, BLOCKS - 1, nc.vector.tensor_copy)

@@ -18,6 +18,7 @@ ALU = mybir.AluOpType
 ACT = mybir.ActivationFunctionType
 
 K = 1024
+SLOT = 11 * K
 P = 128
 S = B * N
 BLOCKS = D // P
@@ -33,40 +34,52 @@ def tile_attend_gex_tnh_wx_kernel(tc, xT, dyT, hT, ts, wm, offs, out_0, out_1):
         ps_dx = ctx.enter_context(tc.psum_pool(name="ps_dx", bufs=3))
         ps_gw = ctx.enter_context(tc.psum_pool(name="ps_gw", bufs=2))
 
-        def sb(buffer, shape, dtype):
-            if isinstance(buffer, tuple):
-                return relay.tile(shape, dtype, name=buffer[0], offset=buffer[1], align_bytes=64)
-            return keep.tile(shape, dtype, name=buffer, align_bytes=64)
+        def sb(name, shape, dtype, place=None):
+            if place is None:
+                return keep.tile(shape, dtype, name=name, align_bytes=64)
+            return relay.tile(shape, dtype, name=name, offset=place, align_bytes=64)
 
         def psum(pool, shape):
             return pool.tile(shape, F32, name="bank")
 
-        def load(src, buffer):
-            raw = sb(buffer, [P, T], F32)
+        def load(name, src, place):
+            raw = sb(name, list(src.shape), F32, place)
             nc.sync.dma_start(raw[:], src)
             return raw
 
+        def first(k):
+            return SLOT * k + 512
+
+        def small(k):
+            return SLOT * k + 8 * K + 256
+
+        def later(k):
+            return SLOT * k
+
+        rest = 9 * SLOT
+        at_ts_row, at_sq, at_dy_g, at_dz, at_x0, at_h_g, at_dzn, at_gw = (
+            rest + k * K for k in (0, 4, 8, 12, 20, 28, 32, 40)
+        )
+
         offsets = keep.tile([P, S // 16], U16, name="offsets")
 
-        def entries(first, last):
-            return offsets[:, first // 16:last // 16]
+        def entries(begin, end):
+            return offsets[:, begin // 16:end // 16]
 
         slots = [slice(b * N, (b + 1) * N) for b in range(B)]
         lists = [entries(b * N, (b + 1) * N) for b in range(B)]
         h_planes = hT.rearrange("(p t) c -> p t c", t=4)
         dy_planes = dyT.rearrange("(p t) c -> p t c", t=4)
+        w_planes = [wm[b].rearrange("(p t) d -> p t d", t=4) for b in range(B)]
 
         nc.sync.dma_start(offsets[:], offs)
-        ts_win = sb(("ts_win", 64 * K), [P, T], F32)
+        ts_win = sb("ts_win", [P, T], F32, first(8))
         nc.sync.dma_start(ts_win[P - 1:P, :], ts[0:1, :])
-        h_win, dy_win = {}, {}
+        h_win, dy_win, x_win, w_raw = {}, {}, {}, {}
         for t in range(4):
-            h_win[t] = load(h_planes[:, t, :], (f"h{t}", 16 * t * K))
-            dy_win[t] = load(dy_planes[:, t, :], (f"dy{t}", (16 * t + 8) * K))
-        w_raw = {}
-        for b in range(B):
-            w_raw[b] = sb((f"w_raw{b}", (72 + 24 * b) * K), [P, 4, D], F32)
-            nc.sync.dma_start(w_raw[b][:], wm[b].rearrange("(p t) d -> p t d", t=4))
+            h_win[t] = load(f"h{t}", h_planes[:, t, :], first(2 * t))
+            dy_win[t] = load(f"dy{t}", dy_planes[:, t, :], first(2 * t + 1))
+        x_win[0] = load("x0", xT[0:P, :], at_x0)
 
         ident = sb("ident", [P, P], F32)
         make_identity(nc, ident[:])
@@ -75,22 +88,22 @@ def tile_attend_gex_tnh_wx_kernel(tc, xT, dyT, hT, ts, wm, offs, out_0, out_1):
         for j in range(BLOCKS):
             nc.gpsimd.memset(gx[j][:], 0.0)
 
-        ts_row = sb(("ts_row", 104 * K), [P, S], F32)
+        ts_row = sb("ts_row", [P, S], F32, at_ts_row)
         ts_g = sb("ts_g", [P, S], F32)
-        dz = [sb(f"dz{b}", [P, 4, N], BF16) for b in range(B)]
-        dzs, dzs_mx = {}, {}
+        dz = [sb(f"dz{b}", [P, 4, N], BF16, at_dz + 4 * K * b) for b in range(B)]
+        dzs, dzs_mx, w_mx, dzn_mx, x_bank, xs, x_mx, dx = {}, {}, {}, {}, {}, {}, {}, {}
 
         def quantize(name, src, fmt, place=None):
-            codes = sb((name + "_codes", place) if place else name + "_codes", [P, src.shape[1] // 4], U32)
+            codes = sb(name + "_codes", [P, src.shape[1] // 4], U32, place)
             scales = sb(name + "_scales", [P, src.shape[1] // 4], U8)
             nc.vector.quantize_mx(out=codes[:].bitcast(fmt), scales=scales[:], in_=src)
             return codes, scales
 
-        def product(bank, stationary, first, moving, cols):
+        def product(bank, stationary, column, moving, cols):
             nc.tensor.matmul_mx(
                 out=bank,
-                lhsT=stationary[0][:, first:first + P].bitcast(E4M3),
-                lhsT_scale=stationary[1][:, first:first + P],
+                lhsT=stationary[0][:, column:column + P].bitcast(E4M3),
+                lhsT_scale=stationary[1][:, column:column + P],
                 rhs=moving[0][:, cols].bitcast(E5M2),
                 rhs_scale=moving[1][:, cols],
                 start=True,
@@ -102,39 +115,44 @@ def tile_attend_gex_tnh_wx_kernel(tc, xT, dyT, hT, ts, wm, offs, out_0, out_1):
             bank = psum(ps_turn, [P, 4, P])
             for s in range(4):
                 nc.tensor.transpose(bank[:, s, :], ts_row[:, b * N + s * P:b * N + (s + 1) * P], ident[:])
-            ts_cols = sb((f"ts_cols{b}", 108 * K + 64 * b), [P, 4, 1], F32)
+            ts_cols = sb(f"ts_cols{b}", [P, 4, 1], F32, at_sq + 64 * b)
             nc.scalar.copy(ts_cols[:], bank[:, :, P - 1:P])
             bank = psum(ps_dx, [P, 4, P])
             for s in range(4):
                 nc.tensor.transpose(bank[:, s, :], ts_cols[:, s, :].to_broadcast([P, P]), ident[:])
             nc.scalar.mul(ts_g[:, slots[b]], bank[:].rearrange("p s q -> p (s q)"), -1.0)
 
-        def turn_dz(t):
-            bank = psum(ps_turn, [P, B, 2, P])
+        def turn_words(pool, words):
+            bank = psum(pool, [P, B, 2, P])
             for b in range(B):
-                words = dz[b][:, t, :].bitcast(F32)
                 for u in range(2):
-                    nc.tensor.transpose(bank[:, b, u, :], words[:, u:N // 2:2], ident[:])
-            dzs[t] = sb((f"dzs{t}", (16, 32, 48, 72)[t] * K), [P, B * 4 * P], BF16)
+                    nc.tensor.transpose(bank[:, b, u, :], words[b][:, u:N // 2:2], ident[:])
+            return bank
+
+        def weave_words(dst, bank):
             nc.scalar.copy(
-                dzs[t][:].bitcast(F32).rearrange("q (b p u) -> q b p u", b=B, u=2),
-                bank[:].rearrange("q b u p -> q b p u"),
+                dst[:].bitcast(F32).rearrange("q (b c u) -> q b c u", b=B, u=2),
+                bank[:].rearrange("q b u c -> q b c u"),
             )
+
+        def turn_dz(t, pool, place):
+            bank = turn_words(pool, [dz[b][:, t, :].bitcast(F32) for b in range(B)])
+            dzs[t] = sb(f"dzs{t}", [P, B * 4 * P], BF16, place)
+            weave_words(dzs[t], bank)
 
         def quantize_dzs(t, place):
             dzs_mx[t] = quantize(f"dzs{t}", dzs[t][:], E5M2, place)
 
         for t in range(4):
-            h_g = sb("h_g", [P, S], F32)
+            h_g = sb(f"h_g{t}", [P, S], F32, at_h_g)
             if t == 0:
                 nc.vector.tensor_copy(h_g[:], h_win[t][:].indirect(offsets[:]))
             else:
                 nc.scalar.activation(h_g[:], h_win[t][:].indirect(offsets[:]), ACT.Copy)
-            if t > 0:
-                turn_dz(t - 1)
-            h_sq = sb((f"h_sq{t}", (108, 104)[t % 2] * K), [P, S], F32)
+                turn_dz(t - 1, ps_turn, small(2 * t))
+            h_sq = sb(f"h_sq{t}", [P, S], F32, (at_sq, at_ts_row)[t % 2])
             nc.scalar.activation(h_sq[:], h_g[:], ACT.Square)
-            dy_g = [sb(f"dy_g{b}", [P, N], F32) for b in range(B)]
+            dy_g = [sb(f"dy_g{t}{b}", [P, N], F32, at_dy_g + 2 * K * b) for b in range(B)]
             for b in range(B):
                 nc.vector.tensor_tensor(dy_g[b][:], dy_win[t][:].indirect(lists[b]), ts_g[:, slots[b]], ALU.mult)
             for b in range(B):
@@ -147,94 +165,119 @@ def tile_attend_gex_tnh_wx_kernel(tc, xT, dyT, hT, ts, wm, offs, out_0, out_1):
                     op1=ALU.mult,
                 )
             if t > 0:
-                quantize_dzs(t - 1, (16 * t + 8) * K)
+                quantize_dzs(t - 1, small(2 * t + 1))
 
-        x_raw = [load(xT[j * P:(j + 1) * P, :], (f"x{j}", (0, 8, 16, 32)[j] * K)) for j in range(BLOCKS)]
+        w_raw[0] = load("w0", w_planes[0], later(0))
+        x_win[1] = load("x1", xT[P:2 * P, :], later(1))
+        w_raw[1] = load("w1", w_planes[1], later(2))
+        x_win[2] = load("x2", xT[2 * P:3 * P, :], later(3))
+        x_win[3] = load("x3", xT[3 * P:4 * P, :], later(4))
 
-        def interleave(copy, dst, src):
+        def interleave(name, copy, src, place):
+            dst = sb(name, [P, 4 * N], BF16, place)
             copy(
-                dst.rearrange("p (c i t) -> p c t i", i=4, t=4),
-                src.rearrange("p t (c i) -> p c t i", i=4),
+                dst[:].rearrange("p (c i t) -> p c t i", i=4, t=4),
+                src[:].rearrange("p t (c i) -> p c t i", i=4),
             )
+            return dst
 
-        w_mx, dzn_mx = {}, {}
-
-        def cast_w(b):
-            w_bf = sb(("h_g", ("w_bf1", 74 * K))[b], [P, 4 * D], BF16)
-            interleave(nc.scalar.copy, w_bf[:], w_raw[b][:])
-            return w_bf
-
-        def join(b):
-            dzn = sb(f"dzn{b}", [P, 4 * N], BF16)
-            interleave(nc.vector.tensor_copy, dzn[:], dz[b][:])
-            return dzn
-
-        w_bf0 = cast_w(0)
-        turn_dz(3)
-        w_bf1 = cast_w(1)
-        dzn0 = join(0)
-        w_mx[0] = quantize("w0", w_bf0[:], E4M3)
-        dzn_mx[0] = quantize("dzn0", dzn0[:], E5M2)
-        dzn1 = join(1)
-        dzn_mx[1] = quantize("dzn1", dzn1[:], E5M2)
-        w_mx[1] = quantize("w1", w_bf1[:], E4M3)
-
-        dx = [sb((f"dx{j}", (50, 58, 42, 26)[j] * K), [P, S], F32) for j in range(BLOCKS)]
-        x_bank, x_mx = {}, {}
-
-        def make_dx(b, j):
+        def make_dx(b, j, copy, place):
             bank = psum(ps_dx, [P, N])
             product(bank[:], w_mx[b], j * P, dzn_mx[b], slice(0, N))
-            nc.scalar.copy(dx[j][:, slots[b]], bank[:])
+            if isinstance(place, int):
+                dx[b, j] = (sb(f"dx{b}{j}", [P, N], F32, place), b * N)
+            else:
+                dx[b, j] = (place, 0)
+            tile, origin = dx[b, j]
+            copy(tile[:, b * N - origin:(b + 1) * N - origin], bank[:])
 
-        def scatter_vector(j, first, last):
-            nc.vector.tensor_copy(gx[j][:].indirect(entries(first, last)), dx[j][:, first:last])
-            if last == S:
+        def scatter_piece(j, begin, end):
+            tile, origin = dx[begin // N, j]
+            nc.scalar.activation(
+                gx[j][:].indirect(entries(begin, end)), tile[:, begin - origin:end - origin], ACT.Copy
+            )
+            if end == S:
                 nc.sync.dma_start(out_1[j * P:(j + 1) * P, :], gx[j][:])
 
-        def scatter_scalar(j):
-            nc.scalar.activation(gx[j][:].indirect(entries(0, PIECE)), dx[j][:, :PIECE], ACT.Copy)
+        def scatter_vector(j, begin, end):
+            tile, origin = dx[begin // N, j]
+            nc.vector.tensor_copy(gx[j][:].indirect(entries(begin, end)), tile[:, begin - origin:end - origin])
+            if end == S:
+                nc.sync.dma_start(out_1[j * P:(j + 1) * P, :], gx[j][:])
 
-        def gather_x(j):
-            x_g = sb((f"x_g{j}", 96 * K), [P, S], BF16)
-            nc.scalar.activation(x_g[:], x_raw[j][:].indirect(offsets[:]), ACT.Copy)
-            words = x_g[:].bitcast(F32)
-            x_bank[j] = psum(ps_turn, [P, B, 2, P])
-            for b in range(B):
-                for u in range(2):
-                    nc.tensor.transpose(x_bank[j][:, b, u, :], words[:, b * N // 2 + u:(b + 1) * N // 2:2], ident[:])
+        def gather_x(j, place):
+            x_g = sb(f"x_g{j}", [P, S], BF16, place)
+            nc.scalar.activation(x_g[:], x_win[j][:].indirect(offsets[:]), ACT.Copy)
+            return x_g
 
-        def quantize_x(j):
-            xs = sb((f"xs{j}", (64 + 2 * j) * K), [P, B * 4 * P], BF16)
-            nc.scalar.copy(
-                xs[:].bitcast(F32).rearrange("q (b d u) -> q b d u", b=B, u=2),
-                x_bank[j][:].rearrange("q b u d -> q b d u"),
-            )
-            x_mx[j] = quantize(f"x{j}", xs[:], E4M3)
+        def turn_x(j, x_g, pool):
+            x_bank[j] = turn_words(pool, [x_g[:, slots[b]].bitcast(F32) for b in range(B)])
 
-        def make_gw(b, j, copy):
+        def weave_x(j, place):
+            xs[j] = sb(f"xs{j}", [P, B * 4 * P], BF16, place)
+            weave_words(xs[j], x_bank[j])
+
+        def quantize_x(j, place):
+            x_mx[j] = quantize(f"x{j}", xs[j][:], E4M3, place)
+
+        def make_gw(b, j, copy, place=None, queue=nc.sync):
             bank = psum(ps_gw, [P, 4, P])
             for t in range(4):
                 product(bank[:, t, :], x_mx[j], b * P, dzs_mx[t], slice(b * P, (b + 1) * P))
-            gw = sb((f"gw{b}{j}", (80 + 2 * (B * j + b)) * K), [P, DV], F32)
+            gw = sb(f"gw{b}{j}", [P, DV], F32, place or at_gw + 2 * K * (B * j + b))
             copy(gw[:].rearrange("d (p t) -> d p t", t=4), bank[:].rearrange("d t p -> d p t"))
-            nc.sync.dma_start(out_0[b, j * P:(j + 1) * P, :], gw[:])
+            queue.dma_start(out_0[b, j * P:(j + 1) * P, :], gw[:])
 
-        make_dx(0, 0)
-        scatter_vector(0, 0, N)
+        x_g = gather_x(0, at_h_g)
+        turn_dz(3, ps_turn, at_x0)
+        turn_x(0, x_g, ps_turn)
+        w_bf0 = interleave("w_bf0", nc.scalar.copy, w_raw[0], at_x0 + 2 * K)
+        weave_x(0, later(0))
+        x_g = gather_x(1, at_h_g)
+        turn_x(1, x_g, ps_turn)
+        for b in range(B):
+            dzn = interleave(f"dzn{b}", nc.vector.tensor_copy, dz[b], at_dzn + 4 * K * b)
+            dzn_mx[b] = quantize(f"dzn{b}", dzn[:], E5M2)
         quantize_dzs(3, None)
-        gather_x(0)
-        make_dx(1, 0)
+        w_mx[0] = quantize("w0", w_bf0[:], E4M3)
+        w_bf1 = interleave("w_bf1", nc.vector.tensor_copy, w_raw[1], at_x0 + 2 * K)
+        make_dx(0, 0, nc.vector.tensor_copy, later(2))
+        w_mx[1] = quantize("w1", w_bf1[:], E4M3)
+
+        make_dx(0, 1, nc.scalar.copy, later(2) + 2 * K)
+        both = sb("dx2", [P, S], F32, later(2) + 6 * K)
+        make_dx(0, 2, nc.scalar.copy, both)
+        weave_x(1, later(2) + 4 * K)
+        scatter_vector(0, 0, N)
+        quantize_x(0, later(2))
+        make_dx(1, 0, nc.scalar.copy, later(5))
         scatter_vector(0, N, S)
-        for j in range(1, BLOCKS):
-            make_dx(0, j)
-            quantize_x(j - 1)
-            scatter_scalar(j)
-            make_dx(1, j)
-            scatter_vector(j, PIECE, S)
-            gather_x(j)
-            for b in range(B):
-                make_gw(b, j - 1, nc.scalar.copy)
-        quantize_x(BLOCKS - 1)
-        make_gw(0, BLOCKS - 1, nc.scalar.copy)
-        make_gw(1, BLOCKS - 1, nc.vector.tensor_copy)
+        quantize_x(1, later(5))
+        scatter_piece(1, 0, PIECE)
+        make_dx(1, 2, nc.scalar.copy, both)
+        scatter_vector(2, 0, S)
+        scatter_piece(1, PIECE, N)
+        make_dx(1, 1, nc.scalar.copy, later(5) + 2 * K)
+        scatter_piece(1, N, N + PIECE)
+        make_gw(0, 0, nc.scalar.copy)
+        scatter_piece(1, N + PIECE, S)
+        make_dx(0, 3, nc.scalar.copy, later(6))
+        scatter_vector(3, 0, N)
+
+        x_g = gather_x(2, later(5) + 2 * K)
+        turn_x(2, x_g, ps_turn)
+        make_gw(1, 0, nc.scalar.copy, later(3))
+        make_gw(0, 1, nc.scalar.copy, later(3) + 2 * K)
+        weave_x(2, later(7))
+        quantize_x(2, later(6))
+        make_dx(1, 3, nc.scalar.copy, later(5) + 2 * K)
+        scatter_vector(3, N, S)
+        x_g = gather_x(3, later(3) + 6 * K)
+        turn_x(3, x_g, ps_turn)
+        make_gw(1, 1, nc.scalar.copy, later(4), nc.scalar)
+        make_gw(0, 2, nc.scalar.copy, later(4) + 2 * K, nc.scalar)
+        weave_x(3, later(7) + 2 * K)
+        quantize_x(3, None)
+        make_gw(1, 2, nc.scalar.copy, later(3) + 6 * K, nc.scalar)
+        make_gw(0, 3, nc.scalar.copy)
+        make_gw(1, 3, nc.vector.tensor_copy)

@@ -131,8 +131,8 @@ def tile_attend_gex_tnh_wx_kernel(tc, xT, dyT, hT, ts, wm, offs, out_0, out_1):
 
         def weave_words(dst, bank):
             nc.scalar.copy(
-                dst[:].bitcast(F32).rearrange("q (b c u) -> q b c u", b=B, u=2),
-                bank[:].rearrange("q b u c -> q b c u"),
+                dst[:].bitcast(F32).rearrange("q (b c i u) -> q b c u i", b=B, i=2, u=2),
+                bank[:].rearrange("q b u (c i) -> q b c u i", i=2),
             )
 
         def turn_dz(t, pool, place):
@@ -173,11 +173,11 @@ def tile_attend_gex_tnh_wx_kernel(tc, xT, dyT, hT, ts, wm, offs, out_0, out_1):
         x_win[2] = load("x2", xT[2 * P:3 * P, :], later(3))
         x_win[3] = load("x3", xT[3 * P:4 * P, :], later(4))
 
-        def interleave(name, copy, src, place):
+        def interleave(name, copy, src, place, run):
             dst = sb(name, [P, 4 * N], BF16, place)
             copy(
-                dst[:].rearrange("p (c i t) -> p c t i", i=4, t=4),
-                src[:].rearrange("p t (c i) -> p c t i", i=4),
+                dst[:].rearrange("p (c i t) -> p c t i", i=run, t=4),
+                src[:].rearrange("p t (c i) -> p c t i", i=run),
             )
             return dst
 
@@ -225,22 +225,25 @@ def tile_attend_gex_tnh_wx_kernel(tc, xT, dyT, hT, ts, wm, offs, out_0, out_1):
             for t in range(4):
                 product(bank[:, t, :], x_mx[j], b * P, dzs_mx[t], slice(b * P, (b + 1) * P))
             gw = sb(f"gw{b}{j}", [P, DV], F32, place or at_gw + 2 * K * (B * j + b))
-            copy(gw[:].rearrange("d (p t) -> d p t", t=4), bank[:].rearrange("d t p -> d p t"))
+            copy(
+                gw[:].rearrange("d (c i t) -> d c t i", i=2, t=4),
+                bank[:].rearrange("d t (c i) -> d c t i", i=2),
+            )
             queue.dma_start(out_0[b, j * P:(j + 1) * P, :], gw[:])
 
         x_g = gather_x(0, at_h_g)
         turn_dz(3, ps_turn, at_x0)
         turn_x(0, x_g, ps_turn)
-        w_bf0 = interleave("w_bf0", nc.scalar.copy, w_raw[0], at_x0 + 2 * K)
+        w_bf0 = interleave("w_bf0", nc.scalar.copy, w_raw[0], at_x0 + 2 * K, 2)
         weave_x(0, later(0))
         x_g = gather_x(1, at_h_g)
         turn_x(1, x_g, ps_turn)
         for b in range(B):
-            dzn = interleave(f"dzn{b}", nc.vector.tensor_copy, dz[b], at_dzn + 4 * K * b)
+            dzn = interleave(f"dzn{b}", nc.vector.tensor_copy, dz[b], at_dzn + 4 * K * b, 4)
             dzn_mx[b] = quantize(f"dzn{b}", dzn[:], E5M2)
         quantize_dzs(3, None)
         w_mx[0] = quantize("w0", w_bf0[:], E4M3)
-        w_bf1 = interleave("w_bf1", nc.vector.tensor_copy, w_raw[1], at_x0 + 2 * K)
+        w_bf1 = interleave("w_bf1", nc.vector.tensor_copy, w_raw[1], at_x0 + 2 * K, 2)
         make_dx(0, 0, nc.vector.tensor_copy, later(2))
         w_mx[1] = quantize("w1", w_bf1[:], E4M3)
 
@@ -276,8 +279,8 @@ def tile_attend_gex_tnh_wx_kernel(tc, xT, dyT, hT, ts, wm, offs, out_0, out_1):
         turn_x(3, x_g, ps_turn)
         make_gw(1, 1, nc.scalar.copy, later(4), nc.scalar)
         make_gw(0, 2, nc.scalar.copy, later(4) + 2 * K, nc.scalar)
+        make_gw(1, 2, nc.scalar.copy, later(4) + 4 * K, nc.scalar)
         weave_x(3, later(7) + 2 * K)
         quantize_x(3, None)
-        make_gw(1, 2, nc.scalar.copy, later(3) + 6 * K, nc.scalar)
         make_gw(0, 3, nc.scalar.copy)
         make_gw(1, 3, nc.vector.tensor_copy)

@@ -91,7 +91,7 @@ def tile_attend_gex_tnh_wx_kernel(tc, xT, dyT, hT, ts, wm, offs, out_0, out_1):
         ts_row = sb("ts_row", [P, S], F32, at_ts_row)
         ts_g = sb("ts_g", [P, S], F32)
         dz = [sb(f"dz{b}", [P, 4, N], BF16, at_dz + 4 * K * b) for b in range(B)]
-        dzs, dzs_mx, w_mx, dzn_mx, x_bank, xs, x_mx, dx = {}, {}, {}, {}, {}, {}, {}, {}
+        dzs, dzs_mx, w_mx, dzn_mx, x_mx, dx = {}, {}, {}, {}, {}, {}
 
         def quantize(name, src, fmt, place=None):
             codes = sb(name + "_codes", [P, src.shape[1] // 4], U32, place)
@@ -123,22 +123,22 @@ def tile_attend_gex_tnh_wx_kernel(tc, xT, dyT, hT, ts, wm, offs, out_0, out_1):
             nc.scalar.mul(ts_g[:, slots[b]], bank[:].rearrange("p s q -> p (s q)"), -1.0)
 
         def turn_words(pool, words):
-            bank = psum(pool, [P, B, 2, P])
-            for b in range(B):
+            bank = psum(pool, [P, len(words), 2, P])
+            for b in range(len(words)):
                 for u in range(2):
                     nc.tensor.transpose(bank[:, b, u, :], words[b][:, u:N // 2:2], ident[:])
             return bank
 
         def weave_words(dst, bank):
             nc.scalar.copy(
-                dst[:].bitcast(F32).rearrange("q (b c i u) -> q b c u i", b=B, i=2, u=2),
+                dst.bitcast(F32).rearrange("q (b c i u) -> q b c u i", c=P // 2, i=2, u=2),
                 bank[:].rearrange("q b u (c i) -> q b c u i", i=2),
             )
 
         def turn_dz(t, pool, place):
             bank = turn_words(pool, [dz[b][:, t, :].bitcast(F32) for b in range(B)])
             dzs[t] = sb(f"dzs{t}", [P, B * 4 * P], BF16, place)
-            weave_words(dzs[t], bank)
+            weave_words(dzs[t][:], bank)
 
         def quantize_dzs(t, place):
             dzs_mx[t] = quantize(f"dzs{t}", dzs[t][:], E5M2, place)
@@ -205,25 +205,21 @@ def tile_attend_gex_tnh_wx_kernel(tc, xT, dyT, hT, ts, wm, offs, out_0, out_1):
             if end == S:
                 nc.sync.dma_start(out_1[j * P:(j + 1) * P, :], gx[j][:])
 
-        def gather_x(j, place):
-            x_g = sb(f"x_g{j}", [P, S], BF16, place)
-            nc.scalar.activation(x_g[:], x_win[j][:].indirect(offsets[:]), ACT.Copy)
-            return x_g
+        def gather_x(j, experts, place):
+            begin, end = experts[0] * N, (experts[-1] + 1) * N
+            x_g = sb(f"x_g{j}{experts[0]}", [P, end - begin], BF16, place)
+            nc.scalar.activation(x_g[:], x_win[j][:].indirect(entries(begin, end)), ACT.Copy)
+            return turn_words(ps_turn, [x_g[:, k * N:(k + 1) * N].bitcast(F32) for k in range(len(experts))])
 
-        def turn_x(j, x_g, pool):
-            x_bank[j] = turn_words(pool, [x_g[:, slots[b]].bitcast(F32) for b in range(B)])
-
-        def weave_x(j, place):
-            xs[j] = sb(f"xs{j}", [P, B * 4 * P], BF16, place)
-            weave_words(xs[j], x_bank[j])
-
-        def quantize_x(j, place):
-            x_mx[j] = quantize(f"x{j}", xs[j][:], E4M3, place)
+        def quantize_x(name, units, xs, place):
+            operand = quantize(name, xs, E4M3, place)
+            for k, unit in enumerate(units):
+                x_mx[unit] = (operand, k * P)
 
         def make_gw(b, j, copy, place=None, queue=nc.sync):
             bank = psum(ps_gw, [P, 4, P])
             for t in range(4):
-                product(bank[:, t, :], x_mx[j], b * P, dzs_mx[t], slice(b * P, (b + 1) * P))
+                product(bank[:, t, :], *x_mx[b, j], dzs_mx[t], slice(b * P, (b + 1) * P))
             gw = sb(f"gw{b}{j}", [P, DV], F32, place or at_gw + 2 * K * (B * j + b))
             copy(
                 gw[:].rearrange("d (c i t) -> d c t i", i=2, t=4),
@@ -231,33 +227,40 @@ def tile_attend_gex_tnh_wx_kernel(tc, xT, dyT, hT, ts, wm, offs, out_0, out_1):
             )
             queue.dma_start(out_0[b, j * P:(j + 1) * P, :], gw[:])
 
-        x_g = gather_x(0, at_h_g)
+        both = (0, 1)
+        behind_w1 = later(2) + 256
+
+        def weave_x(j, bank, place):
+            xs = sb(f"xs{j}", [P, S], BF16, place)
+            weave_words(xs[:], bank)
+            return xs[:]
+
+        def units(j):
+            return [(b, j) for b in range(B)]
+
+        bank0 = gather_x(0, both, at_h_g)
         turn_dz(3, ps_turn, at_x0)
-        turn_x(0, x_g, ps_turn)
         w_bf0 = interleave("w_bf0", nc.scalar.copy, w_raw[0], at_x0 + 2 * K, 2)
-        weave_x(0, later(0))
-        x_g = gather_x(1, at_h_g)
-        turn_x(1, x_g, ps_turn)
+        bank1 = gather_x(1, both, at_h_g)
         for b in range(B):
             dzn = interleave(f"dzn{b}", nc.vector.tensor_copy, dz[b], at_dzn + 4 * K * b, 4)
             dzn_mx[b] = quantize(f"dzn{b}", dzn[:], E5M2)
         quantize_dzs(3, None)
         w_mx[0] = quantize("w0", w_bf0[:], E4M3)
         w_bf1 = interleave("w_bf1", nc.vector.tensor_copy, w_raw[1], at_x0 + 2 * K, 2)
-        make_dx(0, 0, nc.vector.tensor_copy, later(2))
         w_mx[1] = quantize("w1", w_bf1[:], E4M3)
 
-        make_dx(0, 1, nc.scalar.copy, later(2) + 2 * K)
-        both = sb("dx2", [P, S], F32, later(2) + 6 * K)
-        make_dx(0, 2, nc.scalar.copy, both)
-        weave_x(1, later(2) + 4 * K)
+        make_dx(0, 0, nc.scalar.copy, behind_w1 + 64)
         scatter_vector(0, 0, N)
-        quantize_x(0, later(2))
+        make_dx(0, 1, nc.scalar.copy, behind_w1 + 2 * K + 64)
+        dx2 = sb("dx2", [P, S], F32, behind_w1 + 6 * K + 64)
+        make_dx(0, 2, nc.scalar.copy, dx2)
+        quantize_x("x0", units(0), weave_x(0, bank0, behind_w1 - 2 * K + 64), None)
+        quantize_x("x1", units(1), weave_x(1, bank1, behind_w1 + 4 * K + 64), None)
         make_dx(1, 0, nc.scalar.copy, later(5))
         scatter_vector(0, N, S)
-        quantize_x(1, later(5))
         scatter_piece(1, 0, PIECE)
-        make_dx(1, 2, nc.scalar.copy, both)
+        make_dx(1, 2, nc.scalar.copy, dx2)
         scatter_vector(2, 0, S)
         scatter_piece(1, PIECE, N)
         make_dx(1, 1, nc.scalar.copy, later(5) + 2 * K)
@@ -267,20 +270,16 @@ def tile_attend_gex_tnh_wx_kernel(tc, xT, dyT, hT, ts, wm, offs, out_0, out_1):
         make_dx(0, 3, nc.scalar.copy, later(6))
         scatter_vector(3, 0, N)
 
-        x_g = gather_x(2, later(5) + 2 * K)
-        turn_x(2, x_g, ps_turn)
+        bank = gather_x(2, both, later(5) + 2 * K)
         make_gw(1, 0, nc.scalar.copy, later(3))
         make_gw(0, 1, nc.scalar.copy, later(3) + 2 * K)
-        weave_x(2, later(7))
-        quantize_x(2, later(6))
+        quantize_x("x2", units(2), weave_x(2, bank, later(7)), None)
         make_dx(1, 3, nc.scalar.copy, later(5) + 2 * K)
         scatter_vector(3, N, S)
-        x_g = gather_x(3, later(3) + 6 * K)
-        turn_x(3, x_g, ps_turn)
+        bank = gather_x(3, both, later(3) + 6 * K)
         make_gw(1, 1, nc.scalar.copy, later(4), nc.scalar)
         make_gw(0, 2, nc.scalar.copy, later(4) + 2 * K, nc.scalar)
-        make_gw(1, 2, nc.scalar.copy, later(4) + 4 * K, nc.scalar)
-        weave_x(3, later(7) + 2 * K)
-        quantize_x(3, None)
+        quantize_x("x3", units(3), weave_x(3, bank, later(7) + 2 * K), None)
+        make_gw(1, 2, nc.vector.tensor_copy, later(7) + 2 * K)
         make_gw(0, 3, nc.scalar.copy)
         make_gw(1, 3, nc.vector.tensor_copy)

@@ -74,7 +74,7 @@ def tile_attend_gex_tnh_wx_kernel(tc, xT, dyT, hT, ts, wm, offs, out_0, out_1):
 
         nc.sync.dma_start(offsets[:], offs)
         ts_win = sb("ts_win", [P, T], F32, first(8))
-        nc.sync.dma_start(ts_win[P - 1:P, :], ts[0:1, :])
+        nc.scalar.dma_start(ts_win[P - 1:P, :], ts[0:1, :])
         h_win, dy_win, x_win, w_raw = {}, {}, {}, {}
         for t in range(4):
             h_win[t] = load(f"h{t}", h_planes[:, t, :], first(2 * t))
@@ -260,10 +260,10 @@ def tile_attend_gex_tnh_wx_kernel(tc, xT, dyT, hT, ts, wm, offs, out_0, out_1):
         make_dx(1, 0, nc.scalar.copy, later(5))
         scatter_vector(0, N, S)
         scatter_piece(1, 0, PIECE)
+        make_dx(1, 1, nc.scalar.copy, later(5) + 2 * K)
+        scatter_piece(1, PIECE, N)
         make_dx(1, 2, nc.scalar.copy, dx2)
         scatter_vector(2, 0, S)
-        scatter_piece(1, PIECE, N)
-        make_dx(1, 1, nc.scalar.copy, later(5) + 2 * K)
         scatter_piece(1, N, N + PIECE)
         make_gw(0, 0, nc.scalar.copy)
         scatter_piece(1, N + PIECE, S)

@@ -30,17 +30,15 @@ def tile_attend_gex_tnh_wx_kernel(tc, xT, dyT, hT, ts, wm, offs, out_0, out_1):
     with ExitStack() as ctx:
         keep = ctx.enter_context(tc.tile_pool(name="keep", bufs=1))
         relay = ctx.enter_context(tc.tile_pool(name="relay", bufs=1))
-        ps_turn = ctx.enter_context(tc.psum_pool(name="ps_turn", bufs=3))
-        ps_dx = ctx.enter_context(tc.psum_pool(name="ps_dx", bufs=3))
-        ps_gw = ctx.enter_context(tc.psum_pool(name="ps_gw", bufs=2))
+        banks = ctx.enter_context(tc.psum_pool(name="banks", bufs=1))
 
         def sb(name, shape, dtype, place=None):
             if place is None:
                 return keep.tile(shape, dtype, name=name, align_bytes=64)
             return relay.tile(shape, dtype, name=name, offset=place, align_bytes=64)
 
-        def psum(pool, shape):
-            return pool.tile(shape, F32, name="bank")
+        def psum(name, bank, shape):
+            return banks.tile(shape, F32, name=name, offset=2 * K * bank)
 
         def load(name, src, place):
             raw = sb(name, list(src.shape), F32, place)
@@ -57,7 +55,7 @@ def tile_attend_gex_tnh_wx_kernel(tc, xT, dyT, hT, ts, wm, offs, out_0, out_1):
             return SLOT * k
 
         rest = 9 * SLOT
-        at_ts_row, at_sq, at_dy_g, at_dz, at_x0, at_h_g, at_dzn, at_gw = (
+        at_ts_row, at_sq, at_dy_g, at_dz, at_w0, at_h_g, at_dzn, at_gw = (
             rest + k * K for k in (0, 4, 8, 12, 20, 28, 32, 40)
         )
 
@@ -79,7 +77,7 @@ def tile_attend_gex_tnh_wx_kernel(tc, xT, dyT, hT, ts, wm, offs, out_0, out_1):
         for t in range(4):
             h_win[t] = load(f"h{t}", h_planes[:, t, :], first(2 * t))
             dy_win[t] = load(f"dy{t}", dy_planes[:, t, :], first(2 * t + 1))
-        x_win[0] = load("x0", xT[0:P, :], at_x0)
+        w_raw[0] = load("w0", w_planes[0], at_w0)
 
         ident = sb("ident", [P, P], F32)
         make_identity(nc, ident[:])
@@ -112,22 +110,15 @@ def tile_attend_gex_tnh_wx_kernel(tc, xT, dyT, hT, ts, wm, offs, out_0, out_1):
 
         for b in range(B):
             nc.vector.tensor_copy(ts_row[:, slots[b]], ts_win[:].indirect(lists[b]))
-            bank = psum(ps_turn, [P, 4, P])
+            bank = psum(f"ts_turn{b}", b, [P, 4, P])
             for s in range(4):
                 nc.tensor.transpose(bank[:, s, :], ts_row[:, b * N + s * P:b * N + (s + 1) * P], ident[:])
             ts_cols = sb(f"ts_cols{b}", [P, 4, 1], F32, at_sq + 64 * b)
             nc.scalar.copy(ts_cols[:], bank[:, :, P - 1:P])
-            bank = psum(ps_dx, [P, 4, P])
+            bank = psum(f"ts_spread{b}", 3 + b, [P, 4, P])
             for s in range(4):
                 nc.tensor.transpose(bank[:, s, :], ts_cols[:, s, :].to_broadcast([P, P]), ident[:])
             nc.scalar.mul(ts_g[:, slots[b]], bank[:].rearrange("p s q -> p (s q)"), -1.0)
-
-        def turn_words(pool, words):
-            bank = psum(pool, [P, len(words), 2, P])
-            for b in range(len(words)):
-                for u in range(2):
-                    nc.tensor.transpose(bank[:, b, u, :], words[b][:, u:N // 2:2], ident[:])
-            return bank
 
         def weave_words(dst, bank):
             nc.scalar.copy(
@@ -135,8 +126,14 @@ def tile_attend_gex_tnh_wx_kernel(tc, xT, dyT, hT, ts, wm, offs, out_0, out_1):
                 bank[:].rearrange("q b u (c i) -> q b c u i", i=2),
             )
 
-        def turn_dz(t, pool, place):
-            bank = turn_words(pool, [dz[b][:, t, :].bitcast(F32) for b in range(B)])
+        def turn_words(bank, b, words):
+            for u in range(2):
+                nc.tensor.transpose(bank[:, b, u, :], words.bitcast(F32)[:, u:N // 2:2], ident[:])
+
+        def turn_dz(t, place):
+            bank = psum(f"dz_turn{t}", (t + 2) % 3, [P, B, 2, P])
+            for b in range(B):
+                turn_words(bank, b, dz[b][:, t, :])
             dzs[t] = sb(f"dzs{t}", [P, B * 4 * P], BF16, place)
             weave_words(dzs[t][:], bank)
 
@@ -149,7 +146,7 @@ def tile_attend_gex_tnh_wx_kernel(tc, xT, dyT, hT, ts, wm, offs, out_0, out_1):
                 nc.vector.tensor_copy(h_g[:], h_win[t][:].indirect(offsets[:]))
             else:
                 nc.scalar.activation(h_g[:], h_win[t][:].indirect(offsets[:]), ACT.Copy)
-                turn_dz(t - 1, ps_turn, small(2 * t))
+                turn_dz(t - 1, small(2 * t))
             h_sq = sb(f"h_sq{t}", [P, S], F32, (at_sq, at_ts_row)[t % 2])
             nc.scalar.activation(h_sq[:], h_g[:], ACT.Square)
             dy_g = [sb(f"dy_g{t}{b}", [P, N], F32, at_dy_g + 2 * K * b) for b in range(B)]
@@ -167,7 +164,7 @@ def tile_attend_gex_tnh_wx_kernel(tc, xT, dyT, hT, ts, wm, offs, out_0, out_1):
             if t > 0:
                 quantize_dzs(t - 1, small(2 * t + 1))
 
-        w_raw[0] = load("w0", w_planes[0], later(0))
+        x_win[0] = load("x0", xT[0:P, :], later(0))
         x_win[1] = load("x1", xT[P:2 * P, :], later(1))
         w_raw[1] = load("w1", w_planes[1], later(2))
         x_win[2] = load("x2", xT[2 * P:3 * P, :], later(3))
@@ -181,45 +178,58 @@ def tile_attend_gex_tnh_wx_kernel(tc, xT, dyT, hT, ts, wm, offs, out_0, out_1):
             )
             return dst
 
-        def make_dx(b, j, copy, place):
-            bank = psum(ps_dx, [P, N])
-            product(bank[:], w_mx[b], j * P, dzn_mx[b], slice(0, N))
-            if isinstance(place, int):
-                dx[b, j] = (sb(f"dx{b}{j}", [P, N], F32, place), b * N)
-            else:
-                dx[b, j] = (place, 0)
-            tile, origin = dx[b, j]
-            copy(tile[:, b * N - origin:(b + 1) * N - origin], bank[:])
-
-        def scatter_piece(j, begin, end):
-            tile, origin = dx[begin // N, j]
-            nc.scalar.activation(
-                gx[j][:].indirect(entries(begin, end)), tile[:, begin - origin:end - origin], ACT.Copy
+        def join_on_gpsimd(name, src, place):
+            dst = sb(name, [P, 4 * N], BF16, place)
+            nc.gpsimd.tensor_scalar(
+                dst[:].rearrange("p (c t) -> p c t", t=4),
+                src[:].rearrange("p t c -> p c t"),
+                1.0,
+                0.0,
+                ALU.mult,
+                ALU.add,
             )
+            return dst
+
+        def product_dx(b, j, number):
+            bank = psum(f"dx_sum{b}{j}", number, [P, N])
+            product(bank[:], w_mx[b], j * P, dzn_mx[b], slice(0, N))
+            return bank
+
+        def copy_dx(j, begin, end, bank, copy, place):
+            dx[j, begin] = sb(f"dx{j}_{begin}", [P, end - begin], F32, place)
+            copy(dx[j, begin][:], bank[:, begin % N:begin % N + end - begin])
+
+        def make_dx(b, j, number, copy, place):
+            copy_dx(j, b * N, (b + 1) * N, product_dx(b, j, number), copy, place)
+
+        def on_scalar(out, in_):
+            nc.scalar.activation(out, in_, ACT.Copy)
+
+        def scatter(j, begin, end, copy, origin=None):
+            origin = begin if origin is None else origin
+            copy(gx[j][:].indirect(entries(begin, end)), dx[j, origin][:, begin - origin:end - origin])
             if end == S:
                 nc.sync.dma_start(out_1[j * P:(j + 1) * P, :], gx[j][:])
 
-        def scatter_vector(j, begin, end):
-            tile, origin = dx[begin // N, j]
-            nc.vector.tensor_copy(gx[j][:].indirect(entries(begin, end)), tile[:, begin - origin:end - origin])
-            if end == S:
-                nc.sync.dma_start(out_1[j * P:(j + 1) * P, :], gx[j][:])
+        def gather_x(j, number, places):
+            bank = psum(f"x_turn{j}", number, [P, B, 2, P])
+            for b in range(B):
+                x_g = sb(f"x_g{j}{b}", [P, N], BF16, places[b])
+                on_scalar(x_g[:], x_win[j][:].indirect(lists[b]))
+                turn_words(bank, b, x_g[:])
+            return bank
 
-        def gather_x(j, experts, place):
-            begin, end = experts[0] * N, (experts[-1] + 1) * N
-            x_g = sb(f"x_g{j}{experts[0]}", [P, end - begin], BF16, place)
-            nc.scalar.activation(x_g[:], x_win[j][:].indirect(entries(begin, end)), ACT.Copy)
-            return turn_words(ps_turn, [x_g[:, k * N:(k + 1) * N].bitcast(F32) for k in range(len(experts))])
+        def weave_x(j, bank, place):
+            xs[j] = sb(f"xs{j}", [P, S], BF16, place)
+            weave_words(xs[j][:], bank)
 
-        def quantize_x(name, units, xs, place):
-            operand = quantize(name, xs, E4M3, place)
-            for k, unit in enumerate(units):
-                x_mx[unit] = (operand, k * P)
+        def quantize_x(j, place):
+            x_mx[j] = quantize(f"x{j}", xs[j][:], E4M3, place)
 
         def make_gw(b, j, copy, place=None, queue=nc.sync):
-            bank = psum(ps_gw, [P, 4, P])
+            bank = psum(f"gw_sum{b}{j}", 6 + b, [P, 4, P])
             for t in range(4):
-                product(bank[:, t, :], *x_mx[b, j], dzs_mx[t], slice(b * P, (b + 1) * P))
+                product(bank[:, t, :], x_mx[j], b * P, dzs_mx[t], slice(b * P, (b + 1) * P))
             gw = sb(f"gw{b}{j}", [P, DV], F32, place or at_gw + 2 * K * (B * j + b))
             copy(
                 gw[:].rearrange("d (c i t) -> d c t i", i=2, t=4),
@@ -227,59 +237,61 @@ def tile_attend_gex_tnh_wx_kernel(tc, xT, dyT, hT, ts, wm, offs, out_0, out_1):
             )
             queue.dma_start(out_0[b, j * P:(j + 1) * P, :], gw[:])
 
-        both = (0, 1)
-        behind_w1 = later(2) + 256
+        vector, scalar = nc.vector.tensor_copy, nc.scalar.copy
+        xs = {}
+        half = K // 2
 
-        def weave_x(j, bank, place):
-            xs = sb(f"xs{j}", [P, S], BF16, place)
-            weave_words(xs[:], bank)
-            return xs[:]
-
-        def units(j):
-            return [(b, j) for b in range(B)]
-
-        bank0 = gather_x(0, both, at_h_g)
-        turn_dz(3, ps_turn, at_x0)
-        w_bf0 = interleave("w_bf0", nc.scalar.copy, w_raw[0], at_x0 + 2 * K, 2)
-        bank1 = gather_x(1, both, at_h_g)
-        for b in range(B):
-            dzn = interleave(f"dzn{b}", nc.vector.tensor_copy, dz[b], at_dzn + 4 * K * b, 4)
-            dzn_mx[b] = quantize(f"dzn{b}", dzn[:], E5M2)
-        quantize_dzs(3, None)
+        w_bf0 = interleave("w_bf0", scalar, w_raw[0], later(5), 2)
+        turn_dz(3, at_w0 + 2 * K)
+        dzn0 = interleave("dzn0", vector, dz[0], at_dzn, 4)
         w_mx[0] = quantize("w0", w_bf0[:], E4M3)
-        w_bf1 = interleave("w_bf1", nc.vector.tensor_copy, w_raw[1], at_x0 + 2 * K, 2)
+        dzn_mx[0] = quantize("dzn0", dzn0[:], E5M2, at_w0)
+        quantize_dzs(3, None)
+        dzn1 = join_on_gpsimd("dzn1", dz[1], at_w0 + 2 * K)
+        make_dx(0, 0, 5, vector, at_sq)
+        scatter(0, 0, N, vector)
+
+        bank_x0 = gather_x(0, 5, (later(6), later(6) + K))
+        bank_x1 = gather_x(1, 1, (later(6) + 2 * K, later(6) + 5 * K))
+        bank_dx = product_dx(0, 1, 3)
+        copy_dx(1, 0, PIECE, bank_dx, scalar, later(6) + K + half)
+        weave_x(0, bank_x0, later(6) + 2 * K + half)
+        scatter(1, 0, PIECE, on_scalar)
+
+        w_bf1 = interleave("w_bf1", vector, w_raw[1], at_dzn + 4 * K, 2)
+        dzn_mx[1] = quantize("dzn1", dzn1[:], E5M2)
         w_mx[1] = quantize("w1", w_bf1[:], E4M3)
+        quantize_x(0, later(2) + 3 * K)
+        make_dx(0, 2, 4, scalar, later(2))
+        scatter(2, 0, N, vector)
+        copy_dx(1, PIECE, N, bank_dx, scalar, later(2) + 2 * K)
+        weave_x(1, bank_x1, later(0))
+        quantize_x(1, at_dzn + 4 * K)
+        scatter(1, PIECE, N, on_scalar)
 
-        make_dx(0, 0, nc.scalar.copy, behind_w1 + 64)
-        scatter_vector(0, 0, N)
-        make_dx(0, 1, nc.scalar.copy, behind_w1 + 2 * K + 64)
-        dx2 = sb("dx2", [P, S], F32, behind_w1 + 6 * K + 64)
-        make_dx(0, 2, nc.scalar.copy, dx2)
-        quantize_x("x0", units(0), weave_x(0, bank0, behind_w1 - 2 * K + 64), None)
-        quantize_x("x1", units(1), weave_x(1, bank1, behind_w1 + 4 * K + 64), None)
-        make_dx(1, 0, nc.scalar.copy, later(5))
-        scatter_vector(0, N, S)
-        scatter_piece(1, 0, PIECE)
-        make_dx(1, 1, nc.scalar.copy, later(5) + 2 * K)
-        scatter_piece(1, PIECE, N)
-        make_dx(1, 2, nc.scalar.copy, dx2)
-        scatter_vector(2, 0, S)
-        scatter_piece(1, N, N + PIECE)
-        make_gw(0, 0, nc.scalar.copy)
-        scatter_piece(1, N + PIECE, S)
-        make_dx(0, 3, nc.scalar.copy, later(6))
-        scatter_vector(3, 0, N)
+        make_dx(1, 0, 0, scalar, later(5) + 4 * K)
+        scatter(0, N, S, vector)
+        make_dx(1, 1, 2, scalar, later(7) + 3 * K)
+        make_gw(0, 0, scalar)
+        scatter(1, N, N + PIECE, on_scalar)
+        make_dx(1, 2, 4, scalar, at_dy_g)
+        scatter(2, N, S, vector)
+        scatter(1, N + PIECE, S, on_scalar, N)
+        make_gw(1, 0, scalar)
+        make_dx(0, 3, 0, scalar, at_dy_g + 2 * K)
+        scatter(3, 0, N, vector)
 
-        bank = gather_x(2, both, later(5) + 2 * K)
-        make_gw(1, 0, nc.scalar.copy, later(3))
-        make_gw(0, 1, nc.scalar.copy, later(3) + 2 * K)
-        quantize_x("x2", units(2), weave_x(2, bank, later(7)), None)
-        make_dx(1, 3, nc.scalar.copy, later(5) + 2 * K)
-        scatter_vector(3, N, S)
-        bank = gather_x(3, both, later(3) + 6 * K)
-        make_gw(1, 1, nc.scalar.copy, later(4), nc.scalar)
-        make_gw(0, 2, nc.scalar.copy, later(4) + 2 * K, nc.scalar)
-        quantize_x("x3", units(3), weave_x(3, bank, later(7) + 2 * K), None)
-        make_gw(1, 2, nc.vector.tensor_copy, later(7) + 2 * K)
-        make_gw(0, 3, nc.scalar.copy)
-        make_gw(1, 3, nc.vector.tensor_copy)
+        bank_x2 = gather_x(2, 5, (later(7) + 2 * K + half, later(5) + 4 * K))
+        make_gw(0, 1, scalar, later(7) + K)
+        make_gw(1, 1, scalar, later(3))
+        weave_x(2, bank_x2, later(7) + 6 * K)
+        quantize_x(2, None)
+        make_dx(1, 3, 3, scalar, later(5) + 2 * K + half)
+        scatter(3, N, S, vector)
+        bank_x3 = gather_x(3, 1, (later(5) + 4 * K + half, later(7) + 3 * K))
+        make_gw(0, 2, scalar, later(5) + 5 * K, nc.scalar)
+        make_gw(1, 2, vector, later(4))
+        weave_x(3, bank_x3, later(1))
+        quantize_x(3, None)
+        make_gw(0, 3, scalar)
+        make_gw(1, 3, vector)

@@ -164,9 +164,11 @@ def tile_attend_gex_tnh_wx_kernel(tc, xT, dyT, hT, ts, wm, offs, out_0, out_1):
             if t > 0:
                 quantize_dzs(t - 1, small(2 * t + 1))
 
+        half = K // 2
         x_win[0] = load("x0", xT[0:P, :], later(0))
         x_win[1] = load("x1", xT[P:2 * P, :], later(1))
-        w_raw[1] = load("w1", w_planes[1], later(2))
+        w1_first = load("w1_first", w_planes[1][:, :, :P], later(2))
+        w1_rest = load("w1_rest", w_planes[1][:, :, P:], later(2) + 3 * K + half)
         x_win[2] = load("x2", xT[2 * P:3 * P, :], later(3))
         x_win[3] = load("x3", xT[3 * P:4 * P, :], later(4))
 
@@ -179,7 +181,7 @@ def tile_attend_gex_tnh_wx_kernel(tc, xT, dyT, hT, ts, wm, offs, out_0, out_1):
             return dst
 
         def join_on_gpsimd(name, src, place):
-            dst = sb(name, [P, 4 * N], BF16, place)
+            dst = sb(name, [P, 4 * src.shape[2]], BF16, place)
             nc.gpsimd.tensor_scalar(
                 dst[:].rearrange("p (c t) -> p c t", t=4),
                 src[:].rearrange("p t c -> p c t"),
@@ -190,17 +192,22 @@ def tile_attend_gex_tnh_wx_kernel(tc, xT, dyT, hT, ts, wm, offs, out_0, out_1):
             )
             return dst
 
+        def quantize_w(b, blocks, src):
+            operand = quantize(f"w{b}{blocks[0]}", src[:], E4M3)
+            for k, j in enumerate(blocks):
+                w_mx[b, j] = (operand, k * P)
+
         def product_dx(b, j, number):
             bank = psum(f"dx_sum{b}{j}", number, [P, N])
-            product(bank[:], w_mx[b], j * P, dzn_mx[b], slice(0, N))
+            product(bank[:], *w_mx[b, j], dzn_mx[b], slice(0, N))
             return bank
 
-        def copy_dx(j, begin, end, bank, copy, place):
-            dx[j, begin] = sb(f"dx{j}_{begin}", [P, end - begin], F32, place)
-            copy(dx[j, begin][:], bank[:, begin % N:begin % N + end - begin])
-
-        def make_dx(b, j, number, copy, place):
-            copy_dx(j, b * N, (b + 1) * N, product_dx(b, j, number), copy, place)
+        def make_dx(b, j, number, copy, place, pieces=1):
+            bank = product_dx(b, j, number)
+            dx[j, b * N] = sb(f"dx{b}{j}", [P, N], F32, place)
+            for k in range(pieces):
+                cols = slice(k * N // pieces, (k + 1) * N // pieces)
+                copy(dx[j, b * N][:, cols], bank[:, cols])
 
         def on_scalar(out, in_):
             nc.scalar.activation(out, in_, ACT.Copy)
@@ -211,25 +218,41 @@ def tile_attend_gex_tnh_wx_kernel(tc, xT, dyT, hT, ts, wm, offs, out_0, out_1):
             if end == S:
                 nc.sync.dma_start(out_1[j * P:(j + 1) * P, :], gx[j][:])
 
-        def gather_x(j, number, places):
+        def gather_half(j, b, place):
+            x_g[j, b] = sb(f"x_g{j}{b}", [P, N], BF16, place)
+            on_scalar(x_g[j, b][:], x_win[j][:].indirect(lists[b]))
+
+        def turn_x(j, number):
             bank = psum(f"x_turn{j}", number, [P, B, 2, P])
             for b in range(B):
-                x_g = sb(f"x_g{j}{b}", [P, N], BF16, places[b])
-                on_scalar(x_g[:], x_win[j][:].indirect(lists[b]))
-                turn_words(bank, b, x_g[:])
+                turn_words(bank, b, x_g[j, b][:])
             return bank
+
+        def gather_x(j, number, places):
+            for b in range(B):
+                gather_half(j, b, places[b])
+            return turn_x(j, number)
 
         def weave_x(j, bank, place):
             xs[j] = sb(f"xs{j}", [P, S], BF16, place)
             weave_words(xs[j][:], bank)
 
         def quantize_x(j, place):
-            x_mx[j] = quantize(f"x{j}", xs[j][:], E4M3, place)
+            operand = quantize(f"x{j}", xs[j][:], E4M3, place)
+            for b in range(B):
+                x_mx[b, j] = (operand, b * P)
 
-        def make_gw(b, j, copy, place=None, queue=nc.sync):
-            bank = psum(f"gw_sum{b}{j}", 6 + b, [P, 4, P])
+        def turn_half(j, b, number, place):
+            bank = psum(f"x_turn{j}{b}", number, [P, 1, 2, P])
+            turn_words(bank, 0, x_g[j, b][:])
+            xs[j, b] = sb(f"xs{j}{b}", [P, N], BF16, place)
+            weave_words(xs[j, b][:], bank)
+            x_mx[b, j] = (quantize(f"x{j}{b}", xs[j, b][:], E4M3), 0)
+
+        def make_gw(b, j, number, copy, place=None, queue=nc.sync):
+            bank = psum(f"gw_sum{b}{j}", number, [P, 4, P])
             for t in range(4):
-                product(bank[:, t, :], x_mx[j], b * P, dzs_mx[t], slice(b * P, (b + 1) * P))
+                product(bank[:, t, :], *x_mx[b, j], dzs_mx[t], slice(b * P, (b + 1) * P))
             gw = sb(f"gw{b}{j}", [P, DV], F32, place or at_gw + 2 * K * (B * j + b))
             copy(
                 gw[:].rearrange("d (c i t) -> d c t i", i=2, t=4),
@@ -238,13 +261,13 @@ def tile_attend_gex_tnh_wx_kernel(tc, xT, dyT, hT, ts, wm, offs, out_0, out_1):
             queue.dma_start(out_0[b, j * P:(j + 1) * P, :], gw[:])
 
         vector, scalar = nc.vector.tensor_copy, nc.scalar.copy
-        xs = {}
-        half = K // 2
+        xs, x_g = {}, {}
+        base = later(2) + 2 * K
 
         w_bf0 = interleave("w_bf0", scalar, w_raw[0], later(5), 2)
         turn_dz(3, at_w0 + 2 * K)
         dzn0 = interleave("dzn0", vector, dz[0], at_dzn, 4)
-        w_mx[0] = quantize("w0", w_bf0[:], E4M3)
+        quantize_w(0, range(BLOCKS), w_bf0)
         dzn_mx[0] = quantize("dzn0", dzn0[:], E5M2, at_w0)
         quantize_dzs(3, None)
         dzn1 = join_on_gpsimd("dzn1", dz[1], at_w0 + 2 * K)
@@ -252,46 +275,45 @@ def tile_attend_gex_tnh_wx_kernel(tc, xT, dyT, hT, ts, wm, offs, out_0, out_1):
         scatter(0, 0, N, vector)
 
         bank_x0 = gather_x(0, 5, (later(6), later(6) + K))
-        bank_x1 = gather_x(1, 1, (later(6) + 2 * K, later(6) + 5 * K))
-        bank_dx = product_dx(0, 1, 3)
-        copy_dx(1, 0, PIECE, bank_dx, scalar, later(6) + K + half)
+        bank_x1 = gather_x(1, 1, (later(6) + 2 * K, later(6) + 7 * K))
         weave_x(0, bank_x0, later(6) + 2 * K + half)
-        scatter(1, 0, PIECE, on_scalar)
-
-        w_bf1 = interleave("w_bf1", vector, w_raw[1], at_dzn + 4 * K, 2)
-        dzn_mx[1] = quantize("dzn1", dzn1[:], E5M2)
-        w_mx[1] = quantize("w1", w_bf1[:], E4M3)
-        quantize_x(0, later(2) + 3 * K)
-        make_dx(0, 2, 4, scalar, later(2))
-        scatter(2, 0, N, vector)
-        copy_dx(1, PIECE, N, bank_dx, scalar, later(2) + 2 * K)
         weave_x(1, bank_x1, later(0))
-        quantize_x(1, at_dzn + 4 * K)
-        scatter(1, PIECE, N, on_scalar)
-
-        make_dx(1, 0, 0, scalar, later(5) + 4 * K)
+        w_bf1_first = join_on_gpsimd("w_bf1_first", w1_first, later(6) + 4 * K + half)
+        dzn_mx[1] = quantize("dzn1", dzn1[:], E5M2)
+        quantize_x(0, later(2) + half)
+        quantize_w(1, range(1), w_bf1_first)
+        make_dx(0, 2, 4, scalar, later(2) - K - half)
+        scatter(2, 0, N, vector)
+        w_bf1_rest = join_on_gpsimd("w_bf1_rest", w1_rest, later(6) + 4 * K)
+        make_dx(0, 1, 3, scalar, later(2) + K + half, 2)
+        scatter(1, 0, PIECE, on_scalar)
+        make_gw(0, 0, 6, scalar)
+        quantize_w(1, range(1, BLOCKS), w_bf1_rest)
+        make_dx(1, 0, 0, vector, base + 4 * K)
+        quantize_x(1, later(2) + 4 * K + half)
         scatter(0, N, S, vector)
-        make_dx(1, 1, 2, scalar, later(7) + 3 * K)
-        make_gw(0, 0, scalar)
-        scatter(1, N, N + PIECE, on_scalar)
-        make_dx(1, 2, 4, scalar, at_dy_g)
-        scatter(2, N, S, vector)
-        scatter(1, N + PIECE, S, on_scalar, N)
-        make_gw(1, 0, scalar)
-        make_dx(0, 3, 0, scalar, at_dy_g + 2 * K)
-        scatter(3, 0, N, vector)
+        scatter(1, PIECE, N, on_scalar, 0)
 
-        bank_x2 = gather_x(2, 5, (later(7) + 2 * K + half, later(5) + 4 * K))
-        make_gw(0, 1, scalar, later(7) + K)
-        make_gw(1, 1, scalar, later(3))
-        weave_x(2, bank_x2, later(7) + 6 * K)
+        bank_x2 = gather_x(2, 5, (later(2) - K - half, later(2) + K + half))
+        make_dx(1, 2, 4, scalar, later(2) - K)
+        scatter(2, N, S, vector)
+        make_dx(1, 1, 2, scalar, later(2) - 3 * K)
+        weave_x(2, bank_x2, later(5))
         quantize_x(2, None)
-        make_dx(1, 3, 3, scalar, later(5) + 2 * K + half)
+        scatter(1, N, N + PIECE, on_scalar)
+        make_dx(0, 3, 0, scalar, later(2) + 2 * K)
+        scatter(3, 0, N, vector)
+        scatter(1, N + PIECE, S, on_scalar, N)
+        make_gw(1, 0, 7, scalar, later(3))
+        make_gw(0, 1, 6, scalar, later(3) + 2 * K)
+        make_dx(1, 3, 3, scalar, later(3) + 6 * K)
         scatter(3, N, S, vector)
-        bank_x3 = gather_x(3, 1, (later(5) + 4 * K + half, later(7) + 3 * K))
-        make_gw(0, 2, scalar, later(5) + 5 * K, nc.scalar)
-        make_gw(1, 2, vector, later(4))
-        weave_x(3, bank_x3, later(1))
-        quantize_x(3, None)
-        make_gw(0, 3, scalar)
-        make_gw(1, 3, vector)
+        make_gw(1, 1, 7, scalar, later(3) + 4 * K, nc.scalar)
+        make_gw(0, 2, 6, scalar, None, nc.scalar)
+        gather_half(3, 0, later(2) - 3 * K)
+        gather_half(3, 1, later(2) - 2 * K)
+        make_gw(1, 2, 7, vector, later(4))
+        turn_half(3, 0, 1, later(1))
+        turn_half(3, 1, 2, later(1) + K)
+        make_gw(0, 3, 6, scalar)
+        make_gw(1, 3, 7, vector)

@@ -73,11 +73,11 @@ def tile_attend_gex_tnh_wx_kernel(tc, xT, dyT, hT, ts, wm, offs, out_0, out_1):
         nc.sync.dma_start(offsets[:], offs)
         ts_win = sb("ts_win", [P, T], F32, first(8))
         nc.scalar.dma_start(ts_win[P - 1:P, :], ts[0:1, :])
-        h_win, dy_win, x_win, w_raw = {}, {}, {}, {}
+        h_win, dy_win, x_win = {}, {}, {}
         for t in range(4):
             h_win[t] = load(f"h{t}", h_planes[:, t, :], first(2 * t))
             dy_win[t] = load(f"dy{t}", dy_planes[:, t, :], first(2 * t + 1))
-        w_raw[0] = load("w0", w_planes[0], at_w0)
+        w_first = load("w_first", w_planes[0][:, :, :2 * P], at_w0)
 
         ident = sb("ident", [P, P], F32)
         make_identity(nc, ident[:])
@@ -91,10 +91,15 @@ def tile_attend_gex_tnh_wx_kernel(tc, xT, dyT, hT, ts, wm, offs, out_0, out_1):
         dz = [sb(f"dz{b}", [P, 4, N], BF16, at_dz + 4 * K * b) for b in range(B)]
         dzs, dzs_mx, w_mx, dzn_mx, x_mx, dx = {}, {}, {}, {}, {}, {}
 
-        def quantize(name, src, fmt, place=None):
-            codes = sb(name + "_codes", [P, src.shape[1] // 4], U32, place)
-            scales = sb(name + "_scales", [P, src.shape[1] // 4], U8)
-            nc.vector.quantize_mx(out=codes[:].bitcast(fmt), scales=scales[:], in_=src)
+        def quantize(name, src, fmt, place=None, pieces=1):
+            words = src.shape[1] // 4
+            codes = sb(name + "_codes", [P, words], U32, place)
+            scales = sb(name + "_scales", [P, words], U8)
+            for k in range(pieces):
+                begin, end = k * words // pieces, (k + 1) * words // pieces
+                nc.vector.quantize_mx(
+                    out=codes[:, begin:end].bitcast(fmt), scales=scales[:, begin:end], in_=src[:, 4 * begin:4 * end]
+                )
             return codes, scales
 
         def product(bank, stationary, column, moving, cols):
@@ -161,19 +166,34 @@ def tile_attend_gex_tnh_wx_kernel(tc, xT, dyT, hT, ts, wm, offs, out_0, out_1):
                     op0=ALU.subtract,
                     op1=ALU.mult,
                 )
-            if t > 0:
+            if t in (1, 2):
                 quantize_dzs(t - 1, small(2 * t + 1))
 
         half = K // 2
         x_win[0] = load("x0", xT[0:P, :], later(0))
         x_win[1] = load("x1", xT[P:2 * P, :], later(1))
-        w1_first = load("w1_first", w_planes[1][:, :, :P], later(2))
-        w1_rest = load("w1_rest", w_planes[1][:, :, P:], later(2) + 3 * K + half)
+        mid, late = later(2) + 2 * K, later(7)
+
+        def load_w(name, place, pieces):
+            raw = sb(name, [P, 4, P * sum(len(blocks) for b, blocks in pieces)], F32, place)
+            column = 0
+            for b, blocks in pieces:
+                width = P * len(blocks)
+                nc.sync.dma_start(
+                    raw[:, :, column:column + width], w_planes[b][:, :, P * blocks[0]:P * blocks[0] + width]
+                )
+                column = column + width
+            return raw
+
+        mid_units = ((0, (2,)), (1, (0,)))
+        late_units = ((0, (3,)), (1, (1, 2, 3)))
+        w_mid = load_w("w_mid", mid, mid_units)
         x_win[2] = load("x2", xT[2 * P:3 * P, :], later(3))
+        w_late = load_w("w_late", late, late_units)
         x_win[3] = load("x3", xT[3 * P:4 * P, :], later(4))
 
         def interleave(name, copy, src, place, run):
-            dst = sb(name, [P, 4 * N], BF16, place)
+            dst = sb(name, [P, 4 * src.shape[2]], BF16, place)
             copy(
                 dst[:].rearrange("p (c i t) -> p c t i", i=run, t=4),
                 src[:].rearrange("p t (c i) -> p c t i", i=run),
@@ -192,10 +212,10 @@ def tile_attend_gex_tnh_wx_kernel(tc, xT, dyT, hT, ts, wm, offs, out_0, out_1):
             )
             return dst
 
-        def quantize_w(b, blocks, src):
-            operand = quantize(f"w{b}{blocks[0]}", src[:], E4M3)
-            for k, j in enumerate(blocks):
-                w_mx[b, j] = (operand, k * P)
+        def quantize_w(name, pieces, src):
+            operand = quantize(name, src[:], E4M3)
+            for k, unit in enumerate((b, j) for b, blocks in pieces for j in blocks):
+                w_mx[unit] = (operand, k * P)
 
         def product_dx(b, j, number):
             bank = psum(f"dx_sum{b}{j}", number, [P, N])
@@ -262,58 +282,71 @@ def tile_attend_gex_tnh_wx_kernel(tc, xT, dyT, hT, ts, wm, offs, out_0, out_1):
 
         vector, scalar = nc.vector.tensor_copy, nc.scalar.copy
         xs, x_g = {}, {}
-        base = later(2) + 2 * K
+        q = K // 4
 
-        w_bf0 = interleave("w_bf0", scalar, w_raw[0], later(5), 2)
-        turn_dz(3, at_w0 + 2 * K)
+        w_bf = interleave("w_first_bf", scalar, w_first, later(5), 2)
+        gather_half(0, 0, later(6) + K)
+        gather_half(0, 1, later(6) + 5 * K)
+        turn_dz(3, later(6) - half)
         dzn0 = interleave("dzn0", vector, dz[0], at_dzn, 4)
-        quantize_w(0, range(BLOCKS), w_bf0)
-        dzn_mx[0] = quantize("dzn0", dzn0[:], E5M2, at_w0)
-        quantize_dzs(3, None)
-        dzn1 = join_on_gpsimd("dzn1", dz[1], at_w0 + 2 * K)
-        make_dx(0, 0, 5, vector, at_sq)
-        scatter(0, 0, N, vector)
+        quantize_w("w_first", ((0, (0, 1)),), w_bf)
+        dzn_mx[0] = quantize("dzn0", dzn0[:], E5M2, None, 2)
+        quantize_dzs(2, None)
+        dzn1 = join_on_gpsimd("dzn1", dz[1], later(6) + 6 * K + half)
+        dx[0, 0] = sb("dx00", [P, N], F32, at_sq)
+        for k in range(2):
+            cols = slice(k * PIECE, (k + 1) * PIECE)
+            bank = psum(f"dx_sum00{k}", 4 + k, [P, PIECE])
+            product(bank[:], *w_mx[0, 0], dzn_mx[0], cols)
+            vector(dx[0, 0][:, cols], bank[:])
+        scatter(0, 0, PIECE, vector)
+        scatter(0, PIECE, N, vector, 0)
 
-        bank_x0 = gather_x(0, 5, (later(6), later(6) + K))
-        bank_x1 = gather_x(1, 1, (later(6) + 2 * K, later(6) + 7 * K))
-        weave_x(0, bank_x0, later(6) + 2 * K + half)
+        bank_x0 = [psum(f"x_turn0{b}", (0, 5)[b], [P, 1, 2, P]) for b in range(B)]
+        for b in range(B):
+            turn_words(bank_x0[b], 0, x_g[0, b][:])
+        bank_x1 = gather_x(1, 1, (later(6) + 2 * K, at_h_g))
+        xs[0] = sb("xs0", [P, S], BF16, later(6) + 2 * K + half)
+        for b in range(B):
+            weave_words(xs[0][:, slots[b]], bank_x0[b])
         weave_x(1, bank_x1, later(0))
-        w_bf1_first = join_on_gpsimd("w_bf1_first", w1_first, later(6) + 4 * K + half)
+        w_bf = join_on_gpsimd("w_mid_bf", w_mid, at_dzn + 4 * K)
         dzn_mx[1] = quantize("dzn1", dzn1[:], E5M2)
-        quantize_x(0, later(2) + half)
-        quantize_w(1, range(1), w_bf1_first)
-        make_dx(0, 2, 4, scalar, later(2) - K - half)
-        scatter(2, 0, N, vector)
-        w_bf1_rest = join_on_gpsimd("w_bf1_rest", w1_rest, later(6) + 4 * K)
-        make_dx(0, 1, 3, scalar, later(2) + K + half, 2)
-        scatter(1, 0, PIECE, on_scalar)
-        make_gw(0, 0, 6, scalar)
-        quantize_w(1, range(1, BLOCKS), w_bf1_rest)
-        make_dx(1, 0, 0, vector, base + 4 * K)
-        quantize_x(1, later(2) + 4 * K + half)
-        scatter(0, N, S, vector)
-        scatter(1, PIECE, N, on_scalar, 0)
+        quantize_dzs(3, mid + q)
+        quantize_x(0, mid + K + q)
+        quantize_w("w_mid", mid_units, w_bf)
+        make_dx(0, 1, 3, scalar, mid - 2 * K + q)
+        scatter(1, 0, N, vector)
+        w_bf = join_on_gpsimd("w_late_bf", w_late, at_dzn + 4 * K)
 
-        bank_x2 = gather_x(2, 5, (later(2) - K - half, later(2) + K + half))
-        make_dx(1, 2, 4, scalar, later(2) - K)
-        scatter(2, N, S, vector)
-        make_dx(1, 1, 2, scalar, later(2) - 3 * K)
+        bank_x2 = gather_x(2, 0, (mid + 3 * K + q, mid + 2 * K + q))
+        make_gw(0, 0, 6, scalar)
         weave_x(2, bank_x2, later(5))
-        quantize_x(2, None)
-        scatter(1, N, N + PIECE, on_scalar)
-        make_dx(0, 3, 0, scalar, later(2) + 2 * K)
+        quantize_w("w_late", late_units, w_bf)
+        quantize_x(1, late + 4 * K)
+        make_dx(1, 0, 5, scalar, late)
+        scatter(0, N, S, vector)
+        quantize_x(2, late + 5 * K)
+        make_dx(0, 2, 4, scalar, late + 2 * K)
+        make_gw(1, 0, 7, scalar, late + 6 * K)
+        scatter(2, 0, PIECE, on_scalar)
+        make_dx(1, 1, 1, scalar, at_dy_g)
+        scatter(1, N, S, vector)
+        scatter(2, PIECE, N, on_scalar, 0)
+        make_dx(1, 2, 2, scalar, later(1))
+        make_dx(0, 3, 5, scalar, later(3))
         scatter(3, 0, N, vector)
-        scatter(1, N + PIECE, S, on_scalar, N)
-        make_gw(1, 0, 7, scalar, later(3))
-        make_gw(0, 1, 6, scalar, later(3) + 2 * K)
-        make_dx(1, 3, 3, scalar, later(3) + 6 * K)
+        scatter(2, N, N + PIECE, on_scalar)
+        scatter(2, N + PIECE, S, on_scalar, N)
+        make_dx(1, 3, 3, scalar, later(3) + 2 * K)
         scatter(3, N, S, vector)
-        make_gw(1, 1, 7, scalar, later(3) + 4 * K, nc.scalar)
-        make_gw(0, 2, 6, scalar, None, nc.scalar)
-        gather_half(3, 0, later(2) - 3 * K)
-        gather_half(3, 1, later(2) - 2 * K)
+        make_gw(0, 1, 5, scalar, None, nc.scalar)
+        make_gw(1, 1, 2, scalar, None, nc.scalar)
+        make_gw(0, 2, 1, scalar, None, nc.scalar)
+        gather_half(3, 0, later(1))
+        gather_half(3, 1, later(1) + K)
         make_gw(1, 2, 7, vector, later(4))
-        turn_half(3, 0, 1, later(1))
-        turn_half(3, 1, 2, later(1) + K)
+        turn_half(3, 0, 0, later(1) + 2 * K)
+        turn_half(3, 1, 4, later(1) + 3 * K)
         make_gw(0, 3, 6, scalar)
         make_gw(1, 3, 7, vector)

@@ -186,10 +186,12 @@ def tile_attend_gex_tnh_wx_kernel(tc, xT, dyT, hT, ts, wm, offs, out_0, out_1):
             return raw
 
         mid_units = ((0, (2,)), (1, (0,)))
-        late_units = ((0, (3,)), (1, (1, 2, 3)))
+        late_units = ((0, (3,)), (1, (1, 2)))
+        last_units = ((1, (3,)),)
         w_mid = load_w("w_mid", mid, mid_units)
         x_win[2] = load("x2", xT[2 * P:3 * P, :], later(3))
         w_late = load_w("w_late", late, late_units)
+        w_last = load_w("w_last", at_w0 + 4 * K, last_units)
         x_win[3] = load("x3", xT[3 * P:4 * P, :], later(4))
 
         def interleave(name, copy, src, place, run):
@@ -322,13 +324,15 @@ def tile_attend_gex_tnh_wx_kernel(tc, xT, dyT, hT, ts, wm, offs, out_0, out_1):
         bank_x2 = gather_x(2, 0, (mid + 3 * K + q, mid + 2 * K + q))
         make_gw(0, 0, 6, scalar)
         weave_x(2, bank_x2, later(5))
+        quantize_x(1, late + K)
         quantize_w("w_late", late_units, w_bf)
-        quantize_x(1, late + 4 * K)
-        make_dx(1, 0, 5, scalar, late)
+        w_bf = join_on_gpsimd("w_last_bf", w_last, at_dzn + 4 * K)
+        make_dx(1, 0, 5, scalar, late - K)
         scatter(0, N, S, vector)
-        quantize_x(2, late + 5 * K)
+        quantize_w("w_last", last_units, w_bf)
+        quantize_x(2, at_w0 + 4 * K)
         make_dx(0, 2, 4, scalar, late + 2 * K)
-        make_gw(1, 0, 7, scalar, late + 6 * K)
+        make_gw(1, 0, 7, scalar, late + 4 * K)
         scatter(2, 0, PIECE, on_scalar)
         make_dx(1, 1, 1, scalar, at_dy_g)
         scatter(1, N, S, vector)

from contextlib import ExitStack

import concourse.mybir as mybir
from concourse.masks import make_identity

B, N, T, D, DV = 2, 512, 2048, 512, 512
FLOPS = 2 * 2 * B * N * D * DV
BYTES = 4 * (D * T + 2 * DV * T + T + B * DV * D + B * D * DV + D * T) + 2 * 128 * B * N // 16

F32 = mybir.dt.float32
BF16 = mybir.dt.bfloat16
U32 = mybir.dt.uint32
U16 = mybir.dt.uint16
U8 = mybir.dt.uint8
E4M3 = mybir.dt.float8_e4m3fn_x4
E5M2 = mybir.dt.float8_e5m2_x4
ALU = mybir.AluOpType
ACT = mybir.ActivationFunctionType

K = 1024
SLOT = 11 * K
P = 128
S = B * N
BLOCKS = D // P
PIECE = 256


def tile_attend_gex_tnh_wx_kernel(tc, xT, dyT, hT, ts, wm, offs, out_0, out_1):
    nc = tc.nc
    with ExitStack() as ctx:
        keep = ctx.enter_context(tc.tile_pool(name="keep", bufs=1))
        relay = ctx.enter_context(tc.tile_pool(name="relay", bufs=1))
        banks = ctx.enter_context(tc.psum_pool(name="banks", bufs=1))

        def sb(name, shape, dtype, place=None):
            if place is None:
                return keep.tile(shape, dtype, name=name, align_bytes=64)
            return relay.tile(shape, dtype, name=name, offset=place, align_bytes=64)

        def psum(name, bank, shape):
            return banks.tile(shape, F32, name=name, offset=2 * K * bank)

        def load(name, src, place):
            raw = sb(name, list(src.shape), F32, place)
            nc.sync.dma_start(raw[:], src)
            return raw

        def first(k):
            return SLOT * k + 512

        def small(k):
            return SLOT * k + 8 * K + 256

        def later(k):
            return SLOT * k

        rest = 9 * SLOT
        at_ts_row, at_sq, at_dy_g, at_dz, at_w0, at_h_g, at_dzn, at_gw = (
            rest + k * K for k in (0, 4, 8, 12, 20, 28, 32, 40)
        )

        offsets = keep.tile([P, S // 16], U16, name="offsets")

        def entries(begin, end):
            return offsets[:, begin // 16:end // 16]

        slots = [slice(b * N, (b + 1) * N) for b in range(B)]
        lists = [entries(b * N, (b + 1) * N) for b in range(B)]
        h_planes = hT.rearrange("(p t) c -> p t c", t=4)
        dy_planes = dyT.rearrange("(p t) c -> p t c", t=4)
        w_planes = [wm[b].rearrange("(p t) d -> p t d", t=4) for b in range(B)]

        nc.sync.dma_start(offsets[:], offs)
        ts_win = sb("ts_win", [P, T], F32, first(8))
        nc.scalar.dma_start(ts_win[P - 1:P, :], ts[0:1, :])
        h_win, dy_win, x_win = {}, {}, {}
        for t in range(4):
            h_win[t] = load(f"h{t}", h_planes[:, t, :], first(2 * t))
            dy_win[t] = load(f"dy{t}", dy_planes[:, t, :], first(2 * t + 1))
        w_first = load("w_first", w_planes[0][:, :, :2 * P], at_w0)

        ident = sb("ident", [P, P], F32)
        make_identity(nc, ident[:])
        nc.vector.memset(ts_win[:P - 1, :], 0.0)
        gx = [sb(f"gx{j}", [P, T], F32) for j in range(BLOCKS)]
        for j in range(BLOCKS):
            nc.gpsimd.memset(gx[j][:], 0.0)

        ts_row = sb("ts_row", [P, S], F32, at_ts_row)
        ts_g = sb("ts_g", [P, S], F32)
        dz = [sb(f"dz{b}", [P, 4, N], BF16, at_dz + 4 * K * b) for b in range(B)]
        dzs, dzs_mx, w_mx, dzn_mx, x_mx, dx = {}, {}, {}, {}, {}, {}

        def quantize(name, src, fmt, place=None, pieces=1):
            words = src.shape[1] // 4
            codes = sb(name + "_codes", [P, words], U32, place)
            scales = sb(name + "_scales", [P, words], U8)
            for k in range(pieces):
                begin, end = k * words // pieces, (k + 1) * words // pieces
                nc.vector.quantize_mx(
                    out=codes[:, begin:end].bitcast(fmt), scales=scales[:, begin:end], in_=src[:, 4 * begin:4 * end]
                )
            return codes, scales

        def product(bank, stationary, column, moving, cols):
            nc.tensor.matmul_mx(
                out=bank,
                lhsT=stationary[0][:, column:column + P].bitcast(E4M3),
                lhsT_scale=stationary[1][:, column:column + P],
                rhs=moving[0][:, cols].bitcast(E5M2),
                rhs_scale=moving[1][:, cols],
                start=True,
                stop=True,
            )

        for b in range(B):
            nc.vector.tensor_copy(ts_row[:, slots[b]], ts_win[:].indirect(lists[b]))
            bank = psum(f"ts_turn{b}", b, [P, 4, P])
            for s in range(4):
                nc.tensor.transpose(bank[:, s, :], ts_row[:, b * N + s * P:b * N + (s + 1) * P], ident[:])
            ts_cols = sb(f"ts_cols{b}", [P, 4, 1], F32, at_sq + 64 * b)
            nc.scalar.copy(ts_cols[:], bank[:, :, P - 1:P])
            bank = psum(f"ts_spread{b}", 3 + b, [P, 4, P])
            for s in range(4):
                nc.tensor.transpose(bank[:, s, :], ts_cols[:, s, :].to_broadcast([P, P]), ident[:])
            nc.scalar.mul(ts_g[:, slots[b]], bank[:].rearrange("p s q -> p (s q)"), -1.0)

        def weave_words(dst, bank):
            nc.scalar.copy(
                dst.bitcast(F32).rearrange("q (b c i u) -> q b c u i", c=P // 2, i=2, u=2),
                bank[:].rearrange("q b u (c i) -> q b c u i", i=2),
            )

        def turn_words(bank, b, words):
            for u in range(2):
                nc.tensor.transpose(bank[:, b, u, :], words.bitcast(F32)[:, u:N // 2:2], ident[:])

        def turn_dz(t, place):
            bank = psum(f"dz_turn{t}", (t + 2) % 3, [P, B, 2, P])
            for b in range(B):
                turn_words(bank, b, dz[b][:, t, :])
            dzs[t] = sb(f"dzs{t}", [P, B * 4 * P], BF16, place)
            weave_words(dzs[t][:], bank)

        def quantize_dzs(t, place):
            dzs_mx[t] = quantize(f"dzs{t}", dzs[t][:], E5M2, place)

        for t in range(4):
            h_g = sb(f"h_g{t}", [P, S], F32, at_h_g)
            if t == 0:
                nc.vector.tensor_copy(h_g[:], h_win[t][:].indirect(offsets[:]))
            else:
                nc.scalar.activation(h_g[:], h_win[t][:].indirect(offsets[:]), ACT.Copy)
                turn_dz(t - 1, small(2 * t))
            h_sq = sb(f"h_sq{t}", [P, S], F32, (at_sq, at_ts_row)[t % 2])
            nc.scalar.activation(h_sq[:], h_g[:], ACT.Square)
            dy_g = [sb(f"dy_g{t}{b}", [P, N], F32, at_dy_g + 2 * K * b) for b in range(B)]
            for b in range(B):
                nc.vector.tensor_tensor(dy_g[b][:], dy_win[t][:].indirect(lists[b]), ts_g[:, slots[b]], ALU.mult)
            for b in range(B):
                nc.vector.scalar_tensor_tensor(
                    out=dz[b][:, t, :],
                    in0=h_sq[:, slots[b]],
                    scalar=1.0,
                    in1=dy_g[b][:],
                    op0=ALU.subtract,
                    op1=ALU.mult,
                )
            if t in (1, 2):
                quantize_dzs(t - 1, small(2 * t + 1))

        half = K // 2
        x_win[0] = load("x0", xT[0:P, :], later(0))
        x_win[1] = load("x1", xT[P:2 * P, :], later(1))
        mid, late = later(2) + 2 * K, later(7)

        def load_w(name, place, pieces):
            raw = sb(name, [P, 4, P * sum(len(blocks) for b, blocks in pieces)], F32, place)
            column = 0
            for b, blocks in pieces:
                width = P * len(blocks)
                nc.sync.dma_start(
                    raw[:, :, column:column + width], w_planes[b][:, :, P * blocks[0]:P * blocks[0] + width]
                )
                column = column + width
            return raw

        mid_units = ((0, (2,)), (1, (0,)))
        late_units = ((0, (3,)), (1, (1, 2)))
        last_units = ((1, (3,)),)
        w_mid = load_w("w_mid", mid, mid_units)
        x_win[2] = load("x2", xT[2 * P:3 * P, :], later(3))
        w_late = load_w("w_late", late, late_units)
        w_last = load_w("w_last", at_w0 + 4 * K, last_units)
        x_win[3] = load("x3", xT[3 * P:4 * P, :], later(4))

        def interleave(name, copy, src, place, run):
            dst = sb(name, [P, 4 * src.shape[2]], BF16, place)
            copy(
                dst[:].rearrange("p (c i t) -> p c t i", i=run, t=4),
                src[:].rearrange("p t (c i) -> p c t i", i=run),
            )
            return dst

        def join_on_gpsimd(name, src, place):
            dst = sb(name, [P, 4 * src.shape[2]], BF16, place)
            nc.gpsimd.tensor_scalar(
                dst[:].rearrange("p (c t) -> p c t", t=4),
                src[:].rearrange("p t c -> p c t"),
                1.0,
                0.0,
                ALU.mult,
                ALU.add,
            )
            return dst

        def quantize_w(name, pieces, src):
            operand = quantize(name, src[:], E4M3)
            for k, unit in enumerate((b, j) for b, blocks in pieces for j in blocks):
                w_mx[unit] = (operand, k * P)

        def product_dx(b, j, number):
            bank = psum(f"dx_sum{b}{j}", number, [P, N])
            product(bank[:], *w_mx[b, j], dzn_mx[b], slice(0, N))
            return bank

        def make_dx(b, j, number, copy, place, pieces=1):
            bank = product_dx(b, j, number)
            dx[j, b * N] = sb(f"dx{b}{j}", [P, N], F32, place)
            for k in range(pieces):
                cols = slice(k * N // pieces, (k + 1) * N // pieces)
                copy(dx[j, b * N][:, cols], bank[:, cols])

        def on_scalar(out, in_):
            nc.scalar.activation(out, in_, ACT.Copy)

        def scatter(j, begin, end, copy, origin=None):
            origin = begin if origin is None else origin
            copy(gx[j][:].indirect(entries(begin, end)), dx[j, origin][:, begin - origin:end - origin])
            if end == S:
                nc.sync.dma_start(out_1[j * P:(j + 1) * P, :], gx[j][:])

        def gather_half(j, b, place):
            x_g[j, b] = sb(f"x_g{j}{b}", [P, N], BF16, place)
            on_scalar(x_g[j, b][:], x_win[j][:].indirect(lists[b]))

        def turn_x(j, number):
            bank = psum(f"x_turn{j}", number, [P, B, 2, P])
            for b in range(B):
                turn_words(bank, b, x_g[j, b][:])
            return bank

        def gather_x(j, number, places):
            for b in range(B):
                gather_half(j, b, places[b])
            return turn_x(j, number)

        def weave_x(j, bank, place):
            xs[j] = sb(f"xs{j}", [P, S], BF16, place)
            weave_words(xs[j][:], bank)

        def quantize_x(j, place):
            operand = quantize(f"x{j}", xs[j][:], E4M3, place)
            for b in range(B):
                x_mx[b, j] = (operand, b * P)

        def turn_half(j, b, number, place):
            bank = psum(f"x_turn{j}{b}", number, [P, 1, 2, P])
            turn_words(bank, 0, x_g[j, b][:])
            xs[j, b] = sb(f"xs{j}{b}", [P, N], BF16, place)
            weave_words(xs[j, b][:], bank)
            x_mx[b, j] = (quantize(f"x{j}{b}", xs[j, b][:], E4M3), 0)

        def make_gw(b, j, number, copy, place=None, queue=nc.sync):
            bank = psum(f"gw_sum{b}{j}", number, [P, 4, P])
            for t in range(4):
                product(bank[:, t, :], *x_mx[b, j], dzs_mx[t], slice(b * P, (b + 1) * P))
            gw = sb(f"gw{b}{j}", [P, DV], F32, place or at_gw + 2 * K * (B * j + b))
            copy(
                gw[:].rearrange("d (c i t) -> d c t i", i=2, t=4),
                bank[:].rearrange("d t (c i) -> d c t i", i=2),
            )
            queue.dma_start(out_0[b, j * P:(j + 1) * P, :], gw[:])

        vector, scalar = nc.vector.tensor_copy, nc.scalar.copy
        xs, x_g = {}, {}
        q = K // 4

        w_bf = interleave("w_first_bf", scalar, w_first, later(5), 2)
        gather_half(0, 0, later(6) + K)
        gather_half(0, 1, later(6) + 5 * K)
        turn_dz(3, later(6) - half)
        dzn0 = interleave("dzn0", vector, dz[0], at_dzn, 4)
        quantize_w("w_first", ((0, (0, 1)),), w_bf)
        dzn_mx[0] = quantize("dzn0", dzn0[:], E5M2, None, 2)
        quantize_dzs(2, None)
        dzn1 = join_on_gpsimd("dzn1", dz[1], later(6) + 6 * K + half)
        dx[0, 0] = sb("dx00", [P, N], F32, at_sq)
        for k in range(2):
            cols = slice(k * PIECE, (k + 1) * PIECE)
            bank = psum(f"dx_sum00{k}", 4 + k, [P, PIECE])
            product(bank[:], *w_mx[0, 0], dzn_mx[0], cols)
            vector(dx[0, 0][:, cols], bank[:])
        scatter(0, 0, PIECE, vector)
        scatter(0, PIECE, N, vector, 0)

        bank_x0 = [psum(f"x_turn0{b}", (0, 5)[b], [P, 1, 2, P]) for b in range(B)]
        for b in range(B):
            turn_words(bank_x0[b], 0, x_g[0, b][:])
        bank_x1 = gather_x(1, 1, (later(6) + 2 * K, at_h_g))
        xs[0] = sb("xs0", [P, S], BF16, later(6) + 2 * K + half)
        for b in range(B):
            weave_words(xs[0][:, slots[b]], bank_x0[b])
        weave_x(1, bank_x1, later(0))
        w_bf = join_on_gpsimd("w_mid_bf", w_mid, at_dzn + 4 * K)
        dzn_mx[1] = quantize("dzn1", dzn1[:], E5M2)
        quantize_dzs(3, mid + q)
        quantize_x(0, mid + K + q)
        quantize_w("w_mid", mid_units, w_bf)
        make_dx(0, 1, 3, scalar, mid - 2 * K + q)
        scatter(1, 0, N, vector)
        w_bf = join_on_gpsimd("w_late_bf", w_late, at_dzn + 4 * K)

        bank_x2 = gather_x(2, 0, (mid + 3 * K + q, mid + 2 * K + q))
        make_gw(0, 0, 6, scalar)
        weave_x(2, bank_x2, later(5))
        quantize_x(1, late + K)
        quantize_w("w_late", late_units, w_bf)
        w_bf = join_on_gpsimd("w_last_bf", w_last, at_dzn + 4 * K)
        make_dx(1, 0, 5, scalar, late - K)
        scatter(0, N, S, vector)
        quantize_w("w_last", last_units, w_bf)
        quantize_x(2, at_w0 + 4 * K)
        make_dx(0, 2, 4, scalar, late + 2 * K)
        make_gw(1, 0, 7, scalar, late + 4 * K)
        scatter(2, 0, PIECE, on_scalar)
        make_dx(1, 1, 1, scalar, at_dy_g)
        scatter(1, N, S, vector)
        scatter(2, PIECE, N, on_scalar, 0)
        make_dx(1, 2, 2, scalar, later(1))
        make_dx(0, 3, 5, scalar, later(3))
        scatter(3, 0, N, vector)
        scatter(2, N, N + PIECE, on_scalar)
        scatter(2, N + PIECE, S, on_scalar, N)
        make_dx(1, 3, 3, scalar, later(3) + 2 * K)
        scatter(3, N, S, vector)
        make_gw(0, 1, 5, scalar, None, nc.scalar)
        make_gw(1, 1, 2, scalar, None, nc.scalar)
        make_gw(0, 2, 1, scalar, None, nc.scalar)
        gather_half(3, 0, later(1))
        gather_half(3, 1, later(1) + K)
        make_gw(1, 2, 7, vector, later(4))
        turn_half(3, 0, 0, later(1) + 2 * K)
        turn_half(3, 1, 4, later(1) + 3 * K)
        make_gw(0, 3, 6, scalar)
        make_gw(1, 3, 7, vector)
